import numpy as np, ml_dtypes
CORES = [16,18,20,22]
N = 4
BF = ml_dtypes.bfloat16
W, C, CUT, VI, HE, EPS = 4096, 128, 64, 5, 12, 160
def parts(rng, p):
    m = len(p); ty = rng.integers(24, 248, (m, 16)); s = rng.choice(m, (N, 8, W), p=p); u = rng.choice(m, (N, 8, C), p=p)
    x = np.clip(ty[s].transpose(0, 1, 3, 2) + rng.integers(-2, 3, (N, 8, 16, W)), 16, 255)
    x = np.where(rng.random(x.shape) < 0.01, rng.integers(16, 256, x.shape), x)
    ta = rng.integers(0, W, (N, 8, C)); iv = rng.integers(1, W // 8 + 1, (N, 8, 16, C))
    iv = np.where(rng.random((N, 8, 1, C)) < 0.25, rng.integers(1, W, iv.shape), iv)
    e = rng.choice(np.array([EPS // 4, EPS // 2, EPS - EPS // 8, EPS + EPS // 4]), (N, 8, 1, C))
    d = np.clip(32 * ty[u].transpose(0, 1, 3, 2) + rng.integers(-e, e + 1, (N, 8, 16, C)), 512, 8160)
    d = np.where(rng.random(d.shape) < 0.03, rng.integers(512, 8161, d.shape), d)
    return x, ta, iv, d
def gains(rng):
    return 0.5 + rng.random((N, 8, 16, W), dtype=np.float32)
def pack(x, gain, ta, iv, d):
    return {"xs": np.ascontiguousarray(x.reshape(N, 128, W)).astype(np.float32).astype(BF), "gn": np.ascontiguousarray(gain.reshape(N, 128, W)).astype(np.float32).astype(BF),
            "tau": np.ascontiguousarray(ta).astype(np.int32), "iv": np.ascontiguousarray(iv.reshape(N, 128, C)).astype(np.int32), "pf": np.ascontiguousarray(d.reshape(N, 128, C)).astype(np.int32)}
def setup_inputs(rng):
    x, ta, iv, d = parts(rng, [0.4, 0.3, 0.3])
    return pack(x, gains(rng), ta, iv, d)
def setup_inputs_spread(rng):
    x, ta, iv, d = parts(rng, [0.45, 0.3, 0.15, 0.1])
    iv = np.clip(np.exp2((W.bit_length() - 1) * rng.random(iv.shape)).astype(np.int64), 1, W - 1)
    return pack(x, gains(rng) * np.exp2(rng.integers(-1, 2, (N, 8, 1, W))), ta, iv, d)
def setup_inputs_ends(rng):
    i = np.arange(16); v = i[:, None] & i; par = (v ^ (v >> 1) ^ (v >> 2) ^ (v >> 3)) & 1
    ty = par[rng.permutation(16)[:4]][:, rng.permutation(16)] ^ rng.integers(0, 2, 16)
    s = np.repeat(rng.integers(1, 4, (N, 8, W // 8)), 8, axis=2); s[..., 1:17] = 0; s[..., W - 17:W - 1] = 0
    nf = np.where((rng.random((N, 8, W)) < 0.08) & (s > 0), rng.integers(3, 6, (N, 8, W)), 0)[:, :, None, :]
    x = ty[s].transpose(0, 1, 3, 2) ^ (np.argsort(rng.random((N, 8, 16, W), dtype=np.float32), axis=2) < nf)
    u = rng.integers(1, 4, (N, 8, C)); nd = np.where(rng.random((N, 8, C)) < 0.3, rng.integers(1, 5, (N, 8, C)), 0)
    for q in range(N - 1, -1, -2):
        u[q, :, 0] = 0; u[q, :, C - 1] = 0; nd[q, :, 0] = 0; nd[q, :, C - 1] = 16 - HE
    d = ty[u].transpose(0, 1, 3, 2) ^ (np.argsort(rng.random((N, 8, 16, C)), axis=2) < nd[:, :, None, :])
    near = (np.sum(d != ty[0][:, None], axis=2) <= 16 - HE) & (u > 0)
    d = np.where(near[:, :, None, :], ty[u].transpose(0, 1, 3, 2), d)
    mode = rng.integers(0, 3, (N, 8, 1, C)); iv = np.where(mode == 2, rng.integers(0, 2, (N, 8, 16, C)), mode)
    iv = np.where(iv == 1, W - 1, 1); jump = rng.random((N, 8, C)) < 0.8
    iv[:, :, 0] = np.where(jump, rng.integers(1, W, (N, 8, C)), iv[:, :, 0])
    iv[:, :, 8] = np.where(jump & (rng.random((N, 8, C)) < 0.5), rng.integers(1, W, (N, 8, C)), iv[:, :, 8])
    ta = np.where(rng.random((N, 8, C)) < 0.7, (W - 1) * rng.integers(0, 2, (N, 8, C)), rng.integers(0, W, (N, 8, C)))
    iv[..., 0] = 1; iv[..., C - 1] = W - 1; ta[..., 0] = 0; ta[..., C - 1] = W - 1
    gain = np.where(rng.random((N, 8, 16, W)) < 0.3, 0.125, 4.0)
    return pack(np.where(x == 1, 255, 16), gain, ta, iv, np.where(d == 1, 8160, 512))
def setup_inputs_corners(rng):
    x, ta, iv, d = parts(rng, [0.4, 0.3, 0.3]); z = rng.integers(24, 248, 16); junk = 16 + (z - 16 + 100) % 240
    k = np.arange(16); e = k % 2; nb = W // 64
    for q in range(N):
        for g in range(8):
            st = (2, 1, 3, 2)[(g + q) % 4]
            cs = rng.permutation(np.concatenate([np.array([0, C - 1]), 1 + rng.permutation(C - 2)[:nb - 2]]))
            b = 64 * rng.permutation(nb) - 1; on = (b[:, None] + st * k) % W; lt = (on + 1) % W
            mode = rng.integers(0, 9, (nb, 1)); state = rng.integers(0, 4, (nb, 16))
            for j, pat in enumerate((3 + 0 * k, 2 + 0 * k, e, (k == 15) * 1, (k == 0) * 1, 1 - e, 2 * e)):
                state = np.where(mode == j, pat[None, :], state)
            hc = np.zeros(W, bool); hc[on[(state & 1) > 0]] = True; hc[lt[(state & 2) > 0]] = True
            al = np.zeros(W, bool); al[on.reshape(-1)] = True; al[lt.reshape(-1)] = True
            rest = np.where(al[None, :], junk[:, None], x[q, g])
            far = np.argsort(rng.random((16, W)), axis=0) < rng.choice(np.array([0, 16 - HE, 17 - HE]), W, p=[0.7, 0.2, 0.1])[None, :]
            x[q, g] = np.where(hc[None, :] & ~far, z[:, None], rest)
            ta[q, g, cs] = (b - st) % W; iv[q, g][:, cs] = st
            pick = rng.choice(4, nb, p=[0.4, 0.25, 0.25, 0.1]); n1 = np.array([16, 16, HE, HE - 1])[pick]
            size = np.where(np.argsort(rng.random((16, nb)), axis=0) < n1[None, :], EPS, EPS + 1) * (pick > 0)[None, :]
            d[q, g][:, cs] = 32 * z[:, None] + rng.choice(np.array([-1, 1]), (16, nb)) * size
    return pack(x, gains(rng), ta, iv, d)
def setup_inputs_crowd(rng):
    x, ta, iv, d = parts(rng, [0.4, 0.3, 0.3]); z = rng.integers(24, 248, 16); junk = 16 + (z - 16 + 100) % 240
    hop = np.where(np.arange(16) % 2 == 0, W - 1, 1); o = rng.permutation(8)
    for q in range(N):
        for i in range(8):
            g = int(o[i]); v = int(rng.choice(np.array([0, W - 1, int(rng.integers(1, W - 1))]))); cs = rng.permutation(C)
            if i == 6: v = int(rng.integers(1, W // 2))
            n = (C, C, 16, 16, 16, 0, (64, 32, 96)[q % 3], 0)[i]; one = (0, 0, 1, 0, 0, 2, 1, 0)[i]; a = cs[:n]; s = cs[n:n + one]
            if i == 7:
                h = 19 + rng.permutation(45)[:7]; s = np.concatenate([np.arange(9, 19), h, 127 - h, rng.choice(np.array([0, C - 1]), 1)])
            x[q, g, :, (v - 1) % W] = junk; x[q, g, :, v] = z
            ta[q, g, a] = v; iv[q, g][:, a] = hop[:, None]; d[q, g][:, a] = 32 * z[:, None]
            ta[q, g, s] = (v - W // 32) % W; iv[q, g][:, s] = W // 32; d[q, g][:, s] = 32 * z[:, None]
            if i in (1, 4):
                iv[q, g, 15, a[-1]] = W // 2; x[q, g, :, (v - 1 + W // 2) % W] = z
    return pack(x, gains(rng), ta, iv, d)
def setup_inputs_long(rng):
    x, ta, iv, d = parts(rng, [0.4, 0.3, 0.3]); gain = gains(rng); z, z0 = rng.integers(24, 248, (2, 16)); g0 = int(rng.integers(0, 8)); base = int(rng.integers(0, W))
    wd = 16 * 2 ** VI; k = np.arange(16)
    for i in range(min(2, W // (wd * N)) * N):
        r = i % N; b = (base - wd * i) % W
        for g in range(8):
            if g != g0:
                c = int(rng.integers(0, CUT)) + CUT * ((i // N + r) % 2)
                ta[r, g, c] = b; iv[r, g, :, c] = W - 2; d[r, g, :, c] = 32 * z + rng.integers(-EPS, EPS + 1, 16)
        q = (r + VI - 1) % N
        for g in range(8):
            m = rng.integers(0, 3, 16); m[9] = 1; m[15] = 1
            x[q, g][:, ((b - 2 ** VI * (k + 1) + m) % W)[m < 2]] = z[:, None]
        for t in range(VI - 1):
            x[(r + t) % N][:, :, (b - 2 ** (t + 1) * (k[1::2] + 1)) % W] = z[:, None]
    nf = min(C, W // 16); sg = np.where(z0 < 136, 1, -1)
    for q in range(N):
        cs = rng.permutation(C)[:nf]; st = 2 * int(rng.integers(0, W // 2)) + 1; b = int(rng.integers(0, W))
        col = (b + st * (np.arange(16 * nf) + 1)) % W
        x[q, g0][:, col] = z0[:, None]; ta[q, g0, cs] = (b + 16 * st * np.arange(nf)) % W; iv[q, g0][:, cs] = st
        e = rng.integers(-EPS, EPS + 1, (16, nf)); far = np.argsort(rng.random((16, 8)), axis=0); near = EPS * rng.choice(np.array([-1, 1]), (16, 8))
        e[:, :8] = np.where(far < 2, 512 * sg[:, None], np.where(far < 16 - HE, 2080 * sg[:, None], near))
        d[q, g0][:, cs] = 32 * z0[:, None] + e
        gain[q, g0][:, col[:128]] = 4 * (VI - 2) * (0.75 + 0.5 * rng.random((16, 128)))
    return pack(x, gain * 0.25, ta, iv, d)
def check_ranges(d):
    bad = []
    for name, lo, hi in (("xs", 16, 255), ("gn", 0.125, 4), ("tau", 0, W - 1), ("iv", 1, W - 1), ("pf", 512, 8160)):
        a = np.asarray(d[name]).astype(np.float64)
        if not np.all(np.isfinite(a)) or np.min(a) < lo or np.max(a) > hi: bad.append("range of " + name)
        elif name != "gn" and np.any(a != np.floor(a)): bad.append(name + " is not whole")
    return bad
def go(a, t):
    return np.concatenate([a[..., :CUT], np.roll(a[..., CUT:], t, axis=0)], axis=-1)
def reference(xs, gn, tau, iv, pf):
    X = xs.astype(np.float32).astype(np.int32).reshape(N, 8, 16, W) * np.int32(32); GA = gn.astype(np.float64).reshape(N, 8, 16, W)
    I = iv.astype(np.int32).reshape(N, 8, 16, C); D = pf.astype(np.int32).reshape(N, 8, 16, C); ta = tau.astype(np.int32)
    y = np.zeros((N, 8, 16, C)); eight = np.arange(8)[:, None]; rows = np.arange(16)[None, :, None]
    for t in range(VI):
        for r in range(N):
            q = (r + t) % N
            T = go((ta[r][:, None, :] + np.add.accumulate(I[r], axis=1)) & (W - 1), t).transpose(0, 2, 1).reshape(8, 16 * C); T1 = (T + 1) & (W - 1)
            Ds = go(D[r], t); Dx = np.repeat(Ds, 16, axis=2)
            e0 = np.take_along_axis(X[q], T[:, None, :], 2) - Dx; e1 = np.take_along_axis(X[q], T1[:, None, :], 2) - Dx
            on = np.sum((np.abs(e0) <= EPS).astype(np.int32), axis=1) >= HE
            late = ~on & (np.sum((np.abs(e1) <= EPS).astype(np.int32), axis=1) >= HE); heard = on | late
            P = np.where(late, T1, T); E = np.where(late[:, None, :], e1, e0)
            cnt = np.zeros((8, W), np.int32); np.add.at(cnt, (eight, P), heard.astype(np.int32))
            taken = heard & (np.take_along_axis(cnt, P, 1) == 1)
            z = np.where(taken[:, None, :], np.take_along_axis(GA[q], P[:, None, :], 2) * np.exp(-0.00390625 * np.abs(E)), 0.0)
            y[r] += go(np.add.reduce(z.reshape(8, 16, C, 16), axis=3), -t)
            if t == VI - 1: continue
            S = np.add.reduce(np.where(taken[:, None, :], E, 0).reshape(8, 16, C, 16), axis=3)
            D[r] = go(Ds + (S >> 4), -t)
            X[q] = np.where((cnt == 1)[:, None, :], 0, X[q])
            a = go(taken.reshape(8, C, 16).transpose(0, 2, 1), -t); l = go((taken & late).reshape(8, C, 16).transpose(0, 2, 1), -t)
            J = I[r] + l; leave = np.zeros((8, 16, C), bool); leave[:, :15] = ~a[:, :15] & a[:, 1:]
            J[:, 1:] = J[:, 1:] + np.where(leave[:, :15], J[:, :15], 0)
            o = np.argsort(leave.astype(np.int32), axis=1, kind="stable"); n = 16 - np.sum(leave.astype(np.int32), axis=1)[:, None, :]
            src = np.take_along_axis(o, np.where(rows < n, rows, rows - n), 1)
            I[r] = np.take_along_axis(J, src, 1)
    return {"y": y.reshape(N, 128, C).astype(np.float32)}

def check_inputs(d):
    bad = list(check_ranges(d))
    if not bad:
        for name, y in reference(**d).items():
            for q in range(N):
                v = np.abs(np.asarray(y[q], np.float64)); s = np.sqrt(np.mean(v * v))
                if v.max() > 10 * s or s < 2.0 ** -1: bad.append('%s of rank %d is uneven or too small' % (name, q))
    return bad

@@ -1,0 +1,811 @@
+from concourse.bass import DstId, RemoteDMATransfer
+from concourse.mybir import AluOpType as ALU, ActivationFunctionType as AF
+
+F32, BF, F16, I32, U16 = "float32", "bfloat16", "float16", "int32", "uint16"
+NV = 5
+H = 65536.0
+KEY = 16384.0
+BIGL = 1048576.0
+DUMMY = 4098
+RINT = 1.5 * 2.0 ** 23
+
+SCRATCH = {
+    "xb": ("sbuf", [128, 4112], BF), "gw": ("sbuf", [128, 4112], BF), "vw": ("sbuf", [128, 4104], F32),
+    "xh": ("sbuf", [128, 2048], F32), "gneg": ("sbuf", [128, 2048], BF), "gu": ("sbuf", [128, 4112], BF),
+    "ivi": ("sbuf", [128, 128], I32), "pfi": ("sbuf", [128, 128], I32), "tai": ("sbuf", [128, 128], I32),
+    "ivf": ("sbuf", [128, 128], F32), "pff": ("sbuf", [128, 128], F32), "taf": ("sbuf", [128, 128], F32),
+    "one32": ("sbuf", [128, 128], F32), "oneb": ("sbuf", [128, 512], BF),
+    "ix": ("sbuf", [128, 256], F32), "trip": ("sbuf", [128, 128], F32), "tri0": ("sbuf", [128, 128], F32),
+    "tsel": ("sbuf", [128, 128], F32),
+    "idb": ("sbuf", [128, 9 * 128], BF), "id16": ("sbuf", [128, 128], F16),
+    "pm32": ("sbuf", [128, 144], F32), "pm16": ("sbuf", [128, 144], F16),
+    "sel16": ("sbuf", [128, 2048], F16), "selb": ("sbuf", [128, 2048], BF),
+    "ex": ("sbuf", [128, 2048], BF), "rl": ("sbuf", [128, 128], BF), "r01": ("sbuf", [128, 256], BF), "msk": ("sbuf", [128, 1024], BF),
+    "bo0": ("sbuf", [128, 8], BF), "bo": ("sbuf", [128, 8], BF),
+    "tab": ("sbuf", [128, 128], BF), "tb2": ("sbuf", [128, 128], BF),
+    "d2a": ("sbuf", [128, 128], F32), "d2b": ("sbuf", [128, 256], F32), "d2": ("sbuf", [128, 512], F32),
+    "loff": ("sbuf", [128, 5 * 256], U16), "lmp": ("sbuf", [128, 5 * 128], F32),
+    "lm2": ("sbuf", [128, 5 * 256], F16), "ld": ("sbuf", [128, 5 * 128], F32),
+    "soff": ("sbuf", [128, 4 * 256], U16), "smp": ("sbuf", [128, 4 * 128], F32),
+    "sm2": ("sbuf", [128, 4 * 256], F16), "sd": ("sbuf", [128, 4 * 128], F32),
+    "lst": ("sbuf", [128, 4 * 8], F32), "ly": ("sbuf", [128, 4 * 128], F32), "sy": ("sbuf", [128, 4 * 128], F32),
+    "xg": ("sbuf", [128, 4096], BF), "ab": ("sbuf", [128, 4096], BF), "ind": ("sbuf", [128, 4096], BF),
+    "e12": ("sbuf", [128, 128], F32), "late": ("sbuf", [128, 128], BF), "hm": ("sbuf", [128, 128], BF),
+    "hb": ("sbuf", [128, 128], BF), "pint": ("sbuf", [128, 128], I32), "loi": ("sbuf", [128, 128], I32),
+    "hii": ("sbuf", [128, 128], I32), "lo1": ("sbuf", [128, 128], BF), "av": ("sbuf", [128, 128], BF),
+    "bv": ("sbuf", [128, 128], BF), "lt1": ("sbuf", [128, 128], F32),
+    "oh": ("sbuf", [128, 16384], BF), "ptr": ("sbuf", [128, 128], F32), "poff": ("sbuf", [128, 256], U16),
+    "cs": ("sbuf", [128, 330], F32), "ub": ("sbuf", [128, 256], BF), "ucum": ("sbuf", [128, 256], BF),
+    "phi0": ("sbuf", [128, 2048], BF), "phi1": ("sbuf", [128, 2048], BF), "dl": ("sbuf", [128, 256], F32),
+    "nt": ("sbuf", [128, 128], F32), "tl": ("sbuf", [128, 128], BF), "lv": ("sbuf", [128, 136], BF),
+    "wt": ("sbuf", [128, 256], F32), "qb": ("sbuf", [128, 17 * 128], F32),
+    "rnd": ("sbuf", [128, 128], F32), "m16": ("sbuf", [128, 128], F16), "mt16": ("sbuf", [128, 128], F16),
+    "dsc": ("sbuf", [128, 128], F32), "a2": ("sbuf", [128, 256], F32), "x2": ("sbuf", [128, 128], F32),
+    "tt": ("sbuf", [128, 128], F32), "fi": ("sbuf", [128, 128], I32), "dn": ("sbuf", [128, 128], F32),
+    "fc": ("sbuf", [128, 512], F32), "dhi": ("sbuf", [128, 256], BF), "dlo": ("sbuf", [128, 256], BF),
+    "exv": ("sbuf", [128, 2048], F32), "exw": ("sbuf", [128, 1024], F32), "zz": ("sbuf", [128, 2048], F32),
+    "zw": ("sbuf", [128, 2048], F32), "sc": ("sbuf", [128, 1024], F32), "yo": ("sbuf", [128, 128], F32),
+}
+for _b in range(8):
+    SCRATCH["p%d" % _b] = ("psum", [128, 512], F32)
+
+SEMAPHORES = (["cP", "cV", "cA", "cG", "sent", "arrS", "l0", "l1", "l2", "l3", "l4", "l5", "l6", "o0", "o1"]
+              + ["arrA%d" % t for t in range(1, 5)] + ["arrB%d" % t for t in range(1, 5)]
+              + ["arrY%d" % t for t in range(1, 4)])
+
+
+def S(name, c0=None, c1=None, step=1, p0=0, p1=128):
+    if c0 is None:
+        c0, c1 = 0, SCRATCH[name][1][1]
+    return (name, p0, p1, c0, c1, step)
+
+
+def _meet(a, b):
+    if a[0] != b[0] or a[2] <= b[1] or b[2] <= a[1] or a[4] <= b[3] or b[4] <= a[3]:
+        return False
+    if a[5] == b[5] and a[5] > 1 and (a[3] - b[3]) % a[5]:
+        return False
+    return True
+
+
+def plan(rank, cores, topo):
+    ops = []
+
+    def put(q, kind, args, reads, writes, **opt):
+        ops.append((q, kind, args, [r for r in reads if isinstance(r, tuple)], writes, opt))
+
+    def rd(x):
+        return [x[1], x[2]] if x[0] == "*" else [x]
+
+    def ts(out, a, s1, s2, o0, o1=None):
+        put("V", "ts", (out, a, s1, s2, o0, o1), rd(a) + [s1, s2], [out])
+
+    def tt(out, a, b, o):
+        put("V", "tt", (out, a, b, o), rd(a) + [b], [out])
+
+    def cp(out, a):
+        put("V", "cp", (out, a), rd(a), [out])
+
+    def ms(out, v):
+        put("V", "ms", (out, v), [], [out])
+
+    def scan(out, a, b, o):
+        put("V", "scan", (out, a, b, o), [a, b], [out])
+
+    def act(out, a, f, bias=0.0, scale=1.0):
+        put("A", "act", (out, a, f, bias, scale), rd(a) + [bias], [out])
+
+    def mm(out, l, r, st=True, sp=True, **opt):
+        put("P", "mm", (out, l, r, st, sp), [l, r], [out], **opt)
+
+    def aff(out, a, pat, cmp, base, cm):
+        put("G", "aff", (out, a, pat, cmp, base, cm), [a], [out])
+
+    def iota(out, pat, base):
+        put("G", "iota", (out, pat, base), [], [out])
+
+    def gat(win, off):
+        return ("*", win, off)
+
+    def send(trs):
+        put("G", "send", (trs,), [t[0] for t in trs], [])
+
+    def arrive(sem, n, bufs):
+        put("X", "arr", (sem, n), [], bufs)
+
+    def ident(i):
+        return S("idb", 128 * i, 128 * i + 128)
+    I1, IM3, IM32, I2, IMG, IGK, I64, IM128, IM8K = [ident(i) for i in range(9)]
+    I32F = S("ix", 0, 128)
+    ID = AF.Identity
+    me = cores[rank]
+
+    def engs(dst, a, b):
+        e = topo.engines(me, dst)
+        n = len(e) // 4
+        return sum(1 << x for x in e[a * n:b * n]), (b - a) * n
+
+    put("S", "dma", (S("ivi"), ("iv",), "l0"), [], [S("ivi")])
+    put("A", "dma", (S("tai", p1=8), ("tau",), "l1"), [], [S("tai", p1=8)])
+    put("S", "dma", (S("xb", 0, 2048), ("xs", 0, 2048), "l2"), [], [S("xb", 0, 2048)])
+    put("A", "dma", (S("xb", 2048, 4096), ("xs", 2048, 4096), "l3"), [], [S("xb", 2048, 4096)])
+    put("S", "dma", (S("pfi"), ("pf",), "l4"), [], [S("pfi")])
+    ms(S("one32"), 1.0)
+    ms(S("oneb"), 1.0)
+    aff(S("tri0"), S("one32"), [[0, 16], [-16, 8]], ALU.is_ge, 0, 1)
+    aff(S("ix", 0, 128), S("one32"), [[-1, 128]], ALU.is_equal, 0, 1)
+    aff(S("trip"), S("tri0"), [[1, 16], [16, 8]], ALU.is_ge, 0, -1)
+    aff(S("tsel"), S("one32"), [[0, 16], [-1, 8]], ALU.is_equal, 0, 1)
+    aff(S("pm32", 16, 144), S("one32"), [[-1, 8], [-8, 16]], ALU.is_equal, 0, 1)
+    aff(S("bo0"), S("oneb", 0, 8), [[-16, 8]], ALU.is_ge, 0, 1)
+    iota(S("tab", 0, 63), [[1, 63]], -63)
+    aff(S("bo"), S("bo0"), [[16, 8]], ALU.is_ge, 15, -1)
+    iota(S("tab", 63, 128), [[1, 65]], 1)
+    iota(S("tb2"), [[1, 128]], -64)
+    ms(S("vw", 4096, 4104), H)
+    ms(S("xb", 4096, 4112), 0.0)
+    ms(S("gw", 4096, 4112), 0.0)
+    ms(S("gu", 4096, 4112), 0.0)
+    ms(S("ucum"), 0.0)
+    ms(S("lv"), 0.0)
+    ms(S("cs"), 0.0)
+    ms(S("sm2"), 0.0)
+    cp(S("id16"), I32F)
+    for k in range(8):
+        ts(S("sel16", k, 2048, 16), S("id16"), 1.5, None, ALU.mult)
+    cp(S("ivf"), S("ivi"))
+    ts(S("taf", p1=8), S("tai", p1=8), 2048.0, None, ALU.add)
+    cp(S("pm16", 16, 144), S("pm32", 16, 144))
+    cp(S("pm16", 0, 16), S("pm32", 128, 144))
+    act(S("ix", 128, 256), I32F, ID)
+    for ap, v in ((IM3, -3.0), (I1, 1.0), (I64, 64.0), (IM128, -128.0), (IM32, -32.0), (I2, 2.0), (IMG, -BIGL),
+                  (IGK, BIGL + KEY), (IM8K, -8192.0)):
+        act(ap, I32F, ID, 0.0, v)
+    act(S("d2b"), S("ix"), ID, 0.0, -2.0)
+
+    def times_tail(acc, t1, fill=()):
+        home = t1 == 0
+        off = ("loff", 0) if home else ("soff", 256 * (t1 - 1))
+        mp = ("lmp", 0) if home else ("smp", 128 * (t1 - 1))
+        b = 1.5 * 2.0 ** 35
+        for c in fill[:2]:
+            mm(*c)
+        ts(S("rnd"), acc, b, b, ALU.add, ALU.subtract)
+        tt(S("m16"), acc, S("rnd"), ALU.subtract)
+        mm(S("p7", 0, 128), S("m16"), S("id16"))
+        for c in fill[2:]:
+            mm(*c)
+        o = mp[1]
+        if home:
+            ts(S(mp[0], o, o + 128), S("m16"), 2048.0, None, ALU.add)
+        else:
+            ts(S(mp[0], o + 1, o + 128, p0=64), S("m16", 0, 127, p0=64), 2048.0, None, ALU.add)
+            ts(S(mp[0], o, o + 128, p1=64), S("m16", p1=64), 2048.0, None, ALU.add)
+            ts(S(mp[0], o, o + 128, 8, p0=64), S("m16", 7, 128, 8, p0=64), 2048.0, None, ALU.add)
+        cp(S("mt16"), S("p7", 0, 128))
+        mm(S("p6", 0, 64), S("pm16", 16, 144), S("mt16", 0, 64))
+        mm(S("p6", 64, 128), S("pm16", 16, 144) if home else S("pm16", 0, 128), S("mt16", 64, 128))
+        ts(S(off[0], off[1], off[1] + 128), S("p6", 0, 128), 2048.0, None, ALU.add)
+        ts(S(off[0], off[1] + 128, off[1] + 256), S("p6", 0, 128), 2049.0, None, ALU.add)
+
+    def centre_parts(d):
+        act(S("fc", 0, 128), d, ID, -0.484375, 1.0 / 32)
+        act(S("fc", 128, 256), d, ID, -0.484375, -1.0 / 32)
+        act(S("fc", 256, 384), S("fc", 0, 128), ID, RINT)
+        act(S("fc", 384, 512), S("fc", 128, 256), ID, RINT)
+
+    def centre(m2):
+        tt(m2, S("fc", 256, 384), S("fc", 384, 512), ALU.subtract)
+
+    mm(S("p4", 0, 128), S("ivf"), S("trip"), True, False)
+    mm(S("p4", 0, 128), S("taf", p1=8), S("tsel", p1=8), False, True)
+    mm(S("p5", 0, 8), S("taf", p1=8), S("ix", 0, 8, p1=8))
+    cp(S("pff"), S("pfi"))
+    mm(S("p3", 0, 128), S("pff"), I32F)
+    act(S("lst", 0, 8), S("p5", 0, 8), ID, -2048.0)
+    act(S("ld", 0, 128), S("p3", 0, 128), ID)
+    centre_parts(S("ld", 0, 128))
+    times_tail(S("p4", 0, 128), 0)
+    put("S", "dma", (S("gw", 0, 4096), ("gn",), "l5"), [S("loff", 0, 256)], [S("gw", 0, 4096)])
+    trs = []
+    for j, (a, b) in ((1, (0, 1)), (2, (1, 2)), (3, (2, 4))):
+        dst = cores[(rank + j) % 4]
+        trs.append((S("lst", 0, 8), S("lst", 8 * j, 8 * j + 8), dst, engs(dst, a, b)[0], "arrS"))
+    send(trs)
+    for k in range(8, 16):
+        ts(S("sel16", k, 2048, 16), S("id16"), 1.5, None, ALU.mult)
+    centre(S("lm2", 0, 128))
+    cp(S("xb", 4096, 4098), S("xb", 0, 2))
+    aff(S("rl"), S("oneb", 0, 128), [[-1, 4], [-64, 2], [-4, 16]], ALU.is_equal, 0, 1)
+    for j in range(4):
+        aff(S("ex", 512 * j, 512 * j + 512), S("oneb"), [[-1, 4], [-16, 8], [0, 16]], ALU.is_equal, -4 * j, 1)
+    for j in range(4):
+        aff(S("selb", 512 * j, 512 * j + 512), S("oneb"), [[-1, 32], [0, 16]], ALU.is_equal, -32 * j, 1)
+    for j in range(2):
+        aff(S("msk", 512 * j, 512 * j + 512), S("oneb"), [[0, 32], [1, 16]], ALU.is_gt, 0, 0)
+
+    def d2_constants():
+        tt(S("d2a"), S("ix", 127, 255), S("ix", 1, 129), ALU.add)
+        tt(S("d2", 0, 128), S("d2a"), S("d2b", 0, 128), ALU.add)
+        tt(S("d2", 0, 128, 64), S("ix", 1, 128, 64), S("ix", 0, 128, 64), ALU.subtract)
+        tt(S("d2", 62, 128, 64), S("ix", 61, 128, 64), S("d2b", 62, 128, 64), ALU.add)
+        tt(S("d2", 63, 128, 64), S("ix", 62, 128, 64), S("ix", 63, 128, 64), ALU.add)
+        act(S("d2", 128, 256), S("d2", 0, 128), ID, 0.0, -2.0)
+        tt(S("d2a"), S("ix", 0, 128), S("ix", 2, 130), ALU.add)
+        tt(S("d2", 256, 384), S("d2a"), S("d2b", 1, 129), ALU.add)
+        tt(S("d2", 318, 384, 64), S("ix", 62, 128, 64), S("d2b", 63, 128, 64), ALU.add)
+        cp(S("d2", 319, 384, 64), S("ix", 63, 128, 64))
+        act(S("d2", 384, 512), S("d2", 256, 384), ID, 0.0, -2.0)
+
+    def y_diff(t, j, src, bank):
+        o = S(bank)
+        c = 128 * (t % 2)
+        sel = S("selb", 512 * j, 512 * j + 512)
+        return [(o, S("dhi", c, c + 128), sel, True, False), (o, S("dlo", c, c + 128), sel, False, False),
+                (o, IM32, S(src, 512 * j, 512 * j + 512), False, True)]
+
+    def y_exp(bank, out):
+        act(S(bank), S(bank), AF.Abs)
+        act(out, S(bank), AF.Exp, 0.0, -1.0 / 256)
+
+    def y_chunk(t, j, bank):
+        for c in y_diff(t, j, "phi%d" % (t % 2), bank):
+            mm(*c)
+        y_exp(bank, S("exv", 512 * j, 512 * j + 512))
+
+    def y_gain(t, j, n=2):
+        for c in range(512 * j, 512 * (j + n), PIECE):
+            po = 128 * (t % 2) + c // 16
+            tt(S("zz", c, c + PIECE), gat(S("gw", 0, 4104), S("poff", po, po + PIECE // 16)), S("exv", c, c + PIECE), ALU.mult)
+
+    def y_sum(t, h, o, z="zz", first=True):
+        l = S("ix", 16 * t * h, 16 * t * h + 128)
+        return [(o, l, S(z, 1024 * h + k, 1024 * h + 1024, 16), k == 0 and first, k == 15) for k in range(16)]
+
+    def y_keep(t, h, o):
+        act(S("sy", 128 * t + 64 * h, 128 * t + 64 * h + 64), o, ID)
+        if h == 1 and t > 0:
+            dst = cores[(rank - t) % 4]
+            send([(S("sy", 128 * t, 128 * t + 128), S("ly", 128 * t, 128 * t + 128), dst, engs(dst, 0, 2)[0], "arrY%d" % t)])
+
+    nxt = cores[(rank + 1) % 4]
+    n4 = engs(nxt, 0, 1)[1]
+    VW = S("vw", 0, 4104)
+    for t in range(NV):
+        last = t == NV - 1
+        phi = "phi%d" % (t % 2)
+        off, mp = 256 * t, S("lmp", 128 * t, 128 * t + 128)
+        m2, dd = S("lm2", 256 * t, 256 * t + 128), S("ld", 128 * t, 128 * t + 128)
+        if t > 0:
+            arrive("arrB%d" % t, 2 * n4, [S("loff", off, off + 256), mp])
+            arrive("arrA%d" % t, 2 * n4, [S("lm2", 256 * t, 256 * t + 256), dd])
+        win, hh = (S("xb", 0, 4104), 0.0) if t == 0 else (VW, -H)
+        for h in range(2):
+            ts(S("xg", 1024 * h, 1024 * h + 1024), gat(win, S("loff", off + 64 * h, off + 64 * h + 64)), hh, None, ALU.add)
+            act(S("xg", 2048 + 1024 * h, 3072 + 1024 * h), gat(win, S("loff", off + 128 + 64 * h, off + 192 + 64 * h)), ID, hh)
+        if t > 1:
+            y_keep(t - 2, 0, S("p6", 256, 320))
+        bank = {0: "p0", 4: "p1", 1: "p2", 5: "p3", 2: "p4", 6: "p5", 7: "p1", 3: "p0"}
+
+        def e_mm(j, part=3):
+            if part & 1:
+                mm(S(bank[j]), m2, S("sel16", 512 * (j % 4), 512 * (j % 4) + 512), True, False)
+            if part & 2:
+                mm(S(bank[j]), IM3, S("xg", 512 * j, 512 * j + 512), False, True)
+
+        def direct(j):
+            b = 1.5 * 2.0 ** 28
+            ts(S("ind", 512 * j, 512 * j + 512), S(bank[j]), b, b, ALU.add, ALU.is_equal)
+
+        def absd(j):
+            act(S("ab", 512 * j, 512 * j + 512), S(bank[j]), AF.Abs)
+
+        def below(j):
+            ts(S("ind", 512 * j, 512 * j + 512), S("ab", 512 * j, 512 * j + 512), 16.0, None, ALU.is_lt)
+        for j in (0, 4, 1, 5):
+            e_mm(j, 1)
+        for j in (0, 4, 1, 5):
+            e_mm(j, 2)
+        for j in (2, 6):
+            e_mm(j, 1)
+        for j in (6, 2):
+            e_mm(j, 2)
+        direct(0); absd(4); e_mm(7); e_mm(3)
+        direct(1); absd(5); below(4); absd(6); direct(2); below(5); absd(7); below(6); absd(3); below(7)
+        for k in range(16):
+            mm(S("p7", 8 * k, 8 * k + 8, p1=96), S("ind", k, 1536, 16), S("bo"))
+        for k in range(16):
+            mm(S("p6", 128 + 8 * k, 136 + 8 * k), S("ind", 2048 + k, 4096, 16), S("bo"))
+        below(3)
+        for k in range(16):
+            mm(S("p7", 8 * k, 8 * k + 8, p0=96), S("ind", 1536 + k, 2048, 16), S("bo"))
+        if t == 0:
+            for j in range(4):
+                act(S("xh", 512 * j, 512 * j + 512), S("xb", 1024 * j, 1024 * j + 512), ID, H)
+        if last:
+            y_chunk(t - 1, 2, "p0")
+            for c in y_diff(t - 1, 3, "phi%d" % ((t - 1) % 2), "p1"):
+                mm(*c)
+        elif t > 1:
+            for c in y_sum(t - 2, 1, S("p2", 0, 64))[:12]:
+                mm(*c)
+        c0 = S("p7", 0, 128)
+        ts(S("e12"), S("p6", 128, 256), 12.0, 12.0, ALU.is_ge, ALU.mult)
+        tt(S("late"), c0, S("e12"), ALU.is_lt)
+        act(S("r01", 128, 256), S("p6", 128, 256), AF.Relu, -704.0, 64.0)
+        act(S("r01", 0, 128), c0, AF.Relu, -704.0, 64.0)
+        mm(S("p6", 384, 512), I1, S("r01", 128, 256), True, False)
+        mm(S("p6", 384, 512), I1, S("r01", 0, 128), False, True)
+        tt(S("pint"), S("late"), mp, ALU.add)
+        ts(S("loi"), S("pint"), 63, None, ALU.bitwise_and)
+        ts(S("hii"), S("pint"), 6, 63, ALU.arith_shift_right, ALU.bitwise_and)
+        ts(S("lo1"), S("loi"), 1.0, None, ALU.add)
+        ts(S("av"), S("hii"), -63.0, None, ALU.add)
+        tt(S("bv"), S("p6", 384, 512), S("lo1"), ALU.min)
+        act(S("hb"), S("bv"), AF.Sign)
+        mm(S("p7", 128, 256), S("av"), I64, True, False)
+        mm(S("p7", 128, 256), S("bv"), I1, False, False)
+        mm(S("p7", 128, 256), S("hb"), IM8K, False, True)
+        po = 128 * (t % 2)
+        dh = 128 * (t % 2)
+        nv = 128 if last else 96
+
+        def slot_done(s, pb, ramp):
+            c = 264 if ramp else 66 * s
+            if ramp:
+                act(S("cs", c, c + 64), S(pb, 0, 64), ID)
+            else:
+                act(S("cs", c + 1, c + 66), S(pb, 0, 65), ID)
+
+        def slot_diff(s, ramp):
+            c = 264 if ramp else 66 * s
+            d = 256 if ramp else 0
+            o = S("p6", 64 * s, 64 * s + 64)
+            mm(o, S("d2", d, d + 128), S("cs", c, c + 64), True, False)
+            mm(o, S("d2", d, d + 128), S("cs", c + 2, c + 66), False, False)
+            mm(o, S("d2", d + 128, d + 256), S("cs", c + 1, c + 65), False, True)
+
+        def slot_once(s, ramp):
+            ts(S("ub", 64 * s, 64 * s + 64), S("p6", 64 * s, 64 * s + 64), 1.0 if ramp else -1.0, -H, ALU.is_equal, ALU.mult)
+        pend = []
+        side = y_sum(t - 2, 1, S("p2", 0, 64))[0 if last else 12:] if t > 1 else []
+        na = [96]
+        for n in range(nv):
+            g, k = n // 16, n % 16
+            col = 8 * k + g
+            ts(S("oh", 128 * n, 128 * n + 128), S("tab"), S("av", col, col + 1), S("bv", col, col + 1), ALU.max, ALU.min)
+            o = S("p%d" % (4 + (g // 2) % 2), 0, 65, 1, 64 * (g % 2), 64 * (g % 2) + 64)
+            pend.append((o, S("oh", 128 * n, 128 * n + 64), S("oh", 128 * n + 63, 128 * n + 128), k == 0, k == 15))
+            if n % 4 == 3 or n >= nv - 4:
+                for c in pend:
+                    mm(*c, also=S("oh", 128 * n, 128 * n + 128))
+                pend = []
+                for c in side[:2]:
+                    mm(*c)
+                side = side[2:]
+            if not last and n % 6 == 5:
+                for m in (na[0], na[0] + 1):
+                    ga, ka = m // 16, m % 16
+                    ca = 8 * ka + ga
+                    act(S("oh", 128 * m, 128 * m + 64), S("tb2", 0, 64), AF.Relu, S("av", ca, ca + 1), -1.0)
+                    act(S("oh", 128 * m + 64, 128 * m + 128), S("tb2", 64, 128), AF.Relu, S("bv", ca, ca + 1), -1.0)
+                for m in (na[0], na[0] + 1):
+                    ga, ka = m // 16, m % 16
+                    mm(S("p3", 0, 64, 1, 64 * (ga % 2), 64 * (ga % 2) + 64), S("oh", 128 * m, 128 * m + 64),
+                       S("oh", 128 * m + 64, 128 * m + 128), ka == 0, ka == 15,
+                       also=S("oh", 128 * na[0] + 192, 128 * na[0] + 256))
+                na[0] += 2
+            if last and n == 35:
+                y_keep(t - 2, 1, S("p2", 0, 64))
+            if n == (0 if last else 5):
+                act(S("ptr"), S("p7", 128, 256), ID)
+                mm(S("p7", 0, 128), S("pm32", 16, 144), S("ptr"))
+                if last:
+                    y_exp("p1", S("exv", 1536, 2048))
+            if n == 11 and t > 1 and not last:
+                y_keep(t - 2, 1, S("p2", 0, 64))
+            if n == (15 if last else 27):
+                ts(S("poff", po, po + 128), S("p7", 0, 128), 12223.0, float(DUMMY), ALU.add, ALU.min)
+                if last:
+                    act(S("dhi", dh, dh + 128), dd, ID)
+                    tt(S("dlo", dh, dh + 128), dd, S("dhi", dh, dh + 128), ALU.subtract)
+                    for h in range(2):
+                        act(S(phi, 1024 * h, 1024 * h + 1024), gat(VW, S("poff", po + 64 * h, po + 64 * h + 64)), ID, -H)
+            if n == 19 and t == 0:
+                d2_constants()
+            if n == 35 and last:
+                y_gain(t - 1, 0)
+                scan(S("sc"), S("msk"), S("zz", 0, 1024), ALU.mult)
+                y_keep(t - 1, 0, S("sc", 15, 1024, 16))
+            if last and n in (51, 71, 87, 103):
+                j = (51, 71, 87, 103).index(n)
+                pb = ("p2", "p3", "p0", "p1")[j]
+                for c in y_diff(t, j, phi, pb):
+                    mm(*c)
+                y_exp(pb, S(pb) if j < 2 else S("exw", 512 * (j - 2), 512 * (j - 1)))
+            if not last and n in (43, 55, 75):
+                j = (43, 55, 75).index(n)
+                mm(S("p%d" % j), I1, S("xb", 1024 * j + 512, 1024 * j + 1024), True, False)
+            if n % 32 == 5 and n > 32:
+                slot_done(n // 32 - 1, "p%d" % (4 + (n // 32 - 1) % 2), False)
+            if n % 32 == 15 and n > 32:
+                slot_diff(n // 32 - 1, False)
+        s_last = nv // 32 - 1
+        slot_done(s_last, "p%d" % (4 + s_last % 2), False)
+        ts(S("ub", 0, 64 * s_last), S("p6", 0, 64 * s_last), -1.0, -H, ALU.is_equal, ALU.mult)
+        if not last:
+            slot_done(3, "p3", True)
+            slot_diff(3, True)
+            slot_once(3, True)
+        slot_diff(s_last, False)
+        if not last:
+            act(S("lt1"), S("late"), ID, 0.0, 1000.0)
+            act(S("dsc"), dd, ID, 0.0, 2.0 ** -21)
+            act(S("dhi", dh, dh + 128), dd, ID)
+            if t == 1:
+                arrive("arrS", 4 * n4, [S("lst", 8, 32)])
+            so = 8 * t
+            act(S("dl", 0, 8), S("lmp", 128 * t, 128 * t + 8), ID, 6144.0)
+            tt(S("dl", 8, 128), S("lmp", 128 * t + 8, 128 * t + 128), S("lmp", 128 * t, 128 * t + 120), ALU.subtract)
+            act(S("dl", 136, 256), S("dl", 8, 128), ID)
+            if t == 0:
+                tt(S("dl", 128, 136), S("lmp", 0, 8), S("lst", 0, 8), ALU.subtract)
+            else:
+                tt(S("dl", 128, 136, p1=64), S("lmp", 128 * t, 128 * t + 8, p1=64), S("lst", so, so + 8, p1=64), ALU.subtract)
+                tt(S("dl", 128 + t, 136, p0=64), S("lmp", 128 * t + t, 128 * t + 8, p0=64),
+                   S("lst", so, so + 8 - t, p0=64), ALU.subtract)
+                tt(S("dl", 128, 128 + t, p0=64), S("lmp", 128 * t, 128 * t + t, p0=64),
+                   S("lst", so + 8 - t, so + 8, p0=64), ALU.subtract)
+        if t > 0:
+            y_gain(t - 1, 2 if last else 0, 1)
+        slot_once(s_last, False)
+        for bq in ((0, 1, 2, 3) if last else (0, 1, 3, 2)):
+            for q in range(4):
+                mm(S("p7", 64 * q, 64 * q + 64, 1, 32 * bq, 32 * bq + 32), S("rl", 32 * q, 32 * q + 32),
+                   S("ub", 64 * bq, 64 * bq + 64))
+        if not last:
+            mm(S("p3"), I1, S("xb", 3584, 4096), True, False)
+        if t > 0:
+            y_gain(t - 1, 3 if last else 1, 1)
+        tt(S("ucum"), S("p7", 0, 256), S("ucum"), ALU.min)
+        for j in range(8):
+            pb = "p%d" % (((j // 2) % 2 if last else j // 2) if j % 2 else 4 + (j // 2) % 2)
+            if j % 2 and last:
+                mm(S(pb), IM8K if last else I1, S("gw" if last else "xb", 512 * j, 512 * j + 512), True, False)
+            for i in range(2):
+                hx = 2 * j + i
+                mm(S(pb, 256 * i, 256 * i + 256), S("ex", 128 * hx, 128 * hx + 128), S("ucum"),
+                   j % 2 == 0, j % 2 == 0 or i == 1)
+            c = 512 * j
+            if last:
+                if j % 2:
+                    act(S("gu", c, c + 512), S(pb), AF.Relu, -8.0, -1.0 / 8192)
+                else:
+                    tt(S("gu", c, c + 512), S(pb), S("gneg", c // 2, c // 2 + 512), ALU.mult)
+            elif j % 2:
+                act(S("vw", c, c + 512), S(pb), ID, H)
+            else:
+                tt(S("vw", c, c + 512), S(pb), S("xh", c // 2, c // 2 + 512), ALU.add)
+                if j == 2:
+                    cp(S("vw", 4096, 4098), S("vw", 0, 2))
+        if last:
+            for c in y_sum(t - 1, 1, S("p6", 384, 448)):
+                mm(*c)
+            GU = S("gu", 0, 4104)
+            act(S("xg", 0, 1024), gat(GU, S("poff", po, po + 64)), ID)
+            y_keep(t - 1, 1, S("p6", 384, 448))
+            tt(S("zw", 1024, 2048), gat(GU, S("poff", po + 64, po + 128)), S("exw"), ALU.mult)
+            for j in range(2):
+                tt(S("zw", 512 * j, 512 * j + 512), S("p%d" % (2 + j)), S("xg", 512 * j, 512 * j + 512), ALU.mult)
+            scan(S("sc"), S("msk"), S("zw", 0, 1024), ALU.mult)
+            for c in y_sum(t, 1, S("p4", 0, 64), "zw"):
+                mm(c[0], c[1], c[2], c[3], False)
+            for j in (1, 2, 3):
+                arrive("arrY%d" % j, 2 * n4, [S("ly", 128 * j, 128 * j + 128)])
+            for h in (1, 0):
+                pre = [S("sy", 64 * h, 64 * h + 64)] + [S("ly", 128 * j + 64 * h, 128 * j + 64 * h + 64) for j in (1, 2, 3)]
+                for i, r in enumerate(pre):
+                    mm(S("p4" if h else "p5", 0, 64), I32F, r, i == 0 and h == 0, i == 3)
+            act(S("yo", 64, 128), S("p4", 0, 64), ID)
+            tt(S("yo", 0, 64), S("p5", 0, 64), S("sc", 15, 1024, 16), ALU.add)
+            put("A", "dma", (("y",), S("yo"), "o0"), [S("yo")], [])
+            break
+        cp(S(phi, 0, 1024), gat(VW, S("poff", po, po + 64)))
+        act(S(phi, 1024, 2048), gat(VW, S("poff", po + 64, po + 128)), ID)
+        if t > 0:
+            for j in (2, 3):
+                for c in y_diff(t - 1, j, "phi%d" % ((t - 1) % 2), "p%d" % j):
+                    mm(*c)
+            y_exp("p2", S("exv", 1024, 1536))
+        for k in range(16):
+            mm(S("p6", 8 * k, 8 * k + 8), S(phi, k, 2048, 16), S("idb", 0, 128, 16))
+        for k in range(8):
+            mm(S("p7", 0, 128), S(phi, k, 2048, 16), I2, k == 0, False)
+        f0 = S("p6", 0, 128)
+        ts(S("nt"), f0, 1000.0, 2.0, ALU.max, ALU.mult)
+        tt(S("tl"), f0, S("lt1"), ALU.is_lt)
+        tt(S("lv", 8, 128), S("p6", 0, 120), S("nt", 8, 128), ALU.is_gt)
+        for h in range(2):
+            o = S("p5", 128 * h, 128 * h + 128)
+            mm(o, I1, S("tl"), True, False)
+            mm(o, IMG, S("lv", 8, 136), False, False)
+            mm(o, IGK, S("lv", 0, 128), False, True)
+        for k in range(8, 16):
+            mm(S("p7", 0, 128), S(phi, k, 2048, 16), I2, False, k == 15)
+        tt(S("dlo", dh, dh + 128), dd, S("dhi", dh, dh + 128), ALU.subtract)
+        b = 1.5 * 2.0 ** 40
+        act(S("a2", 128, 256), S("p7", 0, 128), ID, b)
+        act(S("a2", 0, 128), S("a2", 128, 256), ID, -b)
+        if t > 0:
+            y_exp("p3", S("exv", 1536, 2048))
+        for g in range(8):
+            scan(S("wt", g, 256, 8), S("p5", g, 256, 8), S("dl", g, 256, 8), ALU.add)
+        sd = 128 * t
+
+        def turn():
+            tt(S("dn"), S("fi"), S("x2"), ALU.add)
+            act(S("sd", sd, sd + 128, p1=64), S("dn", p1=64), ID)
+            act(S("sd", sd + 16, sd + 128, p0=64), S("dn", 0, 112, p0=64), ID)
+            act(S("sd", sd, sd + 16, p0=64), S("dn", 112, 128, p0=64), ID)
+            centre_parts(S("sd", sd, sd + 128))
+        dops = {
+            3: lambda: tt(S("tt"), S("a2", 0, 128), S("dsc"), ALU.mult),
+            5: lambda: tt(S("x2"), S("p7", 0, 128), S("a2", 0, 128), ALU.subtract),
+            6: lambda: ts(S("fi"), S("tt"), -0.46875, None, ALU.add),
+            8: turn,
+        }
+        for s in range(17):
+            i0 = 8 * max(s - 1, 0)
+            q = S("qb", 128 * s + i0, 128 * s + 128)
+            ts(q, S("wt", i0 + 8 * s, 128 + 8 * s), KEY * s, KEY * (s + 1), ALU.max, ALU.min)
+            if s < 9:
+                mm(S("p4", i0, 128), I32F, q, s == 0, False)
+        for s in (10, 12, 14, 16):
+            i0 = 8 * (s - 1)
+            w = S("qb", 128 * (s - 1) + i0, 128 * s)
+            tt(w, w, S("qb", 128 * s + i0, 128 * s + 128), ALU.add)
+            mm(S("p4", i0 - 8, 128), I32F, S("qb", 128 * (s - 1) + i0 - 8, 128 * s), False, s == 16)
+        for s in dops:
+            dops[s]()
+        ye = y_diff(t, 0, phi, "p0")
+        times_tail(S("p4", 0, 128), t + 1, ye)
+        y_exp("p0", S("exv", 0, 512))
+        send([(S("soff", 256 * t, 256 * t + 256), S("loff", 256 * t + 256, 256 * t + 512), nxt, engs(nxt, 2, 3)[0], "arrB%d" % (t + 1)),
+              (S("smp", sd, sd + 128), S("lmp", sd + 128, sd + 256), nxt, engs(nxt, 3, 4)[0], "arrB%d" % (t + 1))])
+        centre(S("sm2", 256 * t, 256 * t + 128))
+        send([(S("sm2", 256 * t, 256 * t + 256), S("lm2", 256 * t + 256, 256 * t + 512), nxt, engs(nxt, 0, 1)[0], "arrA%d" % (t + 1)),
+              (S("sd", sd, sd + 128), S("ld", sd + 128, sd + 256), nxt, engs(nxt, 1, 2)[0], "arrA%d" % (t + 1))])
+        if t == 0:
+            for j in range(4):
+                ts(S("gneg", 512 * j, 512 * j + 512), S("gw", 1024 * j, 1024 * j + 512), -1.0 / H, None, ALU.mult)
+        y_chunk(t, 1, "p1")
+        if t > 0:
+            for c in y_sum(t - 1, 0, S("p6", 256, 320)):
+                mm(*c)
+            y_gain(t - 1, 2)
+    return ops
+
+
+def order(ops):
+    hist = {}
+    banks = {}
+    deps = []
+    after = {}
+    for i, (q, kind, args, reads, writes, opt) in enumerate(ops):
+        d = set()
+        reads = reads + ([opt["also"]] if "also" in opt else [])
+        for acc, w in [(r, False) for r in reads] + [(x, True) for x in writes]:
+            name = acc[0]
+            if SCRATCH[name][0] == "psum":
+                st = banks.setdefault(name, [q, [], []])
+                if st[0] != q:
+                    st[:] = [q, [], st[1]]
+                d.update(st[2])
+                if q == "P":
+                    after[i] = st[1][-1:]
+                    continue
+            for j, a, ww in hist.get(name, []):
+                if (w or ww) and _meet(a, acc) and not (SCRATCH[name][0] == "psum" and ops[j][0] != q):
+                    d.add(j)
+        for acc, w in [(r, False) for r in reads] + [(x, True) for x in writes]:
+            name = acc[0]
+            if SCRATCH[name][0] == "psum" and i not in banks[name][1][-1:]:
+                banks[name][1].append(i)
+            h = hist.setdefault(name, [])
+            if w:
+                h[:] = [e for e in h if not (acc[5] == 1 and acc[1] <= e[1][1] and e[1][2] <= acc[2]
+                                             and acc[3] <= e[1][3] and e[1][4] <= acc[4])]
+            h.append((i, acc, w))
+        d.discard(i)
+        deps.append(d)
+    return deps, after
+
+
+CYC, PCYC, GATHER, HOP, FLIGHT = 0.00104, 0.00052, 1.56, 0.11, 2.2
+PASSES, PIECE = 6, 256
+
+
+def _cost(op):
+    q, kind, a = op[0], op[1], op[2]
+
+    def n(x):
+        return 16 * n(x[2]) if x[0] == "*" else (x[4] - x[3] + x[5] - 1) // x[5]
+
+    def two(*xs):
+        return all(SCRATCH[x[0]][2] in (BF, F16, U16) for x in xs if isinstance(x, tuple))
+    if kind == "mm":
+        return max(min(64, n(a[1])), n(a[2])) * PCYC * (4 if SCRATCH[a[1][0]][2] == F32 else 1)
+    if kind in ("dma", "send", "arr"):
+        return {"dma": 0.1, "send": 0.5, "arr": 0.0}[kind]
+    if kind in ("aff", "iota"):
+        return 0.17 + 2 * n(a[0]) * CYC
+    if kind == "ms":
+        return max(64, n(a[0]) * (0.5 if two(a[0]) else 1)) * CYC
+    if a[1][0] == "*":
+        return 0.06 + GATHER * n(a[1]) * CYC
+    if kind == "act":
+        return 0.03 + max(64, n(a[1])) * CYC
+    if kind == "tt":
+        return max(64, n(a[1]) * (1 if "psum" in (SCRATCH[a[1][0]][0], SCRATCH[a[2][0]][0]) else 2)) * CYC
+    return max(64, n(a[1]) * (0.5 if kind != "scan" and two(*a[:4]) else 1)) * CYC
+
+
+def schedule(ops, deps, after):
+    n = len(ops)
+    cost = [_cost(o) for o in ops]
+    pred = [[(j, HOP) for j in deps[i]] + [(j, 0.0) for j in after.get(i, [])] for i in range(n)]
+    sender = {}
+    for i, o in enumerate(ops):
+        if o[1] == "send":
+            for tr in o[2][0]:
+                sender[tr[4]] = i
+        if o[1] == "arr":
+            pred[i] = [(sender[o[2][0]], FLIGHT - 0.5 - HOP)]
+    for i in range(n):
+        pred[i] = [(j, (2.0 if ops[j][2][0][0] in ("ivi", "tai", "pfi") else 4.5) if ops[j][1] == "dma" else w) for j, w in pred[i]]
+    succ = [[] for _ in range(n)]
+    for i in range(n):
+        for j, w in pred[i]:
+            succ[j].append((i, w))
+    rank = [0.0] * n
+    for i in range(n - 1, -1, -1):
+        rank[i] = cost[i] + max([w + rank[k] for k, w in succ[i]] + [0.0])
+
+    def lay(seq, before):
+        start = [0.0] * n
+        gaps = {}
+        for i in seq:
+            t = max([start[j] + cost[j] + w for j, w in before[i]] + [0.0])
+            c = cost[i] + 1e-6
+            gl = gaps.setdefault(ops[i][0], [[0.0, 1e9]])
+            lo, hi = 0, len(gl) - 1
+            while lo < hi:
+                mid = (lo + hi) // 2
+                if gl[mid][1] < t + c:
+                    lo = mid + 1
+                else:
+                    hi = mid
+            while gl[lo][1] - max(gl[lo][0], t) < c:
+                lo += 1
+            a, b = gl[lo]
+            t = max(a, t)
+            gl[lo:lo + 1] = [e for e in ([a, t], [t + c, b]) if e[1] - e[0] > 0.004]
+            start[i] = t
+        return start, max(start[i] + cost[i] for i in range(n))
+    best = None
+    for seq in (list(range(n)), sorted(range(n), key=lambda i: (-rank[i], i))):
+        for _ in range(PASSES):
+            start, span = lay(seq, pred)
+            if best is None or span < best[0]:
+                best = (span, start)
+            back, _ = lay(sorted(range(n), key=lambda i: (-(start[i] + cost[i]), -i)), succ)
+            seq = sorted(range(n), key=lambda i: (-(back[i] + cost[i]), i))
+    return sorted(range(n), key=lambda i: (best[1][i], i))
+
+
+def rank_program(g, core, T, topo):
+    rank = T.rank_of(core)
+    if rank is None:
+        return
+    ops = plan(rank, list(T.cores), topo)
+    deps, after = order(ops)
+    seq = schedule(ops, deps, after)
+    place = {j: i for i, j in enumerate(seq)}
+    ops = [ops[j] for j in seq]
+    deps = [set(place[k] for k in deps[j]) for j in seq]
+    queue = {"P": g.tensor, "V": g.vector, "A": g.scalar, "G": g, "S": g.sync}
+
+    def own(j):
+        return ops[j][1] in ("dma", "arr")
+    need = []
+    marked = set()
+    for i, d in enumerate(deps):
+        best = {}
+        for j in d:
+            if ops[j][1] == "send":
+                continue
+            key = ("own", j) if own(j) else ops[j][0]
+            best[key] = max(best.get(key, -1), j)
+        need.append(best)
+    seen = {}
+    for i, best in enumerate(need):
+        s = seen.setdefault(ops[i][0], {})
+        for key in list(best):
+            if ops[i][0] == "X" or s.get(key, -1) >= best[key]:
+                del best[key]
+            else:
+                s[key] = best[key]
+                marked.add(best[key])
+    count = {}
+    ticket = {}
+    for i, o in enumerate(ops):
+        if o[1] == "dma":
+            ticket[i] = (o[2][2], 16)
+        elif o[1] == "arr":
+            ticket[i] = o[2]
+        elif i in marked:
+            count[o[0]] = count.get(o[0], 0) + 1
+            ticket[i] = ("c" + o[0], count[o[0]])
+
+    def ap(x):
+        if not isinstance(x, tuple):
+            return x
+        if x[0] == "*":
+            return ap(x[1]).indirect(ap(x[2]))
+        if len(x) == 1:
+            return T[x[0]][:]
+        if len(x) == 3:
+            return T[x[0]][:, x[1]:x[2]]
+        if x[5] == 1:
+            return T[x[0]][x[1]:x[2], x[3]:x[4]]
+        return T[x[0]][x[1]:x[2], x[3]:x[4]:x[5]]
+
+    sent = 0
+    waited = set()
+    for i, (q, kind, a, reads, writes, opt) in enumerate(ops):
+        if kind == "arr":
+            continue
+        e = queue[q]
+        for key in need[i]:
+            s, n = ticket[need[i][key]]
+            e.wait_ge(T.sem[s], n)
+            waited.add((s, n))
+        if kind == "ts":
+            if a[5] is None:
+                ins = e.tensor_scalar(ap(a[0]), ap(a[1]), ap(a[2]), None, a[4])
+            else:
+                ins = e.tensor_scalar(ap(a[0]), ap(a[1]), ap(a[2]), ap(a[3]), a[4], a[5])
+        elif kind == "tt":
+            ins = e.tensor_tensor(ap(a[0]), ap(a[1]), ap(a[2]), a[3])
+        elif kind == "cp":
+            ins = e.tensor_copy(ap(a[0]), ap(a[1]))
+        elif kind == "ms":
+            ins = e.memset(ap(a[0]), a[1])
+        elif kind == "scan":
+            ins = e.tensor_tensor_scan(ap(a[0]), ap(a[1]), ap(a[2]), 0.0, a[3], ALU.add)
+        elif kind == "act":
+            ins = e.activation(ap(a[0]), ap(a[1]), a[2], bias=ap(a[3]), scale=a[4])
+        elif kind == "mm":
+            ins = e.matmul(ap(a[0]), ap(a[1]), ap(a[2]), a[3], a[4])
+        elif kind == "aff":
+            ins = e.affine_select(ap(a[0]), ap(a[1]), a[2], a[3], 0.0, a[4], a[5])
+        elif kind == "iota":
+            ins = e.iota(ap(a[0]), a[1], a[2], 0, allow_small_or_imprecise_dtypes=True)
+        elif kind == "dma":
+            e.dma_start(ap(a[0]), ap(a[1])).then_inc(T.sem[a[2]], 16)
+            continue
+        else:
+            trs = []
+            for src, dst, c, mask, sem in a[0]:
+                rid, pid, _ = topo.addr(c)
+                trs.append(RemoteDMATransfer(dst_ids=[DstId(rid=rid, pnc=pid)], dma_engine_mask=mask,
+                                             remote_sem=T.sem[sem], src=ap(src), dst=ap(dst)))
+                sent += bin(mask).count("1")
+            e.remote_dma_fused(trs, local_sem=T.sem.sent)
+            continue
+        if i in ticket:
+            ins.then_inc(T.sem[ticket[i][0]], 1)
+    g.wait_ge(T.sem.sent, sent)
+    for i in ticket:
+        if own(i) and ticket[i] not in waited:
+            g.sync.wait_ge(T.sem[ticket[i][0]], ticket[i][1])

@@ -3,75 +3,108 @@ from concourse.mybir import AluOpType as ALU, ActivationFunctionType as AF
 
 F32, BF, F16, I32, U16 = "float32", "bfloat16", "float16", "int32", "uint16"
 NV = 5
-H = 65536.0
 KEY = 16384.0
 BIGL = 1048576.0
 DUMMY = 4098
-RINT = 1.5 * 2.0 ** 23
+KAP = 51.0 / 32
+TW = 130
+CS = 68
+WW = 4112
 
 SCRATCH = {
-    "xb": ("sbuf", [128, 4112], BF), "gw": ("sbuf", [128, 4112], BF), "vw": ("sbuf", [128, 4104], F32),
-    "xh": ("sbuf", [128, 2048], F32), "gneg": ("sbuf", [128, 2048], BF), "gu": ("sbuf", [128, 4112], BF),
+    "vw": ("sbuf", [128, 5 * WW], BF), "gw": ("sbuf", [128, 4 * WW], BF),
+    "gneg": ("sbuf", [128, 2048], BF), "gu": ("sbuf", [128, WW], BF),
     "ivi": ("sbuf", [128, 128], I32), "pfi": ("sbuf", [128, 128], I32), "tai": ("sbuf", [128, 128], I32),
     "ivf": ("sbuf", [128, 128], F32), "pff": ("sbuf", [128, 128], F32), "taf": ("sbuf", [128, 128], F32),
-    "one32": ("sbuf", [128, 128], F32), "oneb": ("sbuf", [128, 512], BF),
+    "one32": ("sbuf", [128, 128], F32), "oneb": ("sbuf", [128, 512], BF), "zr": ("sbuf", [128, 256], BF),
     "ix": ("sbuf", [128, 256], F32), "trip": ("sbuf", [128, 128], F32), "tri0": ("sbuf", [128, 128], F32),
-    "tsel": ("sbuf", [128, 128], F32),
-    "idb": ("sbuf", [128, 9 * 128], BF), "id16": ("sbuf", [128, 128], F16),
-    "pm32": ("sbuf", [128, 144], F32), "pm16": ("sbuf", [128, 144], F16),
-    "sel16": ("sbuf", [128, 2048], F16), "selb": ("sbuf", [128, 2048], BF),
-    "ex": ("sbuf", [128, 2048], BF), "rl": ("sbuf", [128, 128], BF), "r01": ("sbuf", [128, 256], BF), "msk": ("sbuf", [128, 1024], BF),
-    "bo0": ("sbuf", [128, 8], BF), "bo": ("sbuf", [128, 8], BF),
-    "tab": ("sbuf", [128, 128], BF), "tb2": ("sbuf", [128, 128], BF),
+    "tsel": ("sbuf", [128, 128], F32), "blk": ("sbuf", [128, 128], F32), "bl2": ("sbuf", [128, 256], BF),
+    "idb": ("sbuf", [128, 12 * 128], BF), "id16": ("sbuf", [128, 128], F16),
+    "jj": ("sbuf", [128, 64], BF), "selk": ("sbuf", [128, 1024], BF),
+    "ex": ("sbuf", [128, 2048], BF), "rl": ("sbuf", [128, 160], BF), "msk": ("sbuf", [128, 1024], BF),
+    "bo1": ("sbuf", [128, 8], BF), "bo0": ("sbuf", [128, 8], BF), "bo": ("sbuf", [128, 8], BF),
+    "fw": ("sbuf", [128, 96], BF), "ci": ("sbuf", [128, 384], BF), "co": ("sbuf", [128, 8, 32], BF),
+    "ca": ("sbuf", [128, 128], BF), "cr": ("sbuf", [128, 128], F16),
+    "tab": ("sbuf", [128, TW], BF), "tb2": ("sbuf", [128, TW], BF),
     "d2a": ("sbuf", [128, 128], F32), "d2b": ("sbuf", [128, 256], F32), "d2": ("sbuf", [128, 512], F32),
-    "loff": ("sbuf", [128, 5 * 256], U16), "lmp": ("sbuf", [128, 5 * 128], F32),
-    "lm2": ("sbuf", [128, 5 * 256], F16), "ld": ("sbuf", [128, 5 * 128], F32),
-    "soff": ("sbuf", [128, 4 * 256], U16), "smp": ("sbuf", [128, 4 * 128], F32),
-    "sm2": ("sbuf", [128, 4 * 256], F16), "sd": ("sbuf", [128, 4 * 128], F32),
-    "lst": ("sbuf", [128, 4 * 8], F32), "ly": ("sbuf", [128, 4 * 128], F32), "sy": ("sbuf", [128, 4 * 128], F32),
-    "xg": ("sbuf", [128, 4096], BF), "ab": ("sbuf", [128, 4096], BF), "ind": ("sbuf", [128, 4096], BF),
-    "e12": ("sbuf", [128, 128], F32), "late": ("sbuf", [128, 128], BF), "hm": ("sbuf", [128, 128], BF),
-    "hb": ("sbuf", [128, 128], BF), "pint": ("sbuf", [128, 128], I32), "loi": ("sbuf", [128, 128], I32),
-    "hii": ("sbuf", [128, 128], I32), "lo1": ("sbuf", [128, 128], BF), "av": ("sbuf", [128, 128], BF),
-    "bv": ("sbuf", [128, 128], BF), "lt1": ("sbuf", [128, 128], F32),
-    "oh": ("sbuf", [128, 16384], BF), "ptr": ("sbuf", [128, 128], F32), "poff": ("sbuf", [128, 256], U16),
-    "cs": ("sbuf", [128, 330], F32), "ub": ("sbuf", [128, 256], BF), "ucum": ("sbuf", [128, 256], BF),
-    "phi0": ("sbuf", [128, 2048], BF), "phi1": ("sbuf", [128, 2048], BF), "dl": ("sbuf", [128, 256], F32),
-    "nt": ("sbuf", [128, 128], F32), "tl": ("sbuf", [128, 128], BF), "lv": ("sbuf", [128, 136], BF),
-    "wt": ("sbuf", [128, 256], F32), "qb": ("sbuf", [128, 17 * 128], F32),
-    "rnd": ("sbuf", [128, 128], F32), "m16": ("sbuf", [128, 128], F16), "mt16": ("sbuf", [128, 128], F16),
-    "dsc": ("sbuf", [128, 128], F32), "a2": ("sbuf", [128, 256], F32), "x2": ("sbuf", [128, 128], F32),
-    "tt": ("sbuf", [128, 128], F32), "fi": ("sbuf", [128, 128], I32), "dn": ("sbuf", [128, 128], F32),
-    "fc": ("sbuf", [128, 512], F32), "dhi": ("sbuf", [128, 256], BF), "dlo": ("sbuf", [128, 256], BF),
+    "off": ("sbuf", [128, 256], U16), "zp": ("sbuf", [128, 512], BF), "ta": ("sbuf", [128, 8, 16], F16),
+    "av": ("sbuf", [128, 128], BF), "r0m": ("sbuf", [128, 128], F16), "st": ("sbuf", [128, 16], F16),
+    "xg": ("sbuf", [128, 4096], BF), "ind": ("sbuf", [128, 4096], BF),
+    "t2a": ("sbuf", [128, 128], F16), "t2": ("sbuf", [128, 128], BF), "uu": ("sbuf", [128, 128], BF),
+    "bv": ("sbuf", [128, 128], BF), "non": ("sbuf", [128, 128], BF), "nn": ("sbuf", [128, 128], BF),
+    "oh": ("sbuf", [128, 128 * TW], BF), "poff": ("sbuf", [128, 128], U16), "pofy": ("sbuf", [128, 256], U16),
+    "cs": ("sbuf", [128, 5 * CS], F32), "cb": ("sbuf", [128, 4 * 66], BF), "ub": ("sbuf", [128, 256], BF),
+    "phi0": ("sbuf", [128, 2048], BF), "phi1": ("sbuf", [128, 2048], BF),
+    "fl": ("sbuf", [128, 16, 17], BF), "wt": ("sbuf", [128, 8, 32], F32), "qb": ("sbuf", [128, 16 * 8, 16], F32),
+    "rnd": ("sbuf", [128, 8, 16], F32), "h128": ("sbuf", [128, 128], BF), "hr": ("sbuf", [128, 128], BF),
+    "sa": ("sbuf", [128, 128], BF), "sb": ("sbuf", [128, 128], BF), "mu": ("sbuf", [128, 128], BF),
+    "tt": ("sbuf", [128, 128], F32), "fi": ("sbuf", [128, 128], I32),
     "exv": ("sbuf", [128, 2048], F32), "exw": ("sbuf", [128, 1024], F32), "zz": ("sbuf", [128, 2048], F32),
     "zw": ("sbuf", [128, 2048], F32), "sc": ("sbuf", [128, 1024], F32), "yo": ("sbuf", [128, 128], F32),
 }
-for _b in range(8):
+for _b in range(6):
     SCRATCH["p%d" % _b] = ("psum", [128, 512], F32)
+SCRATCH["pf_"] = ("psum", [128, 32, 16], F32)
+SCRATCH["pt_"] = ("psum", [128, 16, 32], F32)
+PF, PT = "pf_", "pt_"
 
-SEMAPHORES = (["cP", "cV", "cA", "cG", "sent", "arrS", "l0", "l1", "l2", "l3", "l4", "l5", "l6", "o0", "o1"]
-              + ["arrA%d" % t for t in range(1, 5)] + ["arrB%d" % t for t in range(1, 5)]
-              + ["arrY%d" % t for t in range(1, 4)])
+SEMAPHORES = (["cP", "cV", "cA", "cG", "sent", "l0", "l1", "l2", "l3", "l4", "l5", "o0"]
+              + ["arrW%d" % t for t in range(1, 5)] + ["arrX%d" % t for t in range(1, 5)] + ["arrG%d" % t for t in range(1, 4)])
+
+PIECE, MERGE, NA, Y2, DS = 256, 9, 68, 12, 8
+YL = (7, 39, 71, 103)
+VG, VP, VU, SCAN = 512, 768, 4, (1, 2, 3)
+
+
+def _piece(name, p0, p1, dims):
+    shape = SCRATCH[name][1]
+    if len(dims) == 1:
+        a, b, s = dims[0]
+        cols = range(a, b, s)
+        mask = ((1 << (b - a)) - 1) << a if s == 1 else sum(1 << c for c in cols)
+        return (name, p0, p1, dims, mask, len(cols))
+    (a, b, _), (c, d, _) = dims
+    row = ((1 << (d - c)) - 1) << c
+    return (name, p0, p1, dims, sum(row << (r * shape[2]) for r in range(a, b)), (b - a) * (d - c))
 
 
 def S(name, c0=None, c1=None, step=1, p0=0, p1=128):
+    shape = SCRATCH[name][1]
     if c0 is None:
-        c0, c1 = 0, SCRATCH[name][1][1]
-    return (name, p0, p1, c0, c1, step)
+        c0, c1 = 0, shape[1] * (shape[2] if len(shape) == 3 else 1)
+    if len(shape) == 3:
+        return _piece(name, p0, p1, ((c0 // shape[2], c1 // shape[2], 1), (0, shape[2], 1)))
+    return _piece(name, p0, p1, ((c0, c1, step),))
+
+
+def R(name, a0, a1, b0, b1, p0=0, p1=128):
+    return _piece(name, p0, p1, ((a0, a1, 1), (b0, b1, 1)))
 
 
 def _meet(a, b):
-    if a[0] != b[0] or a[2] <= b[1] or b[2] <= a[1] or a[4] <= b[3] or b[4] <= a[3]:
-        return False
-    if a[5] == b[5] and a[5] > 1 and (a[3] - b[3]) % a[5]:
-        return False
-    return True
+    return a[2] > b[1] and b[2] > a[1] and (a[4] & b[4]) != 0
 
 
 def plan(rank, cores, topo):
     ops = []
+    late = [0]
+    seen = {}
+
+    def side(on):
+        late[0] += 1 if on else -1
+
+    def filler(f):
+        def run(*a, **k):
+            side(True)
+            f(*a, **k)
+            side(False)
+        return run
 
     def put(q, kind, args, reads, writes, **opt):
+        opt["late"] = late[0] > 0
+        name = (q, kind, args[0][0] if kind != "send" else "")
+        seen[name] = seen.get(name, 0) + 1
+        opt["kind"] = name + (seen[name],)
         ops.append((q, kind, args, [r for r in reads if isinstance(r, tuple)], writes, opt))
 
     def rd(x):
@@ -107,482 +140,407 @@ def plan(rank, cores, topo):
     def gat(win, off):
         return ("*", win, off)
 
-    def send(trs):
-        put("G", "send", (trs,), [t[0] for t in trs], [])
+    def send(trs, after=()):
+        put("G", "send", (trs,), [t[0] for t in trs] + list(after), [])
 
     def arrive(sem, n, bufs):
         put("X", "arr", (sem, n), [], bufs)
 
-    def ident(i):
-        return S("idb", 128 * i, 128 * i + 128)
-    I1, IM3, IM32, I2, IMG, IGK, I64, IM128, IM8K = [ident(i) for i in range(9)]
+    scales = (1.0, -32 * KAP, 32 * KAP, -BIGL, BIGL + KEY, 64.0, -1.0, 128.0, -2.0, 0.5, -32.0, -4096.0)
+    I1, IMK, IPK, IMG, IGK, I64, IM1, I128, IM2, IHALF, IM32, IM4K = [S("idb", 128 * i, 128 * i + 128) for i in range(12)]
     I32F = S("ix", 0, 128)
     ID = AF.Identity
-    me = cores[rank]
-
-    def engs(dst, a, b):
-        e = topo.engines(me, dst)
-        n = len(e) // 4
-        return sum(1 << x for x in e[a * n:b * n]), (b - a) * n
+    prev = cores[(rank - 1) % 4]
+    engines = topo.engines(cores[rank], prev)
+    mask = sum(1 << e for e in engines)
 
     put("S", "dma", (S("ivi"), ("iv",), "l0"), [], [S("ivi")])
     put("A", "dma", (S("tai", p1=8), ("tau",), "l1"), [], [S("tai", p1=8)])
-    put("S", "dma", (S("xb", 0, 2048), ("xs", 0, 2048), "l2"), [], [S("xb", 0, 2048)])
-    put("A", "dma", (S("xb", 2048, 4096), ("xs", 2048, 4096), "l3"), [], [S("xb", 2048, 4096)])
     put("S", "dma", (S("pfi"), ("pf",), "l4"), [], [S("pfi")])
+    put("A", "dma", (S("vw", 2048, 4096), ("xs", 2048, 4096), "l3"), [], [S("vw", 2048, 4096)])
+    put("S", "dma", (S("vw", 0, 2048), ("xs", 0, 2048), "l2"), [], [S("vw", 0, 2048)])
     ms(S("one32"), 1.0)
     ms(S("oneb"), 1.0)
-    aff(S("tri0"), S("one32"), [[0, 16], [-16, 8]], ALU.is_ge, 0, 1)
     aff(S("ix", 0, 128), S("one32"), [[-1, 128]], ALU.is_equal, 0, 1)
-    aff(S("trip"), S("tri0"), [[1, 16], [16, 8]], ALU.is_ge, 0, -1)
-    aff(S("tsel"), S("one32"), [[0, 16], [-1, 8]], ALU.is_equal, 0, 1)
-    aff(S("pm32", 16, 144), S("one32"), [[-1, 8], [-8, 16]], ALU.is_equal, 0, 1)
-    aff(S("bo0"), S("oneb", 0, 8), [[-16, 8]], ALU.is_ge, 0, 1)
-    iota(S("tab", 0, 63), [[1, 63]], -63)
+    aff(S("tri0"), S("one32"), [[-16, 8], [0, 16]], ALU.is_ge, 0, 1)
+    aff(S("trip"), S("tri0"), [[16, 8], [1, 16]], ALU.is_ge, 0, -1)
+    aff(S("tsel"), S("one32"), [[-1, 8], [0, 16]], ALU.is_equal, 0, 1)
+    ms(S("bo1"), 128.0)
+    aff(S("bo0"), S("bo1"), [[-16, 8]], ALU.is_ge, 0, 1)
     aff(S("bo"), S("bo0"), [[16, 8]], ALU.is_ge, 15, -1)
-    iota(S("tab", 63, 128), [[1, 65]], 1)
-    iota(S("tb2"), [[1, 128]], -64)
-    ms(S("vw", 4096, 4104), H)
-    ms(S("xb", 4096, 4112), 0.0)
-    ms(S("gw", 4096, 4112), 0.0)
-    ms(S("gu", 4096, 4112), 0.0)
-    ms(S("ucum"), 0.0)
-    ms(S("lv"), 0.0)
-    ms(S("cs"), 0.0)
-    ms(S("sm2"), 0.0)
+    iota(S("tab", 0, 66), [[-1, 66]], 66)
+    iota(S("tab", 66, TW), [[1, TW - 66]], -63)
+    iota(S("tb2", 0, 64), [[1, 64]], -64)
+    iota(S("tb2", 64, TW), [[-1, TW - 64]], 64)
+    ms(S("vw", 4096, WW), 1.0)
+    ms(S("ca"), -1408.0)
+    ms(S("cr"), -1407.0)
     cp(S("id16"), I32F)
-    for k in range(8):
-        ts(S("sel16", k, 2048, 16), S("id16"), 1.5, None, ALU.mult)
+    cp(I1, I32F)
+    tt(S("jj"), S("idb", 0, 64), S("idb", 64, 128), ALU.add)
     cp(S("ivf"), S("ivi"))
     ts(S("taf", p1=8), S("tai", p1=8), 2048.0, None, ALU.add)
-    cp(S("pm16", 16, 144), S("pm32", 16, 144))
-    cp(S("pm16", 0, 16), S("pm32", 128, 144))
     act(S("ix", 128, 256), I32F, ID)
-    for ap, v in ((IM3, -3.0), (I1, 1.0), (I64, 64.0), (IM128, -128.0), (IM32, -32.0), (I2, 2.0), (IMG, -BIGL),
-                  (IGK, BIGL + KEY), (IM8K, -8192.0)):
-        act(ap, I32F, ID, 0.0, v)
-    act(S("d2b"), S("ix"), ID, 0.0, -2.0)
+    for i in range(1, 12):
+        filler(act)(S("idb", 128 * i, 128 * i + 128), I32F, ID, 0.0, scales[i])
+    filler(act)(S("d2b"), S("ix"), ID, 0.0, -2.0)
+    ta = S("ta")
 
-    def times_tail(acc, t1, fill=()):
-        home = t1 == 0
-        off = ("loff", 0) if home else ("soff", 256 * (t1 - 1))
-        mp = ("lmp", 0) if home else ("smp", 128 * (t1 - 1))
+    def times_tail(t1):
         b = 1.5 * 2.0 ** 35
-        for c in fill[:2]:
-            mm(*c)
-        ts(S("rnd"), acc, b, b, ALU.add, ALU.subtract)
-        tt(S("m16"), acc, S("rnd"), ALU.subtract)
-        mm(S("p7", 0, 128), S("m16"), S("id16"))
-        for c in fill[2:]:
-            mm(*c)
-        o = mp[1]
-        if home:
-            ts(S(mp[0], o, o + 128), S("m16"), 2048.0, None, ALU.add)
+        ts(S("rnd"), R(PT, 8, 16, 0, 16), b, b, ALU.add, ALU.subtract)
+        if t1 == 0:
+            tt(ta, R(PT, 8, 16, 0, 16), S("rnd"), ALU.subtract)
         else:
-            ts(S(mp[0], o + 1, o + 128, p0=64), S("m16", 0, 127, p0=64), 2048.0, None, ALU.add)
-            ts(S(mp[0], o, o + 128, p1=64), S("m16", p1=64), 2048.0, None, ALU.add)
-            ts(S(mp[0], o, o + 128, 8, p0=64), S("m16", 7, 128, 8, p0=64), 2048.0, None, ALU.add)
-        cp(S("mt16"), S("p7", 0, 128))
-        mm(S("p6", 0, 64), S("pm16", 16, 144), S("mt16", 0, 64))
-        mm(S("p6", 64, 128), S("pm16", 16, 144) if home else S("pm16", 0, 128), S("mt16", 64, 128))
-        ts(S(off[0], off[1], off[1] + 128), S("p6", 0, 128), 2048.0, None, ALU.add)
-        ts(S(off[0], off[1] + 128, off[1] + 256), S("p6", 0, 128), 2049.0, None, ALU.add)
+            tt(S("ta", p1=64), R(PT, 8, 16, 0, 16, p1=64), S("rnd", p1=64), ALU.subtract)
+            tt(R("ta", 1, 8, 0, 16, p0=64), R(PT, 8, 15, 0, 16, p0=64), R("rnd", 0, 7, 0, 16, p0=64), ALU.subtract)
+            tt(R("ta", 0, 1, 0, 16, p0=64), R(PT, 15, 16, 0, 16, p0=64), R("rnd", 7, 8, 0, 16, p0=64), ALU.subtract)
+        mm(R(PT, 0, 8, 0, 16), ta, S("id16"))
+        ts(S("off", 128, 256), R(PT, 0, 8, 0, 16), 2049.0, None, ALU.add)
+        ts(S("off", 0, 128), S("off", 128, 256), 1.0, None, ALU.subtract)
 
-    def centre_parts(d):
-        act(S("fc", 0, 128), d, ID, -0.484375, 1.0 / 32)
-        act(S("fc", 128, 256), d, ID, -0.484375, -1.0 / 32)
-        act(S("fc", 256, 384), S("fc", 0, 128), ID, RINT)
-        act(S("fc", 384, 512), S("fc", 128, 256), ID, RINT)
+    def digits(step):
+        if step == 0:
+            act(S("h128"), ta, ID, 192.0 - 63.0 / 128, 1.0 / 64)
+            act(S("hr"), S("h128"), AF.Relu, -223.0 * 64, 64.0)
+            mm(S(PF, 0, 128), IM1, ta, True, False)
+            mm(S(PF, 0, 128), I64, S("h128"), False, True)
+            mm(S(PF, 128, 256), I1, S("h128"), True, False)
+            mm(S(PF, 128, 256), IM1, S("hr"), False, True)
+        else:
+            act(S("r0m"), S(PF, 0, 128), ID, -12223.0 + 1407.0)
+            act(S("av"), S(PF, 128, 256), ID, -223.0)
 
-    def centre(m2):
-        tt(m2, S("fc", 256, 384), S("fc", 384, 512), ALU.subtract)
+    def parts(t1, step):
+        o = 256 * (t1 % 2)
+        up = 128 if t1 == 0 else 112
+        if step == 0:
+            if t1:
+                cp(S("p4", 112, 128, p0=64), S("p4", 240, 256, p0=64))
+            act(S("zp", o, o + 128, p1=64), S("p4", 128, 256, p1=64), ID)
+            act(S("zp", o + 128, o + 256, p0=64), S("p4", up, up + 128, p0=64), ID)
+        else:
+            tt(S("zp", o, o + 128, p0=64), S("p4", 128, 256, p1=64), S("zp", o, o + 128, p1=64), ALU.subtract)
+            tt(S("zp", o + 128, o + 256, p1=64), S("p4", up, up + 128, p0=64), S("zp", o + 128, o + 256, p0=64), ALU.subtract)
 
-    mm(S("p4", 0, 128), S("ivf"), S("trip"), True, False)
-    mm(S("p4", 0, 128), S("taf", p1=8), S("tsel", p1=8), False, True)
-    mm(S("p5", 0, 8), S("taf", p1=8), S("ix", 0, 8, p1=8))
+    mm(R(PT, 8, 16, 0, 16), S("ivf"), S("trip"), True, False)
+    mm(R(PT, 8, 16, 0, 16), S("taf", p1=8), S("tsel", p1=8), False, True)
+    mm(S("p3", 0, 8), S("taf", p1=8), S("ix", 0, 8, p1=8))
     cp(S("pff"), S("pfi"))
-    mm(S("p3", 0, 128), S("pff"), I32F)
-    act(S("lst", 0, 8), S("p5", 0, 8), ID, -2048.0)
-    act(S("ld", 0, 128), S("p3", 0, 128), ID)
-    centre_parts(S("ld", 0, 128))
-    times_tail(S("p4", 0, 128), 0)
-    put("S", "dma", (S("gw", 0, 4096), ("gn",), "l5"), [S("loff", 0, 256)], [S("gw", 0, 4096)])
-    trs = []
-    for j, (a, b) in ((1, (0, 1)), (2, (1, 2)), (3, (2, 4))):
-        dst = cores[(rank + j) % 4]
-        trs.append((S("lst", 0, 8), S("lst", 8 * j, 8 * j + 8), dst, engs(dst, a, b)[0], "arrS"))
-    send(trs)
-    for k in range(8, 16):
-        ts(S("sel16", k, 2048, 16), S("id16"), 1.5, None, ALU.mult)
-    centre(S("lm2", 0, 128))
-    cp(S("xb", 4096, 4098), S("xb", 0, 2))
-    aff(S("rl"), S("oneb", 0, 128), [[-1, 4], [-64, 2], [-4, 16]], ALU.is_equal, 0, 1)
+    mm(S("p4", 128, 256), S("pff"), I32F)
+    times_tail(0)
+    for h in range(2):
+        act(S("st", 8 * h, 8 * h + 8), S("p3", 0, 8), ID, -4096.0)
+    parts(0, 0)
+    parts(0, 1)
+    for k in range(16):
+        ts(S("selk", k, 1024, 16), S("jj"), KAP, None, ALU.mult)
+    cp(S("vw", 4096, 4098), S("vw", 0, 2))
+    put("S", "dma", (S("gw", 0, 4096), ("gn",), "l5"), [S("off", 128, 256)], [S("gw", 0, 4096)])
+    aff(S("rl", 0, 128), S("oneb", 0, 128), [[-1, 4], [-64, 2], [-4, 16]], ALU.is_equal, 0, 1)
+    aff(S("rl", 128, 160), S("oneb", 0, 32), [[-64, 2], [-4, 16]], ALU.is_equal, 1, 1)
+    aff(S("blk"), S("tri0"), [[16, 8], [0, 16]], ALU.is_ge, 15, -1)
     for j in range(4):
         aff(S("ex", 512 * j, 512 * j + 512), S("oneb"), [[-1, 4], [-16, 8], [0, 16]], ALU.is_equal, -4 * j, 1)
-    for j in range(4):
-        aff(S("selb", 512 * j, 512 * j + 512), S("oneb"), [[-1, 32], [0, 16]], ALU.is_equal, -32 * j, 1)
-    for j in range(2):
-        aff(S("msk", 512 * j, 512 * j + 512), S("oneb"), [[0, 32], [1, 16]], ALU.is_gt, 0, 0)
 
-    def d2_constants():
-        tt(S("d2a"), S("ix", 127, 255), S("ix", 1, 129), ALU.add)
-        tt(S("d2", 0, 128), S("d2a"), S("d2b", 0, 128), ALU.add)
-        tt(S("d2", 0, 128, 64), S("ix", 1, 128, 64), S("ix", 0, 128, 64), ALU.subtract)
-        tt(S("d2", 62, 128, 64), S("ix", 61, 128, 64), S("d2b", 62, 128, 64), ALU.add)
-        tt(S("d2", 63, 128, 64), S("ix", 62, 128, 64), S("ix", 63, 128, 64), ALU.add)
-        act(S("d2", 128, 256), S("d2", 0, 128), ID, 0.0, -2.0)
+    def late_constants():
+        ms(S("gu", 4096, WW), 0.0)
+        ms(S("zr"), 0.0)
+        mm(S("p5", 0, 128), I1, S("zr", 0, 128), True, False)
+        ms(S("fl"), 0.0)
+        ms(S("cs"), 0.0)
+        ms(S("ci"), 0.0)
+        ms(S("ci", 128, 256), -128.0)
+        ms(S("co"), 0.0)
+        ms(R("co", 0, 8, 0, 1), 8192.0)
+        ms(S("msk"), 1.0)
+        ms(S("msk", 0, 1024, 16), 0.0)
+        ms(S("fw"), 0.0)
+        for c, v in ((0, 1.0), (1, -256.0), (17, 1.0), (33, 1.0), (48, 1.0), (65, 1.0), (81, 1.0)):
+            ts(S("fw", c, c + 15, 2), S("idb", 0, 128, 16), v, None, ALU.mult)
+        cp(S("rl", 128, 160, 16), S("idb", 63, 128, 64))
+        act(S("bl2", 0, 128), S("blk"), ID, 0.0, 256.0)
+        act(S("bl2", 128, 256), S("blk"), ID, 0.0, -1.0 / 32)
         tt(S("d2a"), S("ix", 0, 128), S("ix", 2, 130), ALU.add)
         tt(S("d2", 256, 384), S("d2a"), S("d2b", 1, 129), ALU.add)
         tt(S("d2", 318, 384, 64), S("ix", 62, 128, 64), S("d2b", 63, 128, 64), ALU.add)
         cp(S("d2", 319, 384, 64), S("ix", 63, 128, 64))
         act(S("d2", 384, 512), S("d2", 256, 384), ID, 0.0, -2.0)
+        act(S("d2", 0, 128), S("d2", 256, 384), ID, 0.0, -1.0)
+        tt(S("d2", 0, 128, 64), S("ix", 1, 128, 64), S("ix", 2, 128, 64), ALU.subtract)
+        tt(S("d2", 63, 128, 64), S("d2", 63, 128, 64), S("ix", 0, 128, 64), ALU.subtract)
+        act(S("d2", 128, 256), S("d2", 0, 128), ID, 0.0, -2.0)
 
-    def y_diff(t, j, src, bank):
-        o = S(bank)
-        c = 128 * (t % 2)
-        sel = S("selb", 512 * j, 512 * j + 512)
-        return [(o, S("dhi", c, c + 128), sel, True, False), (o, S("dlo", c, c + 128), sel, False, False),
-                (o, IM32, S(src, 512 * j, 512 * j + 512), False, True)]
+    def d_mm(t, j, bank):
+        z = 256 * (t % 2) + 128 * (j // 2 % 2)
+        mm(S(bank), S("zp", z, z + 128), S("selk", 512 * (j % 2), 512 * (j % 2) + 512), True, False)
 
-    def y_exp(bank, out):
-        act(S(bank), S(bank), AF.Abs)
-        act(out, S(bank), AF.Exp, 0.0, -1.0 / 256)
+    def y_chunk(t, j, bank, out=None):
+        filler(d_mm)(t, j, bank)
+        mm(S(bank), IMK if t == NV - 1 else IPK, S("phi%d" % (t % 2), 512 * j, 512 * j + 512), False, True)
+        act(S(bank), S(bank), AF.Abs, 0.0 if t == NV - 1 else -8192 * KAP)
+        act(out or S("exv", 512 * j, 512 * j + 512), S(bank), AF.Exp, 0.0, -1.0 / (256 * KAP))
 
-    def y_chunk(t, j, bank):
-        for c in y_diff(t, j, "phi%d" % (t % 2), bank):
-            mm(*c)
-        y_exp(bank, S("exv", 512 * j, 512 * j + 512))
-
-    def y_gain(t, j, n=2):
-        for c in range(512 * j, 512 * (j + n), PIECE):
+    def y_gain(t, j):
+        for c in range(512 * j, 512 * j + 512, PIECE):
             po = 128 * (t % 2) + c // 16
-            tt(S("zz", c, c + PIECE), gat(S("gw", 0, 4104), S("poff", po, po + PIECE // 16)), S("exv", c, c + PIECE), ALU.mult)
+            tt(S("zz", c, c + PIECE), gat(S("gw", WW * t, WW * t + 4104), S("pofy", po, po + PIECE // 16)),
+               S("exv", c, c + PIECE), ALU.mult)
 
-    def y_sum(t, h, o, z="zz", first=True):
+    def y_sum(t, h, z="zz", stop=False):
         l = S("ix", 16 * t * h, 16 * t * h + 128)
-        return [(o, l, S(z, 1024 * h + k, 1024 * h + 1024, 16), k == 0 and first, k == 15) for k in range(16)]
+        for k in range(16):
+            mm(S("p5", 64 * h, 64 * h + 64), l, S(z, 1024 * h + k, 1024 * h + 1024, 16), False, k == 15 and stop)
 
-    def y_keep(t, h, o):
-        act(S("sy", 128 * t + 64 * h, 128 * t + 64 * h + 64), o, ID)
-        if h == 1 and t > 0:
-            dst = cores[(rank - t) % 4]
-            send([(S("sy", 128 * t, 128 * t + 128), S("ly", 128 * t, 128 * t + 128), dst, engs(dst, 0, 2)[0], "arrY%d" % t)])
+    def y_scan():
+        scan(S("sc"), S("msk"), S("zz", 0, 1024), ALU.mult)
+        mm(S("p5", 0, 64), I32F, S("sc", 15, 1024, 16), False, False)
 
-    nxt = cores[(rank + 1) % 4]
-    n4 = engs(nxt, 0, 1)[1]
-    VW = S("vw", 0, 4104)
+    y_gain, y_sum, y_scan = filler(y_gain), filler(y_sum), filler(y_scan)
     for t in range(NV):
         last = t == NV - 1
+        seen.clear()
         phi = "phi%d" % (t % 2)
-        off, mp = 256 * t, S("lmp", 128 * t, 128 * t + 128)
-        m2, dd = S("lm2", 256 * t, 256 * t + 128), S("ld", 128 * t, 128 * t + 128)
+        w0, zo = WW * t, 256 * (t % 2)
+        win = S("vw", w0, w0 + 4104)
         if t > 0:
-            arrive("arrB%d" % t, 2 * n4, [S("loff", off, off + 256), mp])
-            arrive("arrA%d" % t, 2 * n4, [S("lm2", 256 * t, 256 * t + 256), dd])
-        win, hh = (S("xb", 0, 4104), 0.0) if t == 0 else (VW, -H)
-        for h in range(2):
-            ts(S("xg", 1024 * h, 1024 * h + 1024), gat(win, S("loff", off + 64 * h, off + 64 * h + 64)), hh, None, ALU.add)
-            act(S("xg", 2048 + 1024 * h, 3072 + 1024 * h), gat(win, S("loff", off + 128 + 64 * h, off + 192 + 64 * h)), ID, hh)
-        if t > 1:
-            y_keep(t - 2, 0, S("p6", 256, 320))
-        bank = {0: "p0", 4: "p1", 1: "p2", 5: "p3", 2: "p4", 6: "p5", 7: "p1", 3: "p0"}
-
-        def e_mm(j, part=3):
-            if part & 1:
-                mm(S(bank[j]), m2, S("sel16", 512 * (j % 4), 512 * (j % 4) + 512), True, False)
-            if part & 2:
-                mm(S(bank[j]), IM3, S("xg", 512 * j, 512 * j + 512), False, True)
-
-        def direct(j):
-            b = 1.5 * 2.0 ** 28
-            ts(S("ind", 512 * j, 512 * j + 512), S(bank[j]), b, b, ALU.add, ALU.is_equal)
-
-        def absd(j):
-            act(S("ab", 512 * j, 512 * j + 512), S(bank[j]), AF.Abs)
-
-        def below(j):
-            ts(S("ind", 512 * j, 512 * j + 512), S("ab", 512 * j, 512 * j + 512), 16.0, None, ALU.is_lt)
-        for j in (0, 4, 1, 5):
-            e_mm(j, 1)
-        for j in (0, 4, 1, 5):
-            e_mm(j, 2)
-        for j in (2, 6):
-            e_mm(j, 1)
-        for j in (6, 2):
-            e_mm(j, 2)
-        direct(0); absd(4); e_mm(7); e_mm(3)
-        direct(1); absd(5); below(4); absd(6); direct(2); below(5); absd(7); below(6); absd(3); below(7)
-        for k in range(16):
-            mm(S("p7", 8 * k, 8 * k + 8, p1=96), S("ind", k, 1536, 16), S("bo"))
-        for k in range(16):
-            mm(S("p6", 128 + 8 * k, 136 + 8 * k), S("ind", 2048 + k, 4096, 16), S("bo"))
-        below(3)
-        for k in range(16):
-            mm(S("p7", 8 * k, 8 * k + 8, p0=96), S("ind", 1536 + k, 2048, 16), S("bo"))
+            arrive("arrW%d" % t, len(engines), [S("vw", w0, w0 + 2048)])
+            arrive("arrX%d" % t, len(engines), [S("vw", w0 + 2048, w0 + WW)])
+        if 0 < t < 4:
+            arrive("arrG%d" % t, len(engines), [S("gw", w0, w0 + WW)])
         if t == 0:
-            for j in range(4):
-                act(S("xh", 512 * j, 512 * j + 512), S("xb", 1024 * j, 1024 * j + 512), ID, H)
-        if last:
-            y_chunk(t - 1, 2, "p0")
-            for c in y_diff(t - 1, 3, "phi%d" % ((t - 1) % 2), "p1"):
-                mm(*c)
-        elif t > 1:
-            for c in y_sum(t - 2, 1, S("p2", 0, 64))[:12]:
-                mm(*c)
-        c0 = S("p7", 0, 128)
-        ts(S("e12"), S("p6", 128, 256), 12.0, 12.0, ALU.is_ge, ALU.mult)
-        tt(S("late"), c0, S("e12"), ALU.is_lt)
-        act(S("r01", 128, 256), S("p6", 128, 256), AF.Relu, -704.0, 64.0)
-        act(S("r01", 0, 128), c0, AF.Relu, -704.0, 64.0)
-        mm(S("p6", 384, 512), I1, S("r01", 128, 256), True, False)
-        mm(S("p6", 384, 512), I1, S("r01", 0, 128), False, True)
-        tt(S("pint"), S("late"), mp, ALU.add)
-        ts(S("loi"), S("pint"), 63, None, ALU.bitwise_and)
-        ts(S("hii"), S("pint"), 6, 63, ALU.arith_shift_right, ALU.bitwise_and)
-        ts(S("lo1"), S("loi"), 1.0, None, ALU.add)
-        ts(S("av"), S("hii"), -63.0, None, ALU.add)
-        tt(S("bv"), S("p6", 384, 512), S("lo1"), ALU.min)
-        act(S("hb"), S("bv"), AF.Sign)
-        mm(S("p7", 128, 256), S("av"), I64, True, False)
-        mm(S("p7", 128, 256), S("bv"), I1, False, False)
-        mm(S("p7", 128, 256), S("hb"), IM8K, False, True)
-        po = 128 * (t % 2)
-        dh = 128 * (t % 2)
-        nv = 128 if last else 96
+            filler(ms)(S("gw", 4096, WW), 0.0)
+            filler(cp)(S("gw", 4096, 4098), S("gw", 0, 2))
+        if t < 3:
+            send([(S("gw", w0, w0 + WW), S("gw", w0 + WW, w0 + 2 * WW), prev, mask, "arrG%d" % (t + 1))], [win])
 
-        def slot_done(s, pb, ramp):
-            c = 264 if ramp else 66 * s
-            if ramp:
-                act(S("cs", c, c + 64), S(pb, 0, 64), ID)
+        def xgat(c0, c1):
+            return S("xg", c0, c1), gat(win, S("off", c0 // 16, c1 // 16))
+        for c0, c1 in ((2048, 2560), (2560, 2560 + VG))[:1 + (VG > 0)]:
+            cp(*xgat(c0, c1))
+        for i, (c0, c1) in enumerate(((3072, 3584),) + ((2560 + VG, 3072),) * (VG < 512) + (
+                (3584, 4096), (0, 512), (512, 1024), (1024, 1536), (1536, 1792), (1792, 2048))):
+            act(*xgat(c0, c1), ID)
+            if i < 2:
+                digits(i)
+        bank = {4: "p3", 6: "p0", 5: "p1", 7: "p2", 0: PF, 1: "p3", 2: "p0"}
+        b = 1.5 * 2.0 ** 32
+        for j in (4, 6, 5, 7, 0, 1, 2, 3):
+            if j != 3:
+                d_mm(t, j, bank[j])
+                mm(S(bank[j]), IMK, S("xg", 512 * j, 512 * j + 512), False, True)
+                ts(S("ind", 512 * j, 512 * j + 512), S(bank[j]), b, b, ALU.add, ALU.is_equal)
             else:
-                act(S("cs", c + 1, c + 66), S(pb, 0, 65), ID)
+                for h, pb in ((0, "p1"), (1, "p2")):
+                    c = 1536 + 256 * h
+                    mm(S(pb, 0, 256), S("zp", zo + 128, zo + 256), S("selk", 512 + 256 * h, 768 + 256 * h), True, False)
+                    mm(S(pb, 0, 256), IMK, S("xg", c, c + 256), False, True)
+                    ts(S("ind", c, c + 256), S(pb, 0, 256), b, b, ALU.add, ALU.is_equal)
+            if j == 0:
+                for k in range(16):
+                    mm(R(PT, 0, 8, k, k + 1), S("ind", 2048 + k, 4096, 16), S("bo"))
+                mm(S("p4", 128, 256), I1, S("r0m"), True, False)
+                mm(S("p4", 128, 256), I1, S("cr"), False, True)
+                mm(S("p4", 0, 128), I1, S("ca"), True, False)
+            if j == 1:
+                tt(S("t2a"), R(PT, 0, 8, 0, 16), S("r0m"), ALU.min)
+                act(S("t2"), S("t2a"), AF.Relu, -1408.0)
+        for p0, p1 in ((0, 64), (64, 96), (96, 128)):
+            for k in range(15):
+                mm(S("p4", k, 128, 16, p0, p1), S("ind", 16 * p0 + k, 16 * p1, 16), S("bo"), False, False)
+        mm(S("p4", 15, 128, 16), S("ind", 15, 2048, 16), S("bo"), False, True)
+        tt(S("uu"), S("p4", 0, 128), S("t2"), ALU.max)
+        tt(S("bv"), S("p4", 128, 256), S("uu"), ALU.min)
+        act(S("non"), S("p4", 0, 128), AF.Sign, 0.5, -1.0)
+        if t == 0:
+            filler(late_constants)()
+        nv = 128 if last else 96
+        for m in range(nv, 128):
+            filler(act)(S("oh", TW * m, TW * m + 64), S("tb2", 0, 64), AF.Relu, S("av", m, m + 1), -1.0)
+        act(S("nn"), S("bv"), AF.Relu, 8192.0, -8192.0)
+        side(True)
+        mm(S("p4", 384, 512), ta, S("id16"), True, False)
+        mm(S("p4", 384, 512), S("non"), IHALF, False, False)
+        mm(S("p4", 384, 512), S("nn"), I1, False, True)
+        ts(S("poff"), S("p4", 384, 512), 2048.5, float(DUMMY), ALU.add, ALU.min)
+        mm(S("p4", 256, 512), I1, S("zr"), True, False)
+        side(False)
 
-        def slot_diff(s, ramp):
-            c = 264 if ramp else 66 * s
-            d = 256 if ramp else 0
-            o = S("p6", 64 * s, 64 * s + 64)
-            mm(o, S("d2", d, d + 128), S("cs", c, c + 64), True, False)
-            mm(o, S("d2", d, d + 128), S("cs", c + 2, c + 66), False, False)
-            mm(o, S("d2", d + 128, d + 256), S("cs", c + 1, c + 65), False, True)
-
-        def slot_once(s, ramp):
-            ts(S("ub", 64 * s, 64 * s + 64), S("p6", 64 * s, 64 * s + 64), 1.0 if ramp else -1.0, -H, ALU.is_equal, ALU.mult)
+        def slot(s, pb, ramp, end=False):
+            c, d = (4 * CS, 256) if ramp else (CS * s, 0)
+            if ramp:
+                act(S("cs", c + 2, c + 67), S(pb, 0, 65), ID)
+            else:
+                act(S("cs", c, c + 66), S(pb, 0, 66), ID)
+            o = S("p3", 66 * s, 66 * s + 65)
+            mm(o, S("d2", d, d + 128), S("cs", c, c + 65), True, False)
+            mm(o, S("d2", d, d + 128), S("cs", c + 2, c + 67), False, False)
+            mm(o, S("d2", d + 128, d + 256), S("cs", c + 1, c + 66), False, True)
+            if end:
+                cp(S("cb", 66 * s, 66 * s + 65), o)
+            else:
+                act(S("cb", 66 * s, 66 * s + 65), o, ID)
+            for q in range(4):
+                w = 64 if q == 3 else 65
+                mm(S("p4", 256 + 64 * q, 256 + 64 * q + w, 1, 32 * s, 32 * s + 32), S("rl", 32 * q, 32 * q + 32),
+                   S("cb", 66 * s, 66 * s + w), False, False)
+            mm(S("p4", 256, 257, 1, 32 * s, 32 * s + 32), S("rl", 128, 160), S("cb", 66 * s + 64, 66 * s + 65), False, False)
+            if end:
+                mm(S("p4", 256, 257), I1, S("zr", 0, 1), False, True)
         pend = []
-        side = y_sum(t - 2, 1, S("p2", 0, 64))[0 if last else 12:] if t > 1 else []
-        na = [96]
+        na = [nv]
         for n in range(nv):
             g, k = n // 16, n % 16
-            col = 8 * k + g
-            ts(S("oh", 128 * n, 128 * n + 128), S("tab"), S("av", col, col + 1), S("bv", col, col + 1), ALU.max, ALU.min)
-            o = S("p%d" % (4 + (g // 2) % 2), 0, 65, 1, 64 * (g % 2), 64 * (g % 2) + 64)
-            pend.append((o, S("oh", 128 * n, 128 * n + 64), S("oh", 128 * n + 63, 128 * n + 128), k == 0, k == 15))
+            c = TW * n
+            ts(S("oh", c, c + 129), S("tab", 0, 129), S("av", n, n + 1), S("bv", n, n + 1), ALU.max, ALU.min)
+            o = S("p%d" % (g // 2 % 2), 0, 66, 1, 64 * (g % 2), 64 * (g % 2) + 64)
+            pend.append((o, S("oh", c + 65, c + 129), S("oh", c, c + 66), k == 0, k == 15))
             if n % 4 == 3 or n >= nv - 4:
-                for c in pend:
-                    mm(*c, also=S("oh", 128 * n, 128 * n + 128))
+                for x in pend:
+                    mm(*x, also=S("oh", c, c + 129))
                 pend = []
-                for c in side[:2]:
-                    mm(*c)
-                side = side[2:]
-            if not last and n % 6 == 5:
+            if not last and n % 4 == 3 and na[0] < 128:
                 for m in (na[0], na[0] + 1):
-                    ga, ka = m // 16, m % 16
-                    ca = 8 * ka + ga
-                    act(S("oh", 128 * m, 128 * m + 64), S("tb2", 0, 64), AF.Relu, S("av", ca, ca + 1), -1.0)
-                    act(S("oh", 128 * m + 64, 128 * m + 128), S("tb2", 64, 128), AF.Relu, S("bv", ca, ca + 1), -1.0)
+                    act(S("oh", TW * m + 64, TW * m + 129), S("tb2", 64, 129), AF.Relu, S("bv", m, m + 1), -1.0)
                 for m in (na[0], na[0] + 1):
-                    ga, ka = m // 16, m % 16
-                    mm(S("p3", 0, 64, 1, 64 * (ga % 2), 64 * (ga % 2) + 64), S("oh", 128 * m, 128 * m + 64),
-                       S("oh", 128 * m + 64, 128 * m + 128), ka == 0, ka == 15,
-                       also=S("oh", 128 * na[0] + 192, 128 * na[0] + 256))
+                    mm(S("p2", 0, 65, 1, 64 * (m // 16 % 2), 64 * (m // 16 % 2) + 64), S("oh", TW * m, TW * m + 64),
+                       S("oh", TW * m + 64, TW * m + 129), m % 16 == 0, m % 16 == 15,
+                       also=S("oh", TW * na[0] + TW + 64, TW * na[0] + TW + 129))
                 na[0] += 2
-            if last and n == 35:
-                y_keep(t - 2, 1, S("p2", 0, 64))
-            if n == (0 if last else 5):
-                act(S("ptr"), S("p7", 128, 256), ID)
-                mm(S("p7", 0, 128), S("pm32", 16, 144), S("ptr"))
-                if last:
-                    y_exp("p1", S("exv", 1536, 2048))
-            if n == 11 and t > 1 and not last:
-                y_keep(t - 2, 1, S("p2", 0, 64))
-            if n == (15 if last else 27):
-                ts(S("poff", po, po + 128), S("p7", 0, 128), 12223.0, float(DUMMY), ALU.add, ALU.min)
-                if last:
-                    act(S("dhi", dh, dh + 128), dd, ID)
-                    tt(S("dlo", dh, dh + 128), dd, S("dhi", dh, dh + 128), ALU.subtract)
-                    for h in range(2):
-                        act(S(phi, 1024 * h, 1024 * h + 1024), gat(VW, S("poff", po + 64 * h, po + 64 * h + 64)), ID, -H)
-            if n == 19 and t == 0:
-                d2_constants()
-            if n == 35 and last:
-                y_gain(t - 1, 0)
-                scan(S("sc"), S("msk"), S("zz", 0, 1024), ALU.mult)
-                y_keep(t - 1, 0, S("sc", 15, 1024, 16))
-            if last and n in (51, 71, 87, 103):
-                j = (51, 71, 87, 103).index(n)
-                pb = ("p2", "p3", "p0", "p1")[j]
-                for c in y_diff(t, j, phi, pb):
-                    mm(*c)
-                y_exp(pb, S(pb) if j < 2 else S("exw", 512 * (j - 2), 512 * (j - 1)))
-            if not last and n in (43, 55, 75):
-                j = (43, 55, 75).index(n)
-                mm(S("p%d" % j), I1, S("xb", 1024 * j + 512, 1024 * j + 1024), True, False)
-            if n % 32 == 5 and n > 32:
-                slot_done(n // 32 - 1, "p%d" % (4 + (n // 32 - 1) % 2), False)
-            if n % 32 == 15 and n > 32:
-                slot_diff(n // 32 - 1, False)
+            if last and n in YL:
+                j = (2, 3, 0, 1)[YL.index(n)]
+                pb = ("p2", PT, PF, PF)[j]
+                act(S(phi, 512 * j, 512 * j + 512), gat(win, S("poff", 32 * j, 32 * j + 32)), ID)
+                y_chunk(t, j, pb, S(pb) if j < 2 else S("exw", 512 * (j - 2), 512 * (j - 1)))
+            if n % 32 == 1 and n > 32:
+                slot(n // 32 - 1, "p%d" % ((n // 32 - 1) % 2), False)
+            if n == NA and not last:
+                slot(3, "p2", True)
+            if n == (NA if not last else 3) and t > 0:
+                y_chunk(t - 1, 3, PT)
+                y_gain(t - 1, 3)
         s_last = nv // 32 - 1
-        slot_done(s_last, "p%d" % (4 + s_last % 2), False)
-        ts(S("ub", 0, 64 * s_last), S("p6", 0, 64 * s_last), -1.0, -H, ALU.is_equal, ALU.mult)
-        if not last:
-            slot_done(3, "p3", True)
-            slot_diff(3, True)
-            slot_once(3, True)
-        slot_diff(s_last, False)
-        if not last:
-            act(S("lt1"), S("late"), ID, 0.0, 1000.0)
-            act(S("dsc"), dd, ID, 0.0, 2.0 ** -21)
-            act(S("dhi", dh, dh + 128), dd, ID)
-            if t == 1:
-                arrive("arrS", 4 * n4, [S("lst", 8, 32)])
-            so = 8 * t
-            act(S("dl", 0, 8), S("lmp", 128 * t, 128 * t + 8), ID, 6144.0)
-            tt(S("dl", 8, 128), S("lmp", 128 * t + 8, 128 * t + 128), S("lmp", 128 * t, 128 * t + 120), ALU.subtract)
-            act(S("dl", 136, 256), S("dl", 8, 128), ID)
-            if t == 0:
-                tt(S("dl", 128, 136), S("lmp", 0, 8), S("lst", 0, 8), ALU.subtract)
-            else:
-                tt(S("dl", 128, 136, p1=64), S("lmp", 128 * t, 128 * t + 8, p1=64), S("lst", so, so + 8, p1=64), ALU.subtract)
-                tt(S("dl", 128 + t, 136, p0=64), S("lmp", 128 * t + t, 128 * t + 8, p0=64),
-                   S("lst", so, so + 8 - t, p0=64), ALU.subtract)
-                tt(S("dl", 128, 128 + t, p0=64), S("lmp", 128 * t, 128 * t + t, p0=64),
-                   S("lst", so + 8 - t, so + 8, p0=64), ALU.subtract)
-        if t > 0:
-            y_gain(t - 1, 2 if last else 0, 1)
-        slot_once(s_last, False)
-        for bq in ((0, 1, 2, 3) if last else (0, 1, 3, 2)):
-            for q in range(4):
-                mm(S("p7", 64 * q, 64 * q + 64, 1, 32 * bq, 32 * bq + 32), S("rl", 32 * q, 32 * q + 32),
-                   S("ub", 64 * bq, 64 * bq + 64))
-        if not last:
-            mm(S("p3"), I1, S("xb", 3584, 4096), True, False)
-        if t > 0:
-            y_gain(t - 1, 3 if last else 1, 1)
-        tt(S("ucum"), S("p7", 0, 256), S("ucum"), ALU.min)
+        slot(s_last, "p%d" % (s_last % 2), False, True)
+        ts(S("ub"), S("p4", 256, 512), 1.0, -256.0, ALU.is_equal, ALU.mult)
         for j in range(8):
-            pb = "p%d" % (((j // 2) % 2 if last else j // 2) if j % 2 else 4 + (j // 2) % 2)
-            if j % 2 and last:
-                mm(S(pb), IM8K if last else I1, S("gw" if last else "xb", 512 * j, 512 * j + 512), True, False)
+            if last:
+                pb = ("p3", "p0", "p4", PF, "p3", "p1", "p4", "p0")[j]
+            else:
+                pb = (PF, "p1", PT, "p2", PF, "p0", PT, "p3")[j]
+            c = 512 * j
+            col = S("vw", w0 + c, w0 + c + 512)
+            ona = j % 2 or (j == 6 and VU == 3 and not last)
+            if ona:
+                filler(mm)(S(pb), IM32 if last else I1, S("gw", c, c + 512) if last else col, True, False)
             for i in range(2):
                 hx = 2 * j + i
-                mm(S(pb, 256 * i, 256 * i + 256), S("ex", 128 * hx, 128 * hx + 128), S("ucum"),
-                   j % 2 == 0, j % 2 == 0 or i == 1)
-            c = 512 * j
+                mm(S(pb, 256 * i, 256 * i + 256), S("ex", 128 * hx, 128 * hx + 128), S("ub"), not ona, not ona or i == 1)
             if last:
                 if j % 2:
-                    act(S("gu", c, c + 512), S(pb), AF.Relu, -8.0, -1.0 / 8192)
+                    act(S("gu", c, c + 512), S(pb), AF.Relu, -8.0, -1.0 / 32)
                 else:
                     tt(S("gu", c, c + 512), S(pb), S("gneg", c // 2, c // 2 + 512), ALU.mult)
-            elif j % 2:
-                act(S("vw", c, c + 512), S(pb), ID, H)
+                    if j == 2:
+                        cp(S("gu", 4096, 4098), S("gu", 0, 2))
+                continue
+            if ona:
+                act(col, S(pb), ID)
             else:
-                tt(S("vw", c, c + 512), S(pb), S("xh", c // 2, c // 2 + 512), ALU.add)
-                if j == 2:
-                    cp(S("vw", 4096, 4098), S("vw", 0, 2))
+                tt(col, S(pb), col, ALU.add)
+            if j == 1:
+                act(S("vw", w0 + 4096, w0 + 4098), S("vw", w0, w0 + 2), ID)
+            if j == 3:
+                send([(S("vw", w0, w0 + 2048), S("vw", w0 + WW, w0 + WW + 2048), prev, mask, "arrW%d" % (t + 1))])
+            if j == 7:
+                send([(S("vw", w0 + 2048, w0 + WW), S("vw", w0 + WW + 2048, w0 + 2 * WW), prev, mask, "arrX%d" % (t + 1))])
+        if t > 0:
+            if t in SCAN:
+                y_scan()
+            else:
+                y_sum(t - 1, 0)
+            y_sum(t - 1, 1)
         if last:
-            for c in y_sum(t - 1, 1, S("p6", 384, 448)):
-                mm(*c)
             GU = S("gu", 0, 4104)
-            act(S("xg", 0, 1024), gat(GU, S("poff", po, po + 64)), ID)
-            y_keep(t - 1, 1, S("p6", 384, 448))
-            tt(S("zw", 1024, 2048), gat(GU, S("poff", po + 64, po + 128)), S("exw"), ALU.mult)
-            for j in range(2):
-                tt(S("zw", 512 * j, 512 * j + 512), S("p%d" % (2 + j)), S("xg", 512 * j, 512 * j + 512), ALU.mult)
+            act(S("xg", 0, 1024), gat(GU, S("poff", 0, 64)), ID)
+            tt(S("zw", 1024, 2048), gat(GU, S("poff", 64, 128)), S("exw"), ALU.mult)
+            for j, pb in enumerate(("p2", PT)):
+                tt(S("zw", 512 * j, 512 * j + 512), S(pb), S("xg", 512 * j, 512 * j + 512), ALU.mult)
             scan(S("sc"), S("msk"), S("zw", 0, 1024), ALU.mult)
-            for c in y_sum(t, 1, S("p4", 0, 64), "zw"):
-                mm(c[0], c[1], c[2], c[3], False)
-            for j in (1, 2, 3):
-                arrive("arrY%d" % j, 2 * n4, [S("ly", 128 * j, 128 * j + 128)])
-            for h in (1, 0):
-                pre = [S("sy", 64 * h, 64 * h + 64)] + [S("ly", 128 * j + 64 * h, 128 * j + 64 * h + 64) for j in (1, 2, 3)]
-                for i, r in enumerate(pre):
-                    mm(S("p4" if h else "p5", 0, 64), I32F, r, i == 0 and h == 0, i == 3)
-            act(S("yo", 64, 128), S("p4", 0, 64), ID)
+            y_sum(t, 1, "zw", True)
+            cp(S("yo", 64, 128), S("p5", 64, 128))
             tt(S("yo", 0, 64), S("p5", 0, 64), S("sc", 15, 1024, 16), ALU.add)
-            put("A", "dma", (("y",), S("yo"), "o0"), [S("yo")], [])
+            put("S", "dma", (("y",), S("yo"), "o0"), [S("yo")], [])
             break
-        cp(S(phi, 0, 1024), gat(VW, S("poff", po, po + 64)))
-        act(S(phi, 1024, 2048), gat(VW, S("poff", po + 64, po + 128)), ID)
-        if t > 0:
-            for j in (2, 3):
-                for c in y_diff(t - 1, j, "phi%d" % ((t - 1) % 2), "p%d" % j):
-                    mm(*c)
-            y_exp("p2", S("exv", 1024, 1536))
-        for k in range(16):
-            mm(S("p6", 8 * k, 8 * k + 8), S(phi, k, 2048, 16), S("idb", 0, 128, 16))
-        for k in range(8):
-            mm(S("p7", 0, 128), S(phi, k, 2048, 16), I2, k == 0, False)
-        f0 = S("p6", 0, 128)
-        ts(S("nt"), f0, 1000.0, 2.0, ALU.max, ALU.mult)
-        tt(S("tl"), f0, S("lt1"), ALU.is_lt)
-        tt(S("lv", 8, 128), S("p6", 0, 120), S("nt", 8, 128), ALU.is_gt)
+        ts(S(phi, 0, VP), gat(win, S("poff", 0, VP // 16)), -1.0, 0.0, ALU.mult, ALU.max)
+        act(S(phi, VP, 2048), gat(win, S("poff", VP // 16, 128)), AF.Relu, 0.0, -1.0)
+        side(True)
+        mm(S(PF, 0, 384), I1, S("ci"), True, False)
+        mm(S(PF, 128, 256), I128, S("non"), False, False)
+        mm(R(PT, 0, 8, 0, 32), I1, S("co"), True, False)
         for h in range(2):
-            o = S("p5", 128 * h, 128 * h + 128)
-            mm(o, I1, S("tl"), True, False)
-            mm(o, IMG, S("lv", 8, 136), False, False)
-            mm(o, IGK, S("lv", 0, 128), False, True)
-        for k in range(8, 16):
-            mm(S("p7", 0, 128), S(phi, k, 2048, 16), I2, False, k == 15)
-        tt(S("dlo", dh, dh + 128), dd, S("dhi", dh, dh + 128), ALU.subtract)
-        b = 1.5 * 2.0 ** 40
-        act(S("a2", 128, 256), S("p7", 0, 128), ID, b)
-        act(S("a2", 0, 128), S("a2", 128, 256), ID, -b)
-        if t > 0:
-            y_exp("p3", S("exv", 1536, 2048))
+            mm(R(PT, 0, 8, 16 * h, 16 * h + 16), I1, ta, False, False)
+            mm(R(PT, 0, 8, 16 * h + 1, 16 * h + 16), IM1, R("ta", 0, 8, 0, 15), False, False)
+            s0 = (8 - t) * h
+            mm(R(PT, 0, 8, 16, 17, 64 * h, 64 * h + 64), S("idb", 768 + 64 * h, 832 + 64 * h), S("st", s0, s0 + 8), False, False)
+        for h in range(2):
+            mm(S("p4", 0, 128, 1, 64 * h, 64 * h + 64), S("jj"), S("zp", zo + 128 * h, zo + 128 * h + 128))
+        side(False)
+        mm(R(PF, 0, 24, 0, 1), S(phi, 0, 2048, 16), S("fw", 1, 48, 2), False, False)
+        for k in range(1, 16):
+            w = 48 * (k == 15)
+            mm(R(PF, 0, 24, k - 1, k + 1), S(phi, k, 2048, 16), S("fw", w, w + 48), False, k == 15)
+        ts(R("fl", 0, 16, 1, 17), S(PF, 0, 256), 0.5, None, ALU.is_gt)
+        act(S("sa"), S(PF, 256, 384), AF.Sign, -0.5)
+        y_chunk(t, 0, "p0")
+        for h in range(2):
+            o = R(PT, 0, 8, 16 * h, 16 * h + 16)
+            mm(o, I1, R("fl", 8, 16, 1, 17), False, False)
+            mm(o, IMG, R("fl", 0, 8, 1, 17), False, False)
+            mm(o, IGK, R("fl", 0, 8, 0, 16), False, h == 1)
         for g in range(8):
-            scan(S("wt", g, 256, 8), S("p5", g, 256, 8), S("dl", g, 256, 8), ALU.add)
-        sd = 128 * t
-
-        def turn():
-            tt(S("dn"), S("fi"), S("x2"), ALU.add)
-            act(S("sd", sd, sd + 128, p1=64), S("dn", p1=64), ID)
-            act(S("sd", sd + 16, sd + 128, p0=64), S("dn", 0, 112, p0=64), ID)
-            act(S("sd", sd, sd + 16, p0=64), S("dn", 112, 128, p0=64), ID)
-            centre_parts(S("sd", sd, sd + 128))
-        dops = {
-            3: lambda: tt(S("tt"), S("a2", 0, 128), S("dsc"), ALU.mult),
-            5: lambda: tt(S("x2"), S("p7", 0, 128), S("a2", 0, 128), ALU.subtract),
-            6: lambda: ts(S("fi"), S("tt"), -0.46875, None, ALU.add),
-            8: turn,
-        }
+            scan(R("wt", g, g + 1, 0, 32), S("oneb", 0, 32), R(PT, g, g + 1, 0, 32), ALU.mult)
+        mm(S("p3", 0, 128), S("sa"), I1)
+        act(S("sb"), S("p3", 0, 128), ID)
+        for k in range(16):
+            mm(S("p4", 128, 256), S(phi, k, 2048, 16), IM2, k == 0, False)
+        mm(S("p4", 128, 256), S("sb"), S("bl2", 0, 128), False, True)
+        mm(S("p3", 256, 384), S("sb"), S("bl2", 128, 256))
+        act(S("mu"), S("p3", 256, 384), ID, 0.5)
+        y_chunk(t, 1, "p1")
+        side(True)
+        mm(S("p3", 128, 256), ta, S("id16"), True, False)
+        mm(S("p3", 128, 256), S("non"), IHALF, False, False)
+        mm(S("p3", 128, 256), S("sa"), IM4K, False, True)
+        ts(S("pofy", zo // 2, zo // 2 + 128), S("p3", 128, 256), 6144.5, float(DUMMY), ALU.add, ALU.min)
+        side(False)
         for s in range(17):
-            i0 = 8 * max(s - 1, 0)
-            q = S("qb", 128 * s + i0, 128 * s + 128)
-            ts(q, S("wt", i0 + 8 * s, 128 + 8 * s), KEY * s, KEY * (s + 1), ALU.max, ALU.min)
-            if s < 9:
-                mm(S("p4", i0, 128), I32F, q, s == 0, False)
-        for s in (10, 12, 14, 16):
-            i0 = 8 * (s - 1)
-            w = S("qb", 128 * (s - 1) + i0, 128 * s)
-            tt(w, w, S("qb", 128 * s + i0, 128 * s + 128), ALU.add)
-            mm(S("p4", i0 - 8, 128), I32F, S("qb", 128 * (s - 1) + i0 - 8, 128 * s), False, s == 16)
-        for s in dops:
-            dops[s]()
-        ye = y_diff(t, 0, phi, "p0")
-        times_tail(S("p4", 0, 128), t + 1, ye)
-        y_exp("p0", S("exv", 0, 512))
-        send([(S("soff", 256 * t, 256 * t + 256), S("loff", 256 * t + 256, 256 * t + 512), nxt, engs(nxt, 2, 3)[0], "arrB%d" % (t + 1)),
-              (S("smp", sd, sd + 128), S("lmp", sd + 128, sd + 256), nxt, engs(nxt, 3, 4)[0], "arrB%d" % (t + 1))])
-        centre(S("sm2", 256 * t, 256 * t + 128))
-        send([(S("sm2", 256 * t, 256 * t + 256), S("lm2", 256 * t + 256, 256 * t + 512), nxt, engs(nxt, 0, 1)[0], "arrA%d" % (t + 1)),
-              (S("sd", sd, sd + 128), S("ld", sd + 128, sd + 256), nxt, engs(nxt, 1, 2)[0], "arrA%d" % (t + 1))])
+            i0, i1, r = max(s - 1, 0), 15 if s == 15 else 16, 8 * min(s, 15)
+            ts(R("qb", r, r + 8, i0, i1), R("wt", 0, 8, i0 + s, i1 + s), KEY * s, KEY * (s + 1), ALU.max, ALU.min)
+            if s == DS:
+                tt(S("tt"), S("p4", 0, 128), S("mu"), ALU.mult)
+            if s == DS + 2:
+                ts(S("fi"), S("tt"), 4096 - 0.46875, None, ALU.add)
+            if s == DS + 4:
+                tt(S("p4", 128, 256), S("p4", 128, 256), S("fi"), ALU.add)
+            if s == DS + 6:
+                parts(t + 1, 0)
+            if s == 16:
+                parts(t + 1, 1)
+            if s == Y2:
+                y_chunk(t, 2, "p2")
+            if s < MERGE:
+                mm(R(PT, 8, 16, i0, 16), I32F, R("qb", r, r + 8, i0, 16), s == 0, False)
+            elif s % 2 == 0 and s < 15:
+                w = R("qb", 8 * s - 8, 8 * s, s - 1, 16)
+                tt(w, w, R("qb", 8 * s, 8 * s + 8, s - 1, 16), ALU.add)
+                mm(R(PT, 8, 16, s - 2, 16), I32F, R("qb", 8 * s - 8, 8 * s, s - 2, 16), False, False)
+        mm(R(PT, 8, 16, 14, 16), I32F, R("qb", 120, 128, 14, 16), False, True)
+        times_tail(t + 1)
+        for j in range(3):
+            y_gain(t, j)
         if t == 0:
             for j in range(4):
-                ts(S("gneg", 512 * j, 512 * j + 512), S("gw", 1024 * j, 1024 * j + 512), -1.0 / H, None, ALU.mult)
-        y_chunk(t, 1, "p1")
-        if t > 0:
-            for c in y_sum(t - 1, 0, S("p6", 256, 320)):
-                mm(*c)
-            y_gain(t - 1, 2)
+                filler(ts)(S("gneg", 512 * j, 512 * j + 512), S("gw", 1024 * j, 1024 * j + 512), -1.0 / 256, None, ALU.mult)
     return ops
 
 
@@ -613,23 +571,23 @@ def order(ops):
                 banks[name][1].append(i)
             h = hist.setdefault(name, [])
             if w:
-                h[:] = [e for e in h if not (acc[5] == 1 and acc[1] <= e[1][1] and e[1][2] <= acc[2]
-                                             and acc[3] <= e[1][3] and e[1][4] <= acc[4])]
+                h[:] = [e for e in h if not (acc[1] <= e[1][1] and e[1][2] <= acc[2] and (e[1][4] & ~acc[4]) == 0)]
             h.append((i, acc, w))
         d.discard(i)
         deps.append(d)
     return deps, after
 
 
-CYC, PCYC, GATHER, HOP, FLIGHT = 0.00104, 0.00052, 1.56, 0.11, 2.2
-PASSES, PIECE = 6, 256
+CYC, PCYC, GATHER, HOP = 0.00104, 0.00052, 1.56, 0.13
+FLIGHT = {"W": 4.0, "X": 4.0, "G": 8.0}
+PASSES, MOVES = 4, 150
 
 
 def _cost(op):
     q, kind, a = op[0], op[1], op[2]
 
     def n(x):
-        return 16 * n(x[2]) if x[0] == "*" else (x[4] - x[3] + x[5] - 1) // x[5]
+        return 16 * x[2][5] if x[0] == "*" else x[5]
 
     def two(*xs):
         return all(SCRATCH[x[0]][2] in (BF, F16, U16) for x in xs if isinstance(x, tuple))
@@ -660,16 +618,13 @@ def schedule(ops, deps, after):
             for tr in o[2][0]:
                 sender[tr[4]] = i
         if o[1] == "arr":
-            pred[i] = [(sender[o[2][0]], FLIGHT - 0.5 - HOP)]
+            pred[i] = [(sender[o[2][0]], FLIGHT[o[2][0][3]])]
     for i in range(n):
         pred[i] = [(j, (2.0 if ops[j][2][0][0] in ("ivi", "tai", "pfi") else 4.5) if ops[j][1] == "dma" else w) for j, w in pred[i]]
     succ = [[] for _ in range(n)]
     for i in range(n):
         for j, w in pred[i]:
             succ[j].append((i, w))
-    rank = [0.0] * n
-    for i in range(n - 1, -1, -1):
-        rank[i] = cost[i] + max([w + rank[k] for k, w in succ[i]] + [0.0])
 
     def lay(seq, before):
         start = [0.0] * n
@@ -692,27 +647,94 @@ def schedule(ops, deps, after):
             gl[lo:lo + 1] = [e for e in ([a, t], [t + c, b]) if e[1] - e[0] > 0.004]
             start[i] = t
         return start, max(start[i] + cost[i] for i in range(n))
+
+    def again(start):
+        back, _ = lay(sorted(range(n), key=lambda i: (-(start[i] + cost[i]), -i)), succ)
+        return sorted(range(n), key=lambda i: (-(back[i] + cost[i]), i))
+
+    def pulled(wanted):
+        out, done = [], [False] * n
+        for i in wanted:
+            stack = [i]
+            while stack:
+                j = stack[-1]
+                todo = [k for k, _ in pred[j] if not done[k]]
+                if todo:
+                    stack += sorted(todo, reverse=True)
+                    continue
+                stack.pop()
+                if not done[j]:
+                    done[j] = True
+                    out.append(j)
+        return out
+
     best = None
-    for seq in (list(range(n)), sorted(range(n), key=lambda i: (-rank[i], i))):
+    for seq in (pulled([j for j in range(n) if not ops[j][5]["late"]] + list(range(n))), list(range(n))):
         for _ in range(PASSES):
             start, span = lay(seq, pred)
             if best is None or span < best[0]:
                 best = (span, start)
-            back, _ = lay(sorted(range(n), key=lambda i: (-(start[i] + cost[i]), -i)), succ)
-            seq = sorted(range(n), key=lambda i: (-(back[i] + cost[i]), i))
-    return sorted(range(n), key=lambda i: (best[1][i], i))
+            seq = again(start)
+    twins = {}
+    for i, o in enumerate(ops):
+        twins.setdefault(o[5]["kind"], []).append(i)
+    span, start = best
+    tried = set()
+    for _ in range(MOVES):
+        ends = {}
+        for i in range(n):
+            ends[(ops[i][0], round(start[i] + cost[i] + 1e-6, 5))] = i
+        i = max(range(n), key=lambda k: start[k] + cost[k])
+        pairs = []
+        while start[i] > 1e-9:
+            ready, j = max([(start[k] + cost[k] + w, k) for k, w in pred[i]] + [(0.0, -1)])
+            if ready < start[i] - 1e-7:
+                j = ends.get((ops[i][0], round(start[i], 5)), j)
+                pairs.append((start[i] - ready, i, j))
+            if j < 0:
+                break
+            i = j
+        pairs = [p for p in pairs if (ops[p[1]][5]["kind"], ops[p[2]][5]["kind"]) not in tried
+                 and ops[p[1]][2][0][0] != ops[p[2]][2][0][0]]
+        if not pairs:
+            break
+        _, i, j = max(pairs)
+        tried.add((ops[i][5]["kind"], ops[j][5]["kind"]))
+        key = list(start)
+        for a in twins[ops[i][5]["kind"]]:
+            for b in twins[ops[j][5]["kind"]]:
+                if 0 < key[a] - key[b] < 8:
+                    key[a] = key[b] - 1e-5
+        s1, e1 = lay(pulled(sorted(range(n), key=lambda k: (key[k], k))), pred)
+        s2, e2 = lay(again(s1), pred)
+        if e1 < e2:
+            s2, e2 = s1, e1
+        if e2 < span - 1e-6:
+            span, start = e2, s2
+            tried = set()
+    return start
+
+
+ORDERED = {}
+
+
+def ordered(ops):
+    if not ORDERED:
+        deps, after = order(ops)
+        start = schedule(ops, deps, after)
+        seq = sorted(range(len(ops)), key=lambda i: (start[i], i))
+        place = {j: i for i, j in enumerate(seq)}
+        ORDERED["seq"] = seq
+        ORDERED["deps"] = [set(place[k] for k in deps[j]) for j in seq]
+        ORDERED["start"] = [start[j] for j in seq]
+    return [ops[j] for j in ORDERED["seq"]], ORDERED["deps"]
 
 
 def rank_program(g, core, T, topo):
     rank = T.rank_of(core)
     if rank is None:
         return
-    ops = plan(rank, list(T.cores), topo)
-    deps, after = order(ops)
-    seq = schedule(ops, deps, after)
-    place = {j: i for i, j in enumerate(seq)}
-    ops = [ops[j] for j in seq]
-    deps = [set(place[k] for k in deps[j]) for j in seq]
+    ops, deps = ordered(plan(rank, list(T.cores), topo))
     queue = {"P": g.tensor, "V": g.vector, "A": g.scalar, "G": g, "S": g.sync}
 
     def own(j):
@@ -756,9 +778,9 @@ def rank_program(g, core, T, topo):
             return T[x[0]][:]
         if len(x) == 3:
             return T[x[0]][:, x[1]:x[2]]
-        if x[5] == 1:
-            return T[x[0]][x[1]:x[2], x[3]:x[4]]
-        return T[x[0]][x[1]:x[2], x[3]:x[4]:x[5]]
+        if len(x[3]) == 2 and x[3][0][1] - x[3][0][0] == 1:
+            return T[x[0]][x[1]:x[2], x[3][0][0], x[3][1][0]:x[3][1][1]]
+        return T[x[0]][(slice(x[1], x[2]),) + tuple(slice(a, b) if s == 1 else slice(a, b, s) for a, b, s in x[3])]
 
     sent = 0
     waited = set()

@@ -19,28 +19,32 @@ SCRATCH = {
     "one32": ("sbuf", [128, 128], F32), "oneb": ("sbuf", [128, 512], BF), "zr": ("sbuf", [128, 256], BF),
     "ix": ("sbuf", [128, 256], F32), "trip": ("sbuf", [128, 128], F32), "tri0": ("sbuf", [128, 128], F32),
     "tsel": ("sbuf", [128, 128], F32), "blk": ("sbuf", [128, 128], F32), "bl2": ("sbuf", [128, 256], BF),
-    "idb": ("sbuf", [128, 12 * 128], BF), "id16": ("sbuf", [128, 128], F16),
+    "idb": ("sbuf", [128, 10 * 128], BF), "id16": ("sbuf", [128, 128], F16),
     "jj": ("sbuf", [128, 64], BF), "selk": ("sbuf", [128, 1024], BF),
-    "ex": ("sbuf", [128, 2048], BF), "rl": ("sbuf", [128, 160], BF), "msk": ("sbuf", [128, 1024], BF),
+    "ex": ("sbuf", [128, 2048], BF), "rl": ("sbuf", [128, 160], BF),
     "bo1": ("sbuf", [128, 8], BF), "bo0": ("sbuf", [128, 8], BF), "bo": ("sbuf", [128, 8], BF),
-    "fw": ("sbuf", [128, 96], BF), "ci": ("sbuf", [128, 384], BF), "co": ("sbuf", [128, 8, 32], BF),
+    "fw": ("sbuf", [128, 96], BF), "ci": ("sbuf", [128, 384], BF),
+    "wl": ("sbuf", [128, 8, 32], BF), "wv": ("sbuf", [128, 8, 32], BF), "wx": ("sbuf", [128, 8, 32], BF),
+    "ws": ("sbuf", [128, 16, 16], BF), "e15": ("sbuf", [128, 128], F32), "neg": ("sbuf", [128, 256], BF),
     "ca": ("sbuf", [128, 128], BF), "cr": ("sbuf", [128, 128], F16),
     "tab": ("sbuf", [128, TW], BF), "tb2": ("sbuf", [128, TW], BF),
     "d2a": ("sbuf", [128, 128], F32), "d2b": ("sbuf", [128, 256], F32), "d2": ("sbuf", [128, 512], F32),
     "off": ("sbuf", [128, 256], U16), "zp": ("sbuf", [128, 512], BF), "ta": ("sbuf", [128, 8, 16], F16),
-    "av": ("sbuf", [128, 128], BF), "r0m": ("sbuf", [128, 128], F16), "st": ("sbuf", [128, 16], F16),
+    "av": ("sbuf", [128, 128], BF), "r0m": ("sbuf", [128, 128], F16), "st": ("sbuf", [128, 128], F16),
+    "tb": ("sbuf", [128, 128], F16), "fb": ("sbuf", [128, 256], BF),
     "xg": ("sbuf", [128, 4096], BF), "ind": ("sbuf", [128, 4096], BF),
     "t2a": ("sbuf", [128, 128], F16), "t2": ("sbuf", [128, 128], BF), "uu": ("sbuf", [128, 128], BF),
     "bv": ("sbuf", [128, 128], BF), "non": ("sbuf", [128, 128], BF), "nn": ("sbuf", [128, 128], BF),
     "oh": ("sbuf", [128, 128 * TW], BF), "poff": ("sbuf", [128, 128], U16), "pofy": ("sbuf", [128, 256], U16),
     "cs": ("sbuf", [128, 5 * CS], F32), "cb": ("sbuf", [128, 4 * 66], BF), "ub": ("sbuf", [128, 256], BF),
     "phi0": ("sbuf", [128, 2048], BF), "phi1": ("sbuf", [128, 2048], BF),
-    "fl": ("sbuf", [128, 16, 17], BF), "wt": ("sbuf", [128, 8, 32], F32), "qb": ("sbuf", [128, 16 * 8, 16], F32),
+    "fl": ("sbuf", [128, 256], BF), "qb": ("sbuf", [128, 16 * 8, 16], F32),
     "rnd": ("sbuf", [128, 8, 16], F32), "h128": ("sbuf", [128, 128], BF), "hr": ("sbuf", [128, 128], BF),
     "sa": ("sbuf", [128, 128], BF), "sb": ("sbuf", [128, 128], BF), "mu": ("sbuf", [128, 128], BF),
     "tt": ("sbuf", [128, 128], F32), "fi": ("sbuf", [128, 128], I32),
     "exv": ("sbuf", [128, 2048], F32), "exw": ("sbuf", [128, 1024], F32), "zz": ("sbuf", [128, 2048], F32),
-    "zw": ("sbuf", [128, 2048], F32), "sc": ("sbuf", [128, 1024], F32), "yo": ("sbuf", [128, 128], F32),
+    "zw": ("sbuf", [128, 2048], F32), "za": ("sbuf", [128, 2048], F32), "sc": ("sbuf", [128, 4, 272], F32),
+    "yo": ("sbuf", [128, 128], F32),
 }
 for _b in range(6):
     SCRATCH["p%d" % _b] = ("psum", [128, 512], F32)
@@ -49,11 +53,12 @@ SCRATCH["pt_"] = ("psum", [128, 16, 32], F32)
 PF, PT = "pf_", "pt_"
 
 SEMAPHORES = (["cP", "cV", "cA", "cG", "sent", "l0", "l1", "l2", "l3", "l4", "l5", "o0"]
-              + ["arrW%d" % t for t in range(1, 5)] + ["arrX%d" % t for t in range(1, 5)] + ["arrG%d" % t for t in range(1, 4)])
+              + ["arrW%d" % t for t in range(1, 5)] + ["arrX%d" % t for t in range(1, 5)] + ["arrG%d" % t for t in range(1, 4)]
+              + ["add%d" % i for i in range(9)] + ["hop%d" % i for i in range(7)])
 
-PIECE, MERGE, NA, Y2, DS = 256, 9, 68, 12, 8
-YL = (7, 39, 71, 103)
-VG, VP, VU, SCAN = 512, 768, 4, (1, 2, 3)
+CUTS, CUTL = (0, 256, 768, 992, 1152, 1472, 2048), tuple(range(0, 2049, 256))
+MERGE, NA, DS, VG, PN = 5, 68, 8, 128, 12
+NVL, AL, YG, YL, LG = 112, 60, 20, (7, 39, 71, 103), (4, 7, 8)
 
 
 def _piece(name, p0, p1, dims):
@@ -63,9 +68,9 @@ def _piece(name, p0, p1, dims):
         cols = range(a, b, s)
         mask = ((1 << (b - a)) - 1) << a if s == 1 else sum(1 << c for c in cols)
         return (name, p0, p1, dims, mask, len(cols))
-    (a, b, _), (c, d, _) = dims
-    row = ((1 << (d - c)) - 1) << c
-    return (name, p0, p1, dims, sum(row << (r * shape[2]) for r in range(a, b)), (b - a) * (d - c))
+    (a, b, _), (c, d, s) = dims
+    row = sum(1 << x for x in range(c, d, s))
+    return (name, p0, p1, dims, sum(row << (r * shape[2]) for r in range(a, b)), (b - a) * len(range(c, d, s)))
 
 
 def S(name, c0=None, c1=None, step=1, p0=0, p1=128):
@@ -77,12 +82,28 @@ def S(name, c0=None, c1=None, step=1, p0=0, p1=128):
     return _piece(name, p0, p1, ((c0, c1, step),))
 
 
-def R(name, a0, a1, b0, b1, p0=0, p1=128):
-    return _piece(name, p0, p1, ((a0, a1, 1), (b0, b1, 1)))
+def R(name, a0, a1, b0, b1, p0=0, p1=128, step=1):
+    return _piece(name, p0, p1, ((a0, a1, 1), (b0, b1, step)))
 
 
 def _meet(a, b):
     return a[2] > b[1] and b[2] > a[1] and (a[4] & b[4]) != 0
+
+
+def helpers(cores, topo):
+    out = {}
+    for r, c in enumerate(cores):
+        if topo.die(c) != topo.die(cores[r - 1]):
+            out[r] = [x for x in topo.cores_of(c) if x not in cores and topo.die(x) == topo.die(c) and x not in out.values()][0]
+    return out
+
+
+def handed_on():
+    out = []
+    for t in range(NV - 1):
+        for name, sem in (("gw", "arrG"), ("vw", "arrW"))[t == NV - 2:]:
+            out.append((S(name, WW * t, WW * t + 2048), S(name, WW * t + WW, WW * t + WW + 2048), sem + str(t + 1)))
+    return out
 
 
 def plan(rank, cores, topo):
@@ -143,11 +164,20 @@ def plan(rank, cores, topo):
     def send(trs, after=()):
         put("G", "send", (trs,), [t[0] for t in trs] + list(after), [])
 
+    halves, handed = handed_on(), []
+    helper = helpers(cores, topo).get(rank)
+
+    def send_half(after=()):
+        src, dst, sem = halves[len(handed)]
+        to, hop = (prev, sem) if helper is None else (helper, "hop%d" % len(handed))
+        handed.append(sem)
+        send([(src, dst, to, sum(1 << e for e in topo.engines(cores[rank], to)), hop, sem)], after)
+
     def arrive(sem, n, bufs):
         put("X", "arr", (sem, n), [], bufs)
 
-    scales = (1.0, -32 * KAP, 32 * KAP, -BIGL, BIGL + KEY, 64.0, -1.0, 128.0, -2.0, 0.5, -32.0, -4096.0)
-    I1, IMK, IPK, IMG, IGK, I64, IM1, I128, IM2, IHALF, IM32, IM4K = [S("idb", 128 * i, 128 * i + 128) for i in range(12)]
+    scales = (1.0, -32 * KAP, 64.0, -1.0, 0.5, 32 * KAP, 128.0, -2.0, -4096.0, -32.0)
+    I1, IMK, I64, IM1, IHALF, IPK, I128, IM2, IM4K, IM32 = [S("idb", 128 * i, 128 * i + 128) for i in range(10)]
     I32F = S("ix", 0, 128)
     ID = AF.Identity
     prev = cores[(rank - 1) % 4]
@@ -181,80 +211,85 @@ def plan(rank, cores, topo):
     cp(S("ivf"), S("ivi"))
     ts(S("taf", p1=8), S("tai", p1=8), 2048.0, None, ALU.add)
     act(S("ix", 128, 256), I32F, ID)
-    for i in range(1, 12):
+    for i in range(1, 10):
         filler(act)(S("idb", 128 * i, 128 * i + 128), I32F, ID, 0.0, scales[i])
     filler(act)(S("d2b"), S("ix"), ID, 0.0, -2.0)
     ta = S("ta")
 
     def times_tail(t1):
         b = 1.5 * 2.0 ** 35
-        ts(S("rnd"), R(PT, 8, 16, 0, 16), b, b, ALU.add, ALU.subtract)
-        if t1 == 0:
-            tt(ta, R(PT, 8, 16, 0, 16), S("rnd"), ALU.subtract)
-        else:
-            tt(S("ta", p1=64), R(PT, 8, 16, 0, 16, p1=64), S("rnd", p1=64), ALU.subtract)
-            tt(R("ta", 1, 8, 0, 16, p0=64), R(PT, 8, 15, 0, 16, p0=64), R("rnd", 0, 7, 0, 16, p0=64), ALU.subtract)
-            tt(R("ta", 0, 1, 0, 16, p0=64), R(PT, 15, 16, 0, 16, p0=64), R("rnd", 7, 8, 0, 16, p0=64), ALU.subtract)
-        mm(R(PT, 0, 8, 0, 16), ta, S("id16"))
-        ts(S("off", 128, 256), R(PT, 0, 8, 0, 16), 2049.0, None, ALU.add)
-        ts(S("off", 0, 128), S("off", 128, 256), 1.0, None, ALU.subtract)
+        for g in (0, 4):
+            ts(R("rnd", g, g + 4, 0, 16), R(PF, g, g + 4, 0, 16), b, b, ALU.add, ALU.subtract)
+        cuts = ((0, 64, 0, 4, 0), (0, 64, 4, 8, 4), (64, 128, 0, 7, 1), (64, 128, 7, 8, 0))
+        for p0, p1, a, e, to in cuts if t1 else ((0, 128, 0, 4, 0), (0, 128, 4, 8, 4)):
+            tt(R("ta", to, to + e - a, 0, 16, p0, p1), R(PF, a, e, 0, 16, p0, p1), R("rnd", a, e, 0, 16, p0, p1), ALU.subtract)
+        for h, pb in enumerate(("p5", "p3")):
+            mm(S(pb, 0, 64), S("ta", p0=64 * h, p1=64 * h + 64), S("id16", 64 * h, 64 * h + 64, 1, 64 * h, 64 * h + 64))
+            ts(S("off", 128 + 64 * h, 192 + 64 * h), S(pb, 0, 64), 2049.0, None, ALU.add)
+            if t1 < NV - 1:
+                act(S("tb", 64 * h, 64 * h + 64), S(pb, 0, 64), ID)
 
     def digits(step):
         if step == 0:
             act(S("h128"), ta, ID, 192.0 - 63.0 / 128, 1.0 / 64)
             act(S("hr"), S("h128"), AF.Relu, -223.0 * 64, 64.0)
-            mm(S(PF, 0, 128), IM1, ta, True, False)
-            mm(S(PF, 0, 128), I64, S("h128"), False, True)
-            mm(S(PF, 128, 256), I1, S("h128"), True, False)
-            mm(S(PF, 128, 256), IM1, S("hr"), False, True)
+            mm(S(PF, 256, 384), IM1, ta, True, False)
+            mm(S(PF, 256, 384), I64, S("h128"), False, True)
+            mm(S(PF, 384, 512), I1, S("h128"), True, False)
+            mm(S(PF, 384, 512), IM1, S("hr"), False, True)
         else:
-            act(S("r0m"), S(PF, 0, 128), ID, -12223.0 + 1407.0)
-            act(S("av"), S(PF, 128, 256), ID, -223.0)
+            act(S("r0m"), S(PF, 256, 384), ID, -12223.0 + 1407.0)
+            act(S("av"), S(PF, 384, 512), ID, -223.0)
 
     def parts(t1, step):
         o = 256 * (t1 % 2)
         up = 128 if t1 == 0 else 112
         if step == 0:
             if t1:
-                cp(S("p4", 112, 128, p0=64), S("p4", 240, 256, p0=64))
+                act(S("p4", 112, 128, p0=64), S("p4", 240, 256, p0=64), ID)
             act(S("zp", o, o + 128, p1=64), S("p4", 128, 256, p1=64), ID)
             act(S("zp", o + 128, o + 256, p0=64), S("p4", up, up + 128, p0=64), ID)
         else:
             tt(S("zp", o, o + 128, p0=64), S("p4", 128, 256, p1=64), S("zp", o, o + 128, p1=64), ALU.subtract)
             tt(S("zp", o + 128, o + 256, p1=64), S("p4", up, up + 128, p0=64), S("zp", o + 128, o + 256, p0=64), ALU.subtract)
 
-    mm(R(PT, 8, 16, 0, 16), S("ivf"), S("trip"), True, False)
-    mm(R(PT, 8, 16, 0, 16), S("taf", p1=8), S("tsel", p1=8), False, True)
-    mm(S("p3", 0, 8), S("taf", p1=8), S("ix", 0, 8, p1=8))
+    mm(S(PF, 0, 128), S("ivf"), S("trip"), True, False)
+    mm(S(PF, 0, 128), S("taf", p1=8), S("tsel", p1=8), False, True)
     cp(S("pff"), S("pfi"))
     mm(S("p4", 128, 256), S("pff"), I32F)
     times_tail(0)
-    for h in range(2):
-        act(S("st", 8 * h, 8 * h + 8), S("p3", 0, 8), ID, -4096.0)
+    filler(act)(S("st", p1=8), S("taf", p1=8), ID, -4096.0)
     parts(0, 0)
     parts(0, 1)
     for k in range(16):
         ts(S("selk", k, 1024, 16), S("jj"), KAP, None, ALU.mult)
     cp(S("vw", 4096, 4098), S("vw", 0, 2))
-    put("S", "dma", (S("gw", 0, 4096), ("gn",), "l5"), [S("off", 128, 256)], [S("gw", 0, 4096)])
+    put("G", "dma", (S("gw", 0, 4096), ("gn",), "l5"), [S("off", 128, 256)], [S("gw", 0, 4096)])
     aff(S("rl", 0, 128), S("oneb", 0, 128), [[-1, 4], [-64, 2], [-4, 16]], ALU.is_equal, 0, 1)
     aff(S("rl", 128, 160), S("oneb", 0, 32), [[-64, 2], [-4, 16]], ALU.is_equal, 1, 1)
     aff(S("blk"), S("tri0"), [[16, 8], [0, 16]], ALU.is_ge, 15, -1)
+    aff(S("e15"), S("one32"), [[-16, 8], [0, 16]], ALU.is_equal, -15, 1)
+    filler(ms)(S("neg"), -1.0)
+    aff(S("ws"), S("neg"), [[0, 2], [-1, 8], [0, 16]], ALU.is_equal, 0, 1)
     for j in range(4):
         aff(S("ex", 512 * j, 512 * j + 512), S("oneb"), [[-1, 4], [-16, 8], [0, 16]], ALU.is_equal, -4 * j, 1)
 
     def late_constants():
         ms(S("gu", 4096, WW), 0.0)
         ms(S("zr"), 0.0)
-        mm(S("p5", 0, 128), I1, S("zr", 0, 128), True, False)
-        ms(S("fl"), 0.0)
         ms(S("cs"), 0.0)
         ms(S("ci"), 0.0)
         ms(S("ci", 128, 256), -128.0)
-        ms(S("co"), 0.0)
-        ms(R("co", 0, 8, 0, 1), 8192.0)
-        ms(S("msk"), 1.0)
-        ms(S("msk", 0, 1024, 16), 0.0)
+        act(R("wl", 0, 8, 0, 16), S("trip"), ID)
+        tt(R("wl", 0, 8, 16, 32), S("trip"), S("blk"), ALU.add)
+        act(S("tt"), I32F, ID, 0.0, -1 - BIGL / KEY)
+        tt(S("tt"), S("tt"), S("trip"), ALU.add)
+        act(R("wv", 0, 8, 0, 16), S("tt"), ID, 0.0, KEY)
+        tt(S("tt"), S("tt"), S("blk"), ALU.add)
+        act(R("wv", 0, 8, 16, 32), S("tt"), ID, 0.0, KEY)
+        act(R("wx", 0, 8, 0, 16), I32F, ID)
+        tt(R("wx", 0, 8, 16, 32), I32F, S("e15"), ALU.add)
+        ms(R("sc", 0, 4, 0, 16), 0.0)
         ms(S("fw"), 0.0)
         for c, v in ((0, 1.0), (1, -256.0), (17, 1.0), (33, 1.0), (48, 1.0), (65, 1.0), (81, 1.0)):
             ts(S("fw", c, c + 15, 2), S("idb", 0, 128, 16), v, None, ALU.mult)
@@ -275,28 +310,34 @@ def plan(rank, cores, topo):
         z = 256 * (t % 2) + 128 * (j // 2 % 2)
         mm(S(bank), S("zp", z, z + 128), S("selk", 512 * (j % 2), 512 * (j % 2) + 512), True, False)
 
-    def y_chunk(t, j, bank, out=None):
+    def y_diff(t, j, bank):
         filler(d_mm)(t, j, bank)
         mm(S(bank), IMK if t == NV - 1 else IPK, S("phi%d" % (t % 2), 512 * j, 512 * j + 512), False, True)
+
+    def y_chunk(t, j, bank, out=None, diff=True):
+        if diff:
+            y_diff(t, j, bank)
         act(S(bank), S(bank), AF.Abs, 0.0 if t == NV - 1 else -8192 * KAP)
         act(out or S("exv", 512 * j, 512 * j + 512), S(bank), AF.Exp, 0.0, -1.0 / (256 * KAP))
 
-    def y_gain(t, j):
-        for c in range(512 * j, 512 * j + 512, PIECE):
-            po = 128 * (t % 2) + c // 16
-            tt(S("zz", c, c + PIECE), gat(S("gw", WW * t, WW * t + 4104), S("pofy", po, po + PIECE // 16)),
-               S("exv", c, c + PIECE), ALU.mult)
+    def y_gain(t, a, b):
+        cuts = CUTL if t == NV - 2 else CUTS
+        for c, d in zip(cuts[a:b], cuts[a + 1:b + 1]) if t >= 0 else ():
+            po = 128 * (t % 2)
+            tt(S("zz" if t else "za", c, d), gat(S("gw", WW * t, WW * t + 4104), S("pofy", po + c // 16, po + d // 16)),
+               S("exv", c, d), ALU.mult)
 
-    def y_sum(t, h, z="zz", stop=False):
-        l = S("ix", 16 * t * h, 16 * t * h + 128)
+    def y_sum(t, z):
         for k in range(16):
-            mm(S("p5", 64 * h, 64 * h + 64), l, S(z, 1024 * h + k, 1024 * h + 1024, 16), False, k == 15 and stop)
+            mm(S("p5", 0, 64), S("ix", 16 * t, 16 * t + 128), S(z, 1024 + k, 2048, 16), k == 0 and t == 0, k == 15 and t == NV - 1)
 
-    def y_scan():
-        scan(S("sc"), S("msk"), S("zz", 0, 1024), ALU.mult)
-        mm(S("p5", 0, 64), I32F, S("sc", 15, 1024, 16), False, False)
+    def y_add(t, h, after=()):
+        r = 16 * t * h
+        for i, (a, b, n) in enumerate(((0, r, 128 - r), (128 - r, 0, r))[:1 + h] if t > 0 else ()):
+            acc, z = S("za", 1024 * h, 1024 * h + 1024, 1, a, a + n), S("zz", 1024 * h, 1024 * h + 1024, 1, b, b + n)
+            put("G", "dma", (acc, z, "add%d" % (3 * t - 3 + h + i)), [acc, z] + list(after), [acc])
 
-    y_gain, y_sum, y_scan = filler(y_gain), filler(y_sum), filler(y_scan)
+    y_sum = filler(y_sum)
     for t in range(NV):
         last = t == NV - 1
         seen.clear()
@@ -307,31 +348,36 @@ def plan(rank, cores, topo):
             arrive("arrW%d" % t, len(engines), [S("vw", w0, w0 + 2048)])
             arrive("arrX%d" % t, len(engines), [S("vw", w0 + 2048, w0 + WW)])
         if 0 < t < 4:
-            arrive("arrG%d" % t, len(engines), [S("gw", w0, w0 + WW)])
+            arrive("arrG%d" % t, 2 * len(engines), [S("gw", w0, w0 + WW)])
         if t == 0:
             filler(ms)(S("gw", 4096, WW), 0.0)
             filler(cp)(S("gw", 4096, 4098), S("gw", 0, 2))
+        early = [len(ops), len(ops) + 1] * (t < 3)
         if t < 3:
-            send([(S("gw", w0, w0 + WW), S("gw", w0 + WW, w0 + 2 * WW), prev, mask, "arrG%d" % (t + 1))], [win])
+            send_half([win])
+            send([(S("gw", w0 + 2048, w0 + WW), S("gw", w0 + WW + 2048, w0 + 2 * WW), prev, mask, "arrG%d" % (t + 1))], [win])
+        y_add(t - 2, 0, [win])
+        y_add(t - 2, 1, [win])
 
         def xgat(c0, c1):
             return S("xg", c0, c1), gat(win, S("off", c0 // 16, c1 // 16))
-        for c0, c1 in ((2048, 2560), (2560, 2560 + VG))[:1 + (VG > 0)]:
+        for c0, c1 in ((2048, 2560), (3072, 3584), (3584, 3584 + VG)):
             cp(*xgat(c0, c1))
-        for i, (c0, c1) in enumerate(((3072, 3584),) + ((2560 + VG, 3072),) * (VG < 512) + (
-                (3584, 4096), (0, 512), (512, 1024), (1024, 1536), (1536, 1792), (1792, 2048))):
+            if c0 == 2048:
+                ts(S("off", 0, 128), S("off", 128, 256), 1.0, None, ALU.subtract)
+        for i, (c0, c1) in enumerate(((2560, 3072), (3584 + VG, 4096), (0, 512), (512, 1024), (1024, 1536), (1536, 1792), (1792, 2048))):
             act(*xgat(c0, c1), ID)
             if i < 2:
                 digits(i)
-        bank = {4: "p3", 6: "p0", 5: "p1", 7: "p2", 0: PF, 1: "p3", 2: "p0"}
+        bank = {4: "p0", 5: "p1", 6: "p2", 7: "p3", 0: PF, 1: "p0", 2: "p1"}
         b = 1.5 * 2.0 ** 32
-        for j in (4, 6, 5, 7, 0, 1, 2, 3):
+        for j in (4, 5, 6, 7, 0, 1, 2, 3):
             if j != 3:
                 d_mm(t, j, bank[j])
                 mm(S(bank[j]), IMK, S("xg", 512 * j, 512 * j + 512), False, True)
                 ts(S("ind", 512 * j, 512 * j + 512), S(bank[j]), b, b, ALU.add, ALU.is_equal)
             else:
-                for h, pb in ((0, "p1"), (1, "p2")):
+                for h, pb in ((0, "p2"), (1, "p3")):
                     c = 1536 + 256 * h
                     mm(S(pb, 0, 256), S("zp", zo + 128, zo + 256), S("selk", 512 + 256 * h, 768 + 256 * h), True, False)
                     mm(S(pb, 0, 256), IMK, S("xg", c, c + 256), False, True)
@@ -349,33 +395,39 @@ def plan(rank, cores, topo):
             for k in range(15):
                 mm(S("p4", k, 128, 16, p0, p1), S("ind", 16 * p0 + k, 16 * p1, 16), S("bo"), False, False)
         mm(S("p4", 15, 128, 16), S("ind", 15, 2048, 16), S("bo"), False, True)
-        tt(S("uu"), S("p4", 0, 128), S("t2"), ALU.max)
-        tt(S("bv"), S("p4", 128, 256), S("uu"), ALU.min)
+        y_gain(t - 1, 0, 1)
+        for c in (0, 64):
+            tt(S("uu", c, c + 64), S("p4", c, c + 64), S("t2", c, c + 64), ALU.max)
+        ops[-1][5]["behind"] = early
+        for c in (0, 64):
+            tt(S("bv", c, c + 64), S("p4", 128 + c, 192 + c), S("uu", c, c + 64), ALU.min)
         act(S("non"), S("p4", 0, 128), AF.Sign, 0.5, -1.0)
         if t == 0:
             filler(late_constants)()
-        nv = 128 if last else 96
+        nv = NVL if last else 96
         for m in range(nv, 128):
             filler(act)(S("oh", TW * m, TW * m + 64), S("tb2", 0, 64), AF.Relu, S("av", m, m + 1), -1.0)
         act(S("nn"), S("bv"), AF.Relu, 8192.0, -8192.0)
-        side(True)
-        mm(S("p4", 384, 512), ta, S("id16"), True, False)
-        mm(S("p4", 384, 512), S("non"), IHALF, False, False)
-        mm(S("p4", 384, 512), S("nn"), I1, False, True)
-        ts(S("poff"), S("p4", 384, 512), 2048.5, float(DUMMY), ALU.add, ALU.min)
         mm(S("p4", 256, 512), I1, S("zr"), True, False)
-        side(False)
+        po = S("p5", 0, 128)
+        mm(po, ta, S("id16"), True, False)
+        mm(po, S("non"), IHALF, False, False)
+        mm(po, S("nn"), I1, False, True)
+        if last:
+            ts(S("poff"), po, 2048.5, float(DUMMY), ALU.add, ALU.min)
+        else:
+            mm(S(PF), I1, S("vw", w0 + 512, w0 + 1024), True, False)
+            mm(S("p3"), I1, S("vw", w0 + 2560, w0 + 3072), True, False)
 
-        def slot(s, pb, ramp, end=False):
-            c, d = (4 * CS, 256) if ramp else (CS * s, 0)
-            if ramp:
-                act(S("cs", c + 2, c + 67), S(pb, 0, 65), ID)
-            else:
-                act(S("cs", c, c + 66), S(pb, 0, 66), ID)
-            o = S("p3", 66 * s, 66 * s + 65)
-            mm(o, S("d2", d, d + 128), S("cs", c, c + 65), True, False)
-            mm(o, S("d2", d, d + 128), S("cs", c + 2, c + 67), False, False)
-            mm(o, S("d2", d + 128, d + 256), S("cs", c + 1, c + 66), False, True)
+        def slot(s, kinds, end=False):
+            ob = kinds[-1][2]
+            o = S(ob, 128, 193)
+            for p0, p1, pb, ramp in kinds:
+                c, d = CS * (4 if ramp and p0 == 0 else s), 256 * ramp
+                act(S("cs", c + 2 * ramp, c + 66 + ramp, 1, p0, p1), S(pb, 0, 66 - ramp, 1, p0, p1), ID)
+                for i, (x, y) in enumerate(((0, 0), (0, 2), (128, 1))):
+                    mm(S(ob, 128, 193, 1, p0, p1), S("d2", d + x + p0, d + x + p1, 1, p0, p1),
+                       S("cs", c + y, c + y + 65, 1, p0, p1), i == 0, i == 2)
             if end:
                 cp(S("cb", 66 * s, 66 * s + 65), o)
             else:
@@ -399,42 +451,54 @@ def plan(rank, cores, topo):
                 for x in pend:
                     mm(*x, also=S("oh", c, c + 129))
                 pend = []
-            if not last and n % 4 == 3 and na[0] < 128:
+            if n % 4 == 3 and na[0] < 128 and n > (AL if last else 0):
                 for m in (na[0], na[0] + 1):
                     act(S("oh", TW * m + 64, TW * m + 129), S("tb2", 64, 129), AF.Relu, S("bv", m, m + 1), -1.0)
                 for m in (na[0], na[0] + 1):
-                    mm(S("p2", 0, 65, 1, 64 * (m // 16 % 2), 64 * (m // 16 % 2) + 64), S("oh", TW * m, TW * m + 64),
+                    mm(S("p3" if last else "p2", 0, 65, 1, 64 * (m // 16 % 2), 64 * (m // 16 % 2) + 64), S("oh", TW * m, TW * m + 64),
                        S("oh", TW * m + 64, TW * m + 129), m % 16 == 0, m % 16 == 15,
                        also=S("oh", TW * na[0] + TW + 64, TW * na[0] + TW + 129))
                 na[0] += 2
+            if last and n == YG:
+                y_gain(t - 1, 1, LG[0])
+                y_add(t - 1, 0)
+                y_sum(0, "za")
             if last and n in YL:
                 j = (2, 3, 0, 1)[YL.index(n)]
                 pb = ("p2", PT, PF, PF)[j]
                 act(S(phi, 512 * j, 512 * j + 512), gat(win, S("poff", 32 * j, 32 * j + 32)), ID)
                 y_chunk(t, j, pb, S(pb) if j < 2 else S("exw", 512 * (j - 2), 512 * (j - 1)))
-            if n % 32 == 1 and n > 32:
-                slot(n // 32 - 1, "p%d" % ((n // 32 - 1) % 2), False)
+            if n % 32 == 1 and 32 < n < nv - 32:
+                slot(n // 32 - 1, [(0, 128, "p%d" % ((n // 32 - 1) % 2), 0)])
+            if n == PN and not last:
+                ts(S("poff"), po, 2048.5, float(DUMMY), ALU.add, ALU.min)
+                mm(S("p5"), I1, S("vw", w0 + 1536, w0 + 2048), True, False)
             if n == NA and not last:
-                slot(3, "p2", True)
+                slot(3, [(0, 128, "p2", 1)])
             if n == (NA if not last else 3) and t > 0:
                 y_chunk(t - 1, 3, PT)
-                y_gain(t - 1, 3)
-        s_last = nv // 32 - 1
-        slot(s_last, "p%d" % (s_last % 2), False, True)
+        y_gain(t - 1, LG[0] if last else 1, LG[1] if last else 2)
+        if last:
+            slot(2, [(0, 128, "p0", 0)])
+            slot(3, [(64, 128, "p3", 1), (0, 64, "p1", 0)], True)
+        else:
+            slot(1, [(0, 128, "p1", 0)])
+            slot(2, [(0, 128, "p0", 0)], True)
+            mm(S("p2"), I1, S("vw", w0 + 3584, w0 + 4096), True, False)
         ts(S("ub"), S("p4", 256, 512), 1.0, -256.0, ALU.is_equal, ALU.mult)
+        y_gain(t - 1, LG[1] if last else 2, LG[2] if last else 3)
         for j in range(8):
             if last:
                 pb = ("p3", "p0", "p4", PF, "p3", "p1", "p4", "p0")[j]
             else:
-                pb = (PF, "p1", PT, "p2", PF, "p0", PT, "p3")[j]
+                pb = (PT, PF, "p1", "p5", "p0", "p3", PT, "p2")[j]
             c = 512 * j
             col = S("vw", w0 + c, w0 + c + 512)
-            ona = j % 2 or (j == 6 and VU == 3 and not last)
-            if ona:
-                filler(mm)(S(pb), IM32 if last else I1, S("gw", c, c + 512) if last else col, True, False)
+            if j % 2 and last:
+                filler(mm)(S(pb), IM32, S("gw", c, c + 512), True, False)
             for i in range(2):
                 hx = 2 * j + i
-                mm(S(pb, 256 * i, 256 * i + 256), S("ex", 128 * hx, 128 * hx + 128), S("ub"), not ona, not ona or i == 1)
+                mm(S(pb, 256 * i, 256 * i + 256), S("ex", 128 * hx, 128 * hx + 128), S("ub"), j % 2 == 0, j % 2 == 0 or i == 1)
             if last:
                 if j % 2:
                     act(S("gu", c, c + 512), S(pb), AF.Relu, -8.0, -1.0 / 32)
@@ -443,45 +507,47 @@ def plan(rank, cores, topo):
                     if j == 2:
                         cp(S("gu", 4096, 4098), S("gu", 0, 2))
                 continue
-            if ona:
+            if j % 2:
                 act(col, S(pb), ID)
             else:
                 tt(col, S(pb), col, ALU.add)
-            if j == 1:
-                act(S("vw", w0 + 4096, w0 + 4098), S("vw", w0, w0 + 2), ID)
+            if j == 2:
+                cp(S("vw", w0 + 4096, w0 + 4098), S("vw", w0, w0 + 2))
             if j == 3:
-                send([(S("vw", w0, w0 + 2048), S("vw", w0 + WW, w0 + WW + 2048), prev, mask, "arrW%d" % (t + 1))])
+                send_half()
             if j == 7:
                 send([(S("vw", w0 + 2048, w0 + WW), S("vw", w0 + WW + 2048, w0 + 2 * WW), prev, mask, "arrX%d" % (t + 1))])
-        if t > 0:
-            if t in SCAN:
-                y_scan()
-            else:
-                y_sum(t - 1, 0)
-            y_sum(t - 1, 1)
+        y_gain(t - 1, LG[2] if last else 3, 8 if last else 4)
         if last:
+            y_sum(t - 1, "zz")
             GU = S("gu", 0, 4104)
             act(S("xg", 0, 1024), gat(GU, S("poff", 0, 64)), ID)
             tt(S("zw", 1024, 2048), gat(GU, S("poff", 64, 128)), S("exw"), ALU.mult)
             for j, pb in enumerate(("p2", PT)):
                 tt(S("zw", 512 * j, 512 * j + 512), S(pb), S("xg", 512 * j, 512 * j + 512), ALU.mult)
-            scan(S("sc"), S("msk"), S("zw", 0, 1024), ALU.mult)
-            y_sum(t, 1, "zw", True)
-            cp(S("yo", 64, 128), S("p5", 64, 128))
-            tt(S("yo", 0, 64), S("p5", 0, 64), S("sc", 15, 1024, 16), ALU.add)
+            for q in range(4):
+                scan(R("sc", q, q + 1, 16, 272), S("za", 256 * q, 256 * q + 256), S("zw", 256 * q, 256 * q + 256), ALU.add)
+            y_sum(t, "zw")
+            act(S("yo", 64, 128), S("p5", 0, 64), ID)
+            tt(S("yo", 0, 64), R("sc", 0, 4, 31, 272, step=16), R("sc", 0, 4, 15, 256, step=16), ALU.subtract)
             put("S", "dma", (("y",), S("yo"), "o0"), [S("yo")], [])
             break
-        ts(S(phi, 0, VP), gat(win, S("poff", 0, VP // 16)), -1.0, 0.0, ALU.mult, ALU.max)
-        act(S(phi, VP, 2048), gat(win, S("poff", VP // 16, 128)), AF.Relu, 0.0, -1.0)
+        for j in range(4):
+            o, a = S(phi, 512 * j, 512 * j + 512), gat(win, S("poff", 32 * j, 32 * j + 32))
+            if j % 2:
+                act(o, a, AF.Relu, 0.0, -1.0)
+            else:
+                ts(o, a, -1.0, 0.0, ALU.mult, ALU.max)
+        for j in range(2):
+            y_diff(t, j, "p%d" % j)
+        y_gain(t - 1, 4, 5)
         side(True)
         mm(S(PF, 0, 384), I1, S("ci"), True, False)
         mm(S(PF, 128, 256), I128, S("non"), False, False)
-        mm(R(PT, 0, 8, 0, 32), I1, S("co"), True, False)
+        mm(R(PT, 0, 8, 0, 32), S("tb"), S("wx"), True, False)
         for h in range(2):
-            mm(R(PT, 0, 8, 16 * h, 16 * h + 16), I1, ta, False, False)
-            mm(R(PT, 0, 8, 16 * h + 1, 16 * h + 16), IM1, R("ta", 0, 8, 0, 15), False, False)
-            s0 = (8 - t) * h
-            mm(R(PT, 0, 8, 16, 17, 64 * h, 64 * h + 64), S("idb", 768 + 64 * h, 832 + 64 * h), S("st", s0, s0 + 8), False, False)
+            g0 = (8 - t) * h
+            mm(R(PT, 0, 8, 16, 32, 64 * h, 64 * h + 64), S("st", 64 * h, 64 * h + 64, p1=8), R("ws", g0, g0 + 8, 0, 16, p1=8), False, False)
         for h in range(2):
             mm(S("p4", 0, 128, 1, 64 * h, 64 * h + 64), S("jj"), S("zp", zo + 128 * h, zo + 128 * h + 128))
         side(False)
@@ -489,55 +555,52 @@ def plan(rank, cores, topo):
         for k in range(1, 16):
             w = 48 * (k == 15)
             mm(R(PF, 0, 24, k - 1, k + 1), S(phi, k, 2048, 16), S("fw", w, w + 48), False, k == 15)
-        ts(R("fl", 0, 16, 1, 17), S(PF, 0, 256), 0.5, None, ALU.is_gt)
-        act(S("sa"), S(PF, 256, 384), AF.Sign, -0.5)
-        y_chunk(t, 0, "p0")
         for h in range(2):
-            o = R(PT, 0, 8, 16 * h, 16 * h + 16)
-            mm(o, I1, R("fl", 8, 16, 1, 17), False, False)
-            mm(o, IMG, R("fl", 0, 8, 1, 17), False, False)
-            mm(o, IGK, R("fl", 0, 8, 0, 16), False, h == 1)
-        for g in range(8):
-            scan(R("wt", g, g + 1, 0, 32), S("oneb", 0, 32), R(PT, g, g + 1, 0, 32), ALU.mult)
-        mm(S("p3", 0, 128), S("sa"), I1)
-        act(S("sb"), S("p3", 0, 128), ID)
+            ts(S("fl", 128 * h, 128 * h + 128), S(PF, 128 * h, 128 * h + 128), 0.5, None, ALU.is_gt)
+        y_gain(t - 1, 5, 6)
+        y_diff(t, 2, "p2")
+        for h in range(2):
+            mm(S(("p3", "p5")[h], 0, 128), S("fl", 128 * h, 128 * h + 128), I1)
+        act(S("fb", 0, 128), S("p3", 0, 128), ID)
+        act(S("fb", 128, 256), S("p5", 0, 128), ID)
+        act(S("sa"), S(PF, 256, 384), AF.Sign, -0.5)
+        mm(R(PT, 0, 8, 0, 32), S("fb", 0, 128), S("wv"), False, False)
+        mm(R(PT, 0, 8, 0, 32), S("fb", 128, 256), S("wl"), False, True)
+        mm(S("p3", 256, 384), S("sa"), I1)
+        act(S("sb"), S("p3", 256, 384), ID)
+        y_chunk(t, 0, "p0", diff=False)
         for k in range(16):
             mm(S("p4", 128, 256), S(phi, k, 2048, 16), IM2, k == 0, False)
         mm(S("p4", 128, 256), S("sb"), S("bl2", 0, 128), False, True)
-        mm(S("p3", 256, 384), S("sb"), S("bl2", 128, 256))
-        act(S("mu"), S("p3", 256, 384), ID, 0.5)
-        y_chunk(t, 1, "p1")
+        mm(S("p3", 384, 512), S("sb"), S("bl2", 128, 256))
+        act(S("mu"), S("p3", 384, 512), ID, 0.5)
+        y_chunk(t, 1, "p1", diff=False)
         side(True)
         mm(S("p3", 128, 256), ta, S("id16"), True, False)
         mm(S("p3", 128, 256), S("non"), IHALF, False, False)
         mm(S("p3", 128, 256), S("sa"), IM4K, False, True)
         ts(S("pofy", zo // 2, zo // 2 + 128), S("p3", 128, 256), 6144.5, float(DUMMY), ALU.add, ALU.min)
         side(False)
+        dsteps = [lambda: tt(S("tt"), S("p4", 0, 128), S("mu"), ALU.mult),
+                  lambda: ts(S("fi"), S("tt"), 4096 - 0.46875, None, ALU.add),
+                  lambda: tt(S("p4", 128, 256), S("p4", 128, 256), S("fi"), ALU.add),
+                  lambda: parts(t + 1, 0), lambda: parts(t + 1, 1)]
         for s in range(17):
             i0, i1, r = max(s - 1, 0), 15 if s == 15 else 16, 8 * min(s, 15)
-            ts(R("qb", r, r + 8, i0, i1), R("wt", 0, 8, i0 + s, i1 + s), KEY * s, KEY * (s + 1), ALU.max, ALU.min)
-            if s == DS:
-                tt(S("tt"), S("p4", 0, 128), S("mu"), ALU.mult)
-            if s == DS + 2:
-                ts(S("fi"), S("tt"), 4096 - 0.46875, None, ALU.add)
-            if s == DS + 4:
-                tt(S("p4", 128, 256), S("p4", 128, 256), S("fi"), ALU.add)
-            if s == DS + 6:
-                parts(t + 1, 0)
-            if s == 16:
-                parts(t + 1, 1)
-            if s == Y2:
-                y_chunk(t, 2, "p2")
+            ts(R("qb", r, r + 8, i0, i1), R(PT, 0, 8, i0 + s, i1 + s), KEY * s - 8192, KEY * s + 8192, ALU.max, ALU.min)
+            if s >= DS and (s - DS) % 2 == 0 and dsteps:
+                dsteps.pop(0)()
             if s < MERGE:
-                mm(R(PT, 8, 16, i0, 16), I32F, R("qb", r, r + 8, i0, 16), s == 0, False)
+                mm(R(PF, 0, 8, i0, 16), I32F, R("qb", r, r + 8, i0, 16), s == 0, False)
             elif s % 2 == 0 and s < 15:
                 w = R("qb", 8 * s - 8, 8 * s, s - 1, 16)
                 tt(w, w, R("qb", 8 * s, 8 * s + 8, s - 1, 16), ALU.add)
-                mm(R(PT, 8, 16, s - 2, 16), I32F, R("qb", 8 * s - 8, 8 * s, s - 2, 16), False, False)
-        mm(R(PT, 8, 16, 14, 16), I32F, R("qb", 120, 128, 14, 16), False, True)
+                mm(R(PF, 0, 8, s - 2, 16), I32F, R("qb", 8 * s - 8, 8 * s, s - 2, 16), False, False)
+        mm(R(PF, 0, 8, 14, 16), I32F, R("qb", 120, 128, 14, 16), False, True)
+        y_chunk(t, 2, "p2", diff=False)
         times_tail(t + 1)
-        for j in range(3):
-            y_gain(t, j)
+        for f in dsteps:
+            f()
         if t == 0:
             for j in range(4):
                 filler(ts)(S("gneg", 512 * j, 512 * j + 512), S("gw", 1024 * j, 1024 * j + 512), -1.0 / 256, None, ALU.mult)
@@ -578,9 +641,10 @@ def order(ops):
     return deps, after
 
 
-CYC, PCYC, GATHER, HOP = 0.00104, 0.00052, 1.56, 0.13
-FLIGHT = {"W": 4.0, "X": 4.0, "G": 8.0}
-PASSES, MOVES = 4, 150
+CYC, PCYC, GATHER, HOP, HOPS = 0.00104, 0.00052, 1.56, 0.19, (0.12, 0.3)
+FLIGHT = {"W": 6.0, "X": 4.0, "G": 8.0}
+LOAD = {"ivi": 2.0, "tai": 2.0, "pfi": 2.0, "za": 9.0}
+PASSES, MOVES = 3, 150
 
 
 def _cost(op):
@@ -594,7 +658,7 @@ def _cost(op):
     if kind == "mm":
         return max(min(64, n(a[1])), n(a[2])) * PCYC * (4 if SCRATCH[a[1][0]][2] == F32 else 1)
     if kind in ("dma", "send", "arr"):
-        return {"dma": 0.1, "send": 0.5, "arr": 0.0}[kind]
+        return {"dma": 1.0 if q == "G" else 0.1, "send": 0.5, "arr": 0.0}[kind]
     if kind in ("aff", "iota"):
         return 0.17 + 2 * n(a[0]) * CYC
     if kind == "ms":
@@ -611,16 +675,16 @@ def _cost(op):
 def schedule(ops, deps, after):
     n = len(ops)
     cost = [_cost(o) for o in ops]
-    pred = [[(j, HOP) for j in deps[i]] + [(j, 0.0) for j in after.get(i, [])] for i in range(n)]
+    pred = [[(j, HOP) for j in deps[i]] + [(j, 0.0) for j in after.get(i, []) + ops[i][5].get("behind", [])] for i in range(n)]
     sender = {}
     for i, o in enumerate(ops):
         if o[1] == "send":
             for tr in o[2][0]:
-                sender[tr[4]] = i
+                sender[tr[-1]] = i
         if o[1] == "arr":
             pred[i] = [(sender[o[2][0]], FLIGHT[o[2][0][3]])]
     for i in range(n):
-        pred[i] = [(j, (2.0 if ops[j][2][0][0] in ("ivi", "tai", "pfi") else 4.5) if ops[j][1] == "dma" else w) for j, w in pred[i]]
+        pred[i] = [(j, LOAD.get(ops[j][2][0][0], 4.5) if ops[j][1] == "dma" else w) for j, w in pred[i]]
     succ = [[] for _ in range(n)]
     for i in range(n):
         for j, w in pred[i]:
@@ -668,10 +732,22 @@ def schedule(ops, deps, after):
                     out.append(j)
         return out
 
+    def worth(start):
+        total = 0.0
+        seq = sorted(range(n), key=lambda i: (start[i], i))
+        for hop in HOPS:
+            end, free = [0.0] * n, {}
+            for i in seq:
+                t = max([end[j] + (hop if w == HOP else w) for j, w in pred[i]] + [free.get(ops[i][0], 0.0) if ops[i][0] != "X" else 0.0])
+                end[i] = free[ops[i][0]] = t + cost[i]
+            total += max(end) / (1 + hop)
+        return total
+
     best = None
     for seq in (pulled([j for j in range(n) if not ops[j][5]["late"]] + list(range(n))), list(range(n))):
         for _ in range(PASSES):
-            start, span = lay(seq, pred)
+            start, _ = lay(seq, pred)
+            span = worth(start)
             if best is None or span < best[0]:
                 best = (span, start)
             seq = again(start)
@@ -694,19 +770,20 @@ def schedule(ops, deps, after):
             if j < 0:
                 break
             i = j
-        pairs = [p for p in pairs if (ops[p[1]][5]["kind"], ops[p[2]][5]["kind"]) not in tried
-                 and ops[p[1]][2][0][0] != ops[p[2]][2][0][0]]
-        if not pairs:
+        moves = [(w, ops[i][5]["kind"], how) for w, i, j in pairs for how in (0, 1)]
+        moves += [(w, ops[j][5]["kind"], 2) for w, i, j in pairs if ops[j][5]["late"]]
+        moves = [m for m in moves if m[1:] not in tried and m[0] > 0.05]
+        if not moves:
             break
-        _, i, j = max(pairs)
-        tried.add((ops[i][5]["kind"], ops[j][5]["kind"]))
+        w, kind, how = max(moves)
+        tried.add((kind, how))
         key = list(start)
-        for a in twins[ops[i][5]["kind"]]:
-            for b in twins[ops[j][5]["kind"]]:
-                if 0 < key[a] - key[b] < 8:
-                    key[a] = key[b] - 1e-5
-        s1, e1 = lay(pulled(sorted(range(n), key=lambda k: (key[k], k))), pred)
-        s2, e2 = lay(again(s1), pred)
+        for a in twins[kind]:
+            ready = max([start[k] + cost[k] + x for k, x in pred[a]] + [0.0])
+            key[a] = (ready - 1e-5, ready - 0.6, start[a] + 1.5)[how]
+        s1, _ = lay(pulled(sorted(range(n), key=lambda k: (key[k], k))), pred)
+        s2, _ = lay(again(s1), pred)
+        e1, e2 = worth(s1), worth(s2)
         if e1 < e2:
             s2, e2 = s1, e1
         if e2 < span - 1e-6:
@@ -733,6 +810,16 @@ def ordered(ops):
 def rank_program(g, core, T, topo):
     rank = T.rank_of(core)
     if rank is None:
+        cores = list(T.cores)
+        for r, c in helpers(cores, topo).items():
+            if c == core:
+                rid, pid, _ = topo.addr(cores[r - 1])
+                engines = topo.engines(core, cores[r - 1])
+                for i, (_, dst, sem) in enumerate(handed_on()):
+                    piece = T[dst[0]][:, dst[3][0][0]:dst[3][0][1]]
+                    g.wait_ge(T.sem["hop%d" % i], len(topo.engines(cores[r], core)))
+                    g.remote_dma(piece, piece, T.sem[sem], T.sem.sent, pid, rid, sum(1 << e for e in engines))
+                g.wait_ge(T.sem.sent, len(engines) * len(handed_on()))
         return
     ops, deps = ordered(plan(rank, list(T.cores), topo))
     queue = {"P": g.tensor, "V": g.vector, "A": g.scalar, "G": g, "S": g.sync}
@@ -814,11 +901,14 @@ def rank_program(g, core, T, topo):
         elif kind == "iota":
             ins = e.iota(ap(a[0]), a[1], a[2], 0, allow_small_or_imprecise_dtypes=True)
         elif kind == "dma":
-            e.dma_start(ap(a[0]), ap(a[1])).then_inc(T.sem[a[2]], 16)
+            if a[0][0] == "za":
+                e.dma_start(ap(a[0]), ap(a[1]), accum_op=ALU.add).then_inc(T.sem[a[2]], 16)
+            else:
+                e.dma_start(ap(a[0]), ap(a[1])).then_inc(T.sem[a[2]], 16)
             continue
         else:
             trs = []
-            for src, dst, c, mask, sem in a[0]:
+            for src, dst, c, mask, sem in [x[:5] for x in a[0]]:
                 rid, pid, _ = topo.addr(c)
                 trs.append(RemoteDMATransfer(dst_ids=[DstId(rid=rid, pnc=pid)], dma_engine_mask=mask,
                                              remote_sem=T.sem[sem], src=ap(src), dst=ap(dst)))

from concourse.bass import DstId, RemoteDMATransfer
from concourse.mybir import AluOpType as ALU, ActivationFunctionType as AF

F32, BF, F16, I32, U16 = "float32", "bfloat16", "float16", "int32", "uint16"
NV = 5
KEY = 16384.0
BIGL = 1048576.0
DUMMY = 4098
KAP = 51.0 / 32
TW = 130
CS = 68
WW = 4112

SCRATCH = {
    "vw": ("sbuf", [128, 5 * WW], BF), "gw": ("sbuf", [128, 4 * WW], BF),
    "gneg": ("sbuf", [128, 2048], BF), "gu": ("sbuf", [128, WW], BF),
    "ivi": ("sbuf", [128, 128], I32), "pfi": ("sbuf", [128, 128], I32), "tai": ("sbuf", [128, 128], I32),
    "ivf": ("sbuf", [128, 128], F32), "pff": ("sbuf", [128, 128], F32), "taf": ("sbuf", [128, 128], F32),
    "one32": ("sbuf", [128, 128], F32), "oneb": ("sbuf", [128, 512], BF), "zr": ("sbuf", [128, 256], BF),
    "ix": ("sbuf", [128, 256], F32), "trip": ("sbuf", [128, 128], F32), "tri0": ("sbuf", [128, 128], F32),
    "tsel": ("sbuf", [128, 128], F32), "blk": ("sbuf", [128, 128], F32), "bl2": ("sbuf", [128, 256], BF),
    "idb": ("sbuf", [128, 10 * 128], BF), "id16": ("sbuf", [128, 128], F16),
    "jj": ("sbuf", [128, 64], BF), "selk": ("sbuf", [128, 1024], BF),
    "ex": ("sbuf", [128, 2048], BF), "rl": ("sbuf", [128, 160], BF),
    "bo1": ("sbuf", [128, 8], BF), "bo0": ("sbuf", [128, 8], BF), "bo": ("sbuf", [128, 8], BF),
    "fw": ("sbuf", [128, 96], BF), "ci": ("sbuf", [128, 384], BF),
    "wl": ("sbuf", [128, 8, 32], BF), "wv": ("sbuf", [128, 8, 32], BF), "wx": ("sbuf", [128, 8, 32], BF),
    "ws": ("sbuf", [128, 16, 16], BF), "e15": ("sbuf", [128, 128], F32), "neg": ("sbuf", [128, 256], BF),
    "ca": ("sbuf", [128, 128], BF), "cr": ("sbuf", [128, 128], F16),
    "tab": ("sbuf", [128, TW], BF), "tb2": ("sbuf", [128, TW], BF),
    "d2a": ("sbuf", [128, 128], F32), "d2b": ("sbuf", [128, 256], F32), "d2": ("sbuf", [128, 512], F32),
    "off": ("sbuf", [128, 256], U16), "zp": ("sbuf", [128, 512], BF), "ta": ("sbuf", [128, 8, 16], F16),
    "av": ("sbuf", [128, 128], BF), "r0m": ("sbuf", [128, 128], F16), "st": ("sbuf", [128, 128], F16),
    "tb": ("sbuf", [128, 128], F16), "fb": ("sbuf", [128, 256], BF),
    "xg": ("sbuf", [128, 4096], BF), "ind": ("sbuf", [128, 4096], BF),
    "t2a": ("sbuf", [128, 128], F16), "t2": ("sbuf", [128, 128], BF), "uu": ("sbuf", [128, 128], BF),
    "bv": ("sbuf", [128, 128], BF), "non": ("sbuf", [128, 128], BF), "nn": ("sbuf", [128, 128], BF),
    "oh": ("sbuf", [128, 128 * TW], BF), "poff": ("sbuf", [128, 128], U16), "pofy": ("sbuf", [128, 256], U16),
    "cs": ("sbuf", [128, 5 * CS], F32), "cb": ("sbuf", [128, 4 * 66], BF), "ub": ("sbuf", [128, 256], BF),
    "phi0": ("sbuf", [128, 2048], BF), "phi1": ("sbuf", [128, 2048], BF),
    "fl": ("sbuf", [128, 256], BF), "qb": ("sbuf", [128, 16 * 8, 16], F32),
    "rnd": ("sbuf", [128, 8, 16], F32), "h128": ("sbuf", [128, 128], BF), "hr": ("sbuf", [128, 128], BF),
    "sa": ("sbuf", [128, 128], BF), "sb": ("sbuf", [128, 128], BF), "mu": ("sbuf", [128, 128], BF),
    "tt": ("sbuf", [128, 128], F32), "fi": ("sbuf", [128, 128], I32),
    "exv": ("sbuf", [128, 2048], F32), "exw": ("sbuf", [128, 1024], F32), "zz": ("sbuf", [128, 2048], F32),
    "zw": ("sbuf", [128, 2048], F32), "za": ("sbuf", [128, 2048], F32), "sc": ("sbuf", [128, 4, 272], F32),
    "yo": ("sbuf", [128, 128], F32),
}
for _b in range(6):
    SCRATCH["p%d" % _b] = ("psum", [128, 512], F32)
SCRATCH["pf_"] = ("psum", [128, 32, 16], F32)
SCRATCH["pt_"] = ("psum", [128, 16, 32], F32)
PF, PT = "pf_", "pt_"

SEMAPHORES = (["cP", "cV", "cA", "cG", "sent", "l0", "l1", "l2", "l3", "l4", "l5", "o0"]
              + ["arrW%d" % t for t in range(1, 5)] + ["arrX%d" % t for t in range(1, 5)] + ["arrG%d" % t for t in range(1, 4)]
              + ["add%d" % i for i in range(9)] + ["hop%d" % i for i in range(7)])

CUTS, CUTL = (0, 256, 768, 992, 1152, 1472, 2048), tuple(range(0, 2049, 256))
MERGE, NA, DS, VG, PN = 5, 68, 8, 128, 12
NVL, AL, YG, YL, LG = 112, 60, 20, (7, 39, 71, 103), (4, 7, 8)


def _piece(name, p0, p1, dims):
    shape = SCRATCH[name][1]
    if len(dims) == 1:
        a, b, s = dims[0]
        cols = range(a, b, s)
        mask = ((1 << (b - a)) - 1) << a if s == 1 else sum(1 << c for c in cols)
        return (name, p0, p1, dims, mask, len(cols))
    (a, b, _), (c, d, s) = dims
    row = sum(1 << x for x in range(c, d, s))
    return (name, p0, p1, dims, sum(row << (r * shape[2]) for r in range(a, b)), (b - a) * len(range(c, d, s)))


def S(name, c0=None, c1=None, step=1, p0=0, p1=128):
    shape = SCRATCH[name][1]
    if c0 is None:
        c0, c1 = 0, shape[1] * (shape[2] if len(shape) == 3 else 1)
    if len(shape) == 3:
        return _piece(name, p0, p1, ((c0 // shape[2], c1 // shape[2], 1), (0, shape[2], 1)))
    return _piece(name, p0, p1, ((c0, c1, step),))


def R(name, a0, a1, b0, b1, p0=0, p1=128, step=1):
    return _piece(name, p0, p1, ((a0, a1, 1), (b0, b1, step)))


def _meet(a, b):
    return a[2] > b[1] and b[2] > a[1] and (a[4] & b[4]) != 0


def helpers(cores, topo):
    out = {}
    for r, c in enumerate(cores):
        if topo.die(c) != topo.die(cores[r - 1]):
            out[r] = [x for x in topo.cores_of(c) if x not in cores and topo.die(x) == topo.die(c) and x not in out.values()][0]
    return out


def handed_on():
    out = []
    for t in range(NV - 1):
        for name, sem in (("gw", "arrG"), ("vw", "arrW"))[t == NV - 2:]:
            out.append((S(name, WW * t, WW * t + 2048), S(name, WW * t + WW, WW * t + WW + 2048), sem + str(t + 1)))
    return out


def plan(rank, cores, topo):
    ops = []
    late = [0]
    seen = {}

    def side(on):
        late[0] += 1 if on else -1

    def filler(f):
        def run(*a, **k):
            side(True)
            f(*a, **k)
            side(False)
        return run

    def put(q, kind, args, reads, writes, **opt):
        opt["late"] = late[0] > 0
        name = (q, kind, args[0][0] if kind != "send" else "")
        seen[name] = seen.get(name, 0) + 1
        opt["kind"] = name + (seen[name],)
        ops.append((q, kind, args, [r for r in reads if isinstance(r, tuple)], writes, opt))

    def rd(x):
        return [x[1], x[2]] if x[0] == "*" else [x]

    def ts(out, a, s1, s2, o0, o1=None):
        put("V", "ts", (out, a, s1, s2, o0, o1), rd(a) + [s1, s2], [out])

    def tt(out, a, b, o):
        put("V", "tt", (out, a, b, o), rd(a) + [b], [out])

    def cp(out, a):
        put("V", "cp", (out, a), rd(a), [out])

    def ms(out, v):
        put("V", "ms", (out, v), [], [out])

    def scan(out, a, b, o):
        put("V", "scan", (out, a, b, o), [a, b], [out])

    def act(out, a, f, bias=0.0, scale=1.0):
        put("A", "act", (out, a, f, bias, scale), rd(a) + [bias], [out])

    def mm(out, l, r, st=True, sp=True, **opt):
        put("P", "mm", (out, l, r, st, sp), [l, r], [out], **opt)

    def aff(out, a, pat, cmp, base, cm):
        put("G", "aff", (out, a, pat, cmp, base, cm), [a], [out])

    def iota(out, pat, base):
        put("G", "iota", (out, pat, base), [], [out])

    def gat(win, off):
        return ("*", win, off)

    def send(trs, after=()):
        put("G", "send", (trs,), [t[0] for t in trs] + list(after), [])

    halves, handed = handed_on(), []
    helper = helpers(cores, topo).get(rank)

    def send_half(after=()):
        src, dst, sem = halves[len(handed)]
        to, hop = (prev, sem) if helper is None else (helper, "hop%d" % len(handed))
        handed.append(sem)
        send([(src, dst, to, sum(1 << e for e in topo.engines(cores[rank], to)), hop, sem)], after)

    def arrive(sem, n, bufs):
        put("X", "arr", (sem, n), [], bufs)

    scales = (1.0, -32 * KAP, 64.0, -1.0, 0.5, 32 * KAP, 128.0, -2.0, -4096.0, -32.0)
    I1, IMK, I64, IM1, IHALF, IPK, I128, IM2, IM4K, IM32 = [S("idb", 128 * i, 128 * i + 128) for i in range(10)]
    I32F = S("ix", 0, 128)
    ID = AF.Identity
    prev = cores[(rank - 1) % 4]
    engines = topo.engines(cores[rank], prev)
    mask = sum(1 << e for e in engines)

    put("S", "dma", (S("ivi"), ("iv",), "l0"), [], [S("ivi")])
    put("A", "dma", (S("tai", p1=8), ("tau",), "l1"), [], [S("tai", p1=8)])
    put("S", "dma", (S("pfi"), ("pf",), "l4"), [], [S("pfi")])
    put("A", "dma", (S("vw", 2048, 4096), ("xs", 2048, 4096), "l3"), [], [S("vw", 2048, 4096)])
    put("S", "dma", (S("vw", 0, 2048), ("xs", 0, 2048), "l2"), [], [S("vw", 0, 2048)])
    ms(S("one32"), 1.0)
    ms(S("oneb"), 1.0)
    aff(S("ix", 0, 128), S("one32"), [[-1, 128]], ALU.is_equal, 0, 1)
    aff(S("tri0"), S("one32"), [[-16, 8], [0, 16]], ALU.is_ge, 0, 1)
    aff(S("trip"), S("tri0"), [[16, 8], [1, 16]], ALU.is_ge, 0, -1)
    aff(S("tsel"), S("one32"), [[-1, 8], [0, 16]], ALU.is_equal, 0, 1)
    ms(S("bo1"), 128.0)
    aff(S("bo0"), S("bo1"), [[-16, 8]], ALU.is_ge, 0, 1)
    aff(S("bo"), S("bo0"), [[16, 8]], ALU.is_ge, 15, -1)
    iota(S("tab", 0, 66), [[-1, 66]], 66)
    iota(S("tab", 66, TW), [[1, TW - 66]], -63)
    iota(S("tb2", 0, 64), [[1, 64]], -64)
    iota(S("tb2", 64, TW), [[-1, TW - 64]], 64)
    ms(S("vw", 4096, WW), 1.0)
    ms(S("ca"), -1408.0)
    ms(S("cr"), -1407.0)
    cp(S("id16"), I32F)
    cp(I1, I32F)
    tt(S("jj"), S("idb", 0, 64), S("idb", 64, 128), ALU.add)
    cp(S("ivf"), S("ivi"))
    ts(S("taf", p1=8), S("tai", p1=8), 2048.0, None, ALU.add)
    act(S("ix", 128, 256), I32F, ID)
    for i in range(1, 10):
        filler(act)(S("idb", 128 * i, 128 * i + 128), I32F, ID, 0.0, scales[i])
    filler(act)(S("d2b"), S("ix"), ID, 0.0, -2.0)
    ta = S("ta")

    def times_tail(t1):
        b = 1.5 * 2.0 ** 35
        for g in (0, 4):
            ts(R("rnd", g, g + 4, 0, 16), R(PF, g, g + 4, 0, 16), b, b, ALU.add, ALU.subtract)
        cuts = ((0, 64, 0, 4, 0), (0, 64, 4, 8, 4), (64, 128, 0, 7, 1), (64, 128, 7, 8, 0))
        for p0, p1, a, e, to in cuts if t1 else ((0, 128, 0, 4, 0), (0, 128, 4, 8, 4)):
            tt(R("ta", to, to + e - a, 0, 16, p0, p1), R(PF, a, e, 0, 16, p0, p1), R("rnd", a, e, 0, 16, p0, p1), ALU.subtract)
        for h, pb in enumerate(("p5", "p3")):
            mm(S(pb, 0, 64), S("ta", p0=64 * h, p1=64 * h + 64), S("id16", 64 * h, 64 * h + 64, 1, 64 * h, 64 * h + 64))
            ts(S("off", 128 + 64 * h, 192 + 64 * h), S(pb, 0, 64), 2049.0, None, ALU.add)
            if t1 < NV - 1:
                act(S("tb", 64 * h, 64 * h + 64), S(pb, 0, 64), ID)

    def digits(step):
        if step == 0:
            act(S("h128"), ta, ID, 192.0 - 63.0 / 128, 1.0 / 64)
            act(S("hr"), S("h128"), AF.Relu, -223.0 * 64, 64.0)
            mm(S(PF, 256, 384), IM1, ta, True, False)
            mm(S(PF, 256, 384), I64, S("h128"), False, True)
            mm(S(PF, 384, 512), I1, S("h128"), True, False)
            mm(S(PF, 384, 512), IM1, S("hr"), False, True)
        else:
            act(S("r0m"), S(PF, 256, 384), ID, -12223.0 + 1407.0)
            act(S("av"), S(PF, 384, 512), ID, -223.0)

    def parts(t1, step):
        o = 256 * (t1 % 2)
        up = 128 if t1 == 0 else 112
        if step == 0:
            if t1:
                act(S("p4", 112, 128, p0=64), S("p4", 240, 256, p0=64), ID)
            act(S("zp", o, o + 128, p1=64), S("p4", 128, 256, p1=64), ID)
            act(S("zp", o + 128, o + 256, p0=64), S("p4", up, up + 128, p0=64), ID)
        else:
            tt(S("zp", o, o + 128, p0=64), S("p4", 128, 256, p1=64), S("zp", o, o + 128, p1=64), ALU.subtract)
            tt(S("zp", o + 128, o + 256, p1=64), S("p4", up, up + 128, p0=64), S("zp", o + 128, o + 256, p0=64), ALU.subtract)

    mm(S(PF, 0, 128), S("ivf"), S("trip"), True, False)
    mm(S(PF, 0, 128), S("taf", p1=8), S("tsel", p1=8), False, True)
    cp(S("pff"), S("pfi"))
    mm(S("p4", 128, 256), S("pff"), I32F)
    times_tail(0)
    filler(act)(S("st", p1=8), S("taf", p1=8), ID, -4096.0)
    parts(0, 0)
    parts(0, 1)
    for k in range(16):
        ts(S("selk", k, 1024, 16), S("jj"), KAP, None, ALU.mult)
    cp(S("vw", 4096, 4098), S("vw", 0, 2))
    put("G", "dma", (S("gw", 0, 4096), ("gn",), "l5"), [S("off", 128, 256)], [S("gw", 0, 4096)])
    aff(S("rl", 0, 128), S("oneb", 0, 128), [[-1, 4], [-64, 2], [-4, 16]], ALU.is_equal, 0, 1)
    aff(S("rl", 128, 160), S("oneb", 0, 32), [[-64, 2], [-4, 16]], ALU.is_equal, 1, 1)
    aff(S("blk"), S("tri0"), [[16, 8], [0, 16]], ALU.is_ge, 15, -1)
    aff(S("e15"), S("one32"), [[-16, 8], [0, 16]], ALU.is_equal, -15, 1)
    filler(ms)(S("neg"), -1.0)
    aff(S("ws"), S("neg"), [[0, 2], [-1, 8], [0, 16]], ALU.is_equal, 0, 1)
    for j in range(4):
        aff(S("ex", 512 * j, 512 * j + 512), S("oneb"), [[-1, 4], [-16, 8], [0, 16]], ALU.is_equal, -4 * j, 1)

    def late_constants():
        ms(S("gu", 4096, WW), 0.0)
        ms(S("zr"), 0.0)
        ms(S("cs"), 0.0)
        ms(S("ci"), 0.0)
        ms(S("ci", 128, 256), -128.0)
        act(R("wl", 0, 8, 0, 16), S("trip"), ID)
        tt(R("wl", 0, 8, 16, 32), S("trip"), S("blk"), ALU.add)
        act(S("tt"), I32F, ID, 0.0, -1 - BIGL / KEY)
        tt(S("tt"), S("tt"), S("trip"), ALU.add)
        act(R("wv", 0, 8, 0, 16), S("tt"), ID, 0.0, KEY)
        tt(S("tt"), S("tt"), S("blk"), ALU.add)
        act(R("wv", 0, 8, 16, 32), S("tt"), ID, 0.0, KEY)
        act(R("wx", 0, 8, 0, 16), I32F, ID)
        tt(R("wx", 0, 8, 16, 32), I32F, S("e15"), ALU.add)
        ms(R("sc", 0, 4, 0, 16), 0.0)
        ms(S("fw"), 0.0)
        for c, v in ((0, 1.0), (1, -256.0), (17, 1.0), (33, 1.0), (48, 1.0), (65, 1.0), (81, 1.0)):
            ts(S("fw", c, c + 15, 2), S("idb", 0, 128, 16), v, None, ALU.mult)
        cp(S("rl", 128, 160, 16), S("idb", 63, 128, 64))
        act(S("bl2", 0, 128), S("blk"), ID, 0.0, 256.0)
        act(S("bl2", 128, 256), S("blk"), ID, 0.0, -1.0 / 32)
        tt(S("d2a"), S("ix", 0, 128), S("ix", 2, 130), ALU.add)
        tt(S("d2", 256, 384), S("d2a"), S("d2b", 1, 129), ALU.add)
        tt(S("d2", 318, 384, 64), S("ix", 62, 128, 64), S("d2b", 63, 128, 64), ALU.add)
        cp(S("d2", 319, 384, 64), S("ix", 63, 128, 64))
        act(S("d2", 384, 512), S("d2", 256, 384), ID, 0.0, -2.0)
        act(S("d2", 0, 128), S("d2", 256, 384), ID, 0.0, -1.0)
        tt(S("d2", 0, 128, 64), S("ix", 1, 128, 64), S("ix", 2, 128, 64), ALU.subtract)
        tt(S("d2", 63, 128, 64), S("d2", 63, 128, 64), S("ix", 0, 128, 64), ALU.subtract)
        act(S("d2", 128, 256), S("d2", 0, 128), ID, 0.0, -2.0)

    def d_mm(t, j, bank):
        z = 256 * (t % 2) + 128 * (j // 2 % 2)
        mm(S(bank), S("zp", z, z + 128), S("selk", 512 * (j % 2), 512 * (j % 2) + 512), True, False)

    def y_diff(t, j, bank):
        filler(d_mm)(t, j, bank)
        mm(S(bank), IMK if t == NV - 1 else IPK, S("phi%d" % (t % 2), 512 * j, 512 * j + 512), False, True)

    def y_chunk(t, j, bank, out=None, diff=True):
        if diff:
            y_diff(t, j, bank)
        act(S(bank), S(bank), AF.Abs, 0.0 if t == NV - 1 else -8192 * KAP)
        act(out or S("exv", 512 * j, 512 * j + 512), S(bank), AF.Exp, 0.0, -1.0 / (256 * KAP))

    def y_gain(t, a, b):
        cuts = CUTL if t == NV - 2 else CUTS
        for c, d in zip(cuts[a:b], cuts[a + 1:b + 1]) if t >= 0 else ():
            po = 128 * (t % 2)
            tt(S("zz" if t else "za", c, d), gat(S("gw", WW * t, WW * t + 4104), S("pofy", po + c // 16, po + d // 16)),
               S("exv", c, d), ALU.mult)

    def y_sum(t, z):
        for k in range(16):
            mm(S("p5", 0, 64), S("ix", 16 * t, 16 * t + 128), S(z, 1024 + k, 2048, 16), k == 0 and t == 0, k == 15 and t == NV - 1)

    def y_add(t, h, after=()):
        r = 16 * t * h
        for i, (a, b, n) in enumerate(((0, r, 128 - r), (128 - r, 0, r))[:1 + h] if t > 0 else ()):
            acc, z = S("za", 1024 * h, 1024 * h + 1024, 1, a, a + n), S("zz", 1024 * h, 1024 * h + 1024, 1, b, b + n)
            put("G", "dma", (acc, z, "add%d" % (3 * t - 3 + h + i)), [acc, z] + list(after), [acc])

    y_sum = filler(y_sum)
    for t in range(NV):
        last = t == NV - 1
        seen.clear()
        phi = "phi%d" % (t % 2)
        w0, zo = WW * t, 256 * (t % 2)
        win = S("vw", w0, w0 + 4104)
        if t > 0:
            arrive("arrW%d" % t, len(engines), [S("vw", w0, w0 + 2048)])
            arrive("arrX%d" % t, len(engines), [S("vw", w0 + 2048, w0 + WW)])
        if 0 < t < 4:
            arrive("arrG%d" % t, 2 * len(engines), [S("gw", w0, w0 + WW)])
        if t == 0:
            filler(ms)(S("gw", 4096, WW), 0.0)
            filler(cp)(S("gw", 4096, 4098), S("gw", 0, 2))
        early = [len(ops), len(ops) + 1] * (t < 3)
        if t < 3:
            send_half([win])
            send([(S("gw", w0 + 2048, w0 + WW), S("gw", w0 + WW + 2048, w0 + 2 * WW), prev, mask, "arrG%d" % (t + 1))], [win])
        y_add(t - 2, 0, [win])
        y_add(t - 2, 1, [win])

        def xgat(c0, c1):
            return S("xg", c0, c1), gat(win, S("off", c0 // 16, c1 // 16))
        for c0, c1 in ((2048, 2560), (3072, 3584), (3584, 3584 + VG)):
            cp(*xgat(c0, c1))
            if c0 == 2048:
                ts(S("off", 0, 128), S("off", 128, 256), 1.0, None, ALU.subtract)
        for i, (c0, c1) in enumerate(((2560, 3072), (3584 + VG, 4096), (0, 512), (512, 1024), (1024, 1536), (1536, 1792), (1792, 2048))):
            act(*xgat(c0, c1), ID)
            if i < 2:
                digits(i)
        bank = {4: "p0", 5: "p1", 6: "p2", 7: "p3", 0: PF, 1: "p0", 2: "p1"}
        b = 1.5 * 2.0 ** 32
        for j in (4, 5, 6, 7, 0, 1, 2, 3):
            if j != 3:
                d_mm(t, j, bank[j])
                mm(S(bank[j]), IMK, S("xg", 512 * j, 512 * j + 512), False, True)
                ts(S("ind", 512 * j, 512 * j + 512), S(bank[j]), b, b, ALU.add, ALU.is_equal)
            else:
                for h, pb in ((0, "p2"), (1, "p3")):
                    c = 1536 + 256 * h
                    mm(S(pb, 0, 256), S("zp", zo + 128, zo + 256), S("selk", 512 + 256 * h, 768 + 256 * h), True, False)
                    mm(S(pb, 0, 256), IMK, S("xg", c, c + 256), False, True)
                    ts(S("ind", c, c + 256), S(pb, 0, 256), b, b, ALU.add, ALU.is_equal)
            if j == 0:
                for k in range(16):
                    mm(R(PT, 0, 8, k, k + 1), S("ind", 2048 + k, 4096, 16), S("bo"))
                mm(S("p4", 128, 256), I1, S("r0m"), True, False)
                mm(S("p4", 128, 256), I1, S("cr"), False, True)
                mm(S("p4", 0, 128), I1, S("ca"), True, False)
            if j == 1:
                tt(S("t2a"), R(PT, 0, 8, 0, 16), S("r0m"), ALU.min)
                act(S("t2"), S("t2a"), AF.Relu, -1408.0)
        for p0, p1 in ((0, 64), (64, 96), (96, 128)):
            for k in range(15):
                mm(S("p4", k, 128, 16, p0, p1), S("ind", 16 * p0 + k, 16 * p1, 16), S("bo"), False, False)
        mm(S("p4", 15, 128, 16), S("ind", 15, 2048, 16), S("bo"), False, True)
        y_gain(t - 1, 0, 1)
        for c in (0, 64):
            tt(S("uu", c, c + 64), S("p4", c, c + 64), S("t2", c, c + 64), ALU.max)
        ops[-1][5]["behind"] = early
        for c in (0, 64):
            tt(S("bv", c, c + 64), S("p4", 128 + c, 192 + c), S("uu", c, c + 64), ALU.min)
        act(S("non"), S("p4", 0, 128), AF.Sign, 0.5, -1.0)
        if t == 0:
            filler(late_constants)()
        nv = NVL if last else 96
        for m in range(nv, 128):
            filler(act)(S("oh", TW * m, TW * m + 64), S("tb2", 0, 64), AF.Relu, S("av", m, m + 1), -1.0)
        act(S("nn"), S("bv"), AF.Relu, 8192.0, -8192.0)
        mm(S("p4", 256, 512), I1, S("zr"), True, False)
        po = S("p5", 0, 128)
        mm(po, ta, S("id16"), True, False)
        mm(po, S("non"), IHALF, False, False)
        mm(po, S("nn"), I1, False, True)
        if last:
            ts(S("poff"), po, 2048.5, float(DUMMY), ALU.add, ALU.min)
        else:
            mm(S(PF), I1, S("vw", w0 + 512, w0 + 1024), True, False)
            mm(S("p3"), I1, S("vw", w0 + 2560, w0 + 3072), True, False)

        def slot(s, kinds, end=False):
            ob = kinds[-1][2]
            o = S(ob, 128, 193)
            for p0, p1, pb, ramp in kinds:
                c, d = CS * (4 if ramp and p0 == 0 else s), 256 * ramp
                act(S("cs", c + 2 * ramp, c + 66 + ramp, 1, p0, p1), S(pb, 0, 66 - ramp, 1, p0, p1), ID)
                for i, (x, y) in enumerate(((0, 0), (0, 2), (128, 1))):
                    mm(S(ob, 128, 193, 1, p0, p1), S("d2", d + x + p0, d + x + p1, 1, p0, p1),
                       S("cs", c + y, c + y + 65, 1, p0, p1), i == 0, i == 2)
            if end:
                cp(S("cb", 66 * s, 66 * s + 65), o)
            else:
                act(S("cb", 66 * s, 66 * s + 65), o, ID)
            for q in range(4):
                w = 64 if q == 3 else 65
                mm(S("p4", 256 + 64 * q, 256 + 64 * q + w, 1, 32 * s, 32 * s + 32), S("rl", 32 * q, 32 * q + 32),
                   S("cb", 66 * s, 66 * s + w), False, False)
            mm(S("p4", 256, 257, 1, 32 * s, 32 * s + 32), S("rl", 128, 160), S("cb", 66 * s + 64, 66 * s + 65), False, False)
            if end:
                mm(S("p4", 256, 257), I1, S("zr", 0, 1), False, True)
        pend = []
        na = [nv]
        for n in range(nv):
            g, k = n // 16, n % 16
            c = TW * n
            ts(S("oh", c, c + 129), S("tab", 0, 129), S("av", n, n + 1), S("bv", n, n + 1), ALU.max, ALU.min)
            o = S("p%d" % (g // 2 % 2), 0, 66, 1, 64 * (g % 2), 64 * (g % 2) + 64)
            pend.append((o, S("oh", c + 65, c + 129), S("oh", c, c + 66), k == 0, k == 15))
            if n % 4 == 3 or n >= nv - 4:
                for x in pend:
                    mm(*x, also=S("oh", c, c + 129))
                pend = []
            if n % 4 == 3 and na[0] < 128 and n > (AL if last else 0):
                for m in (na[0], na[0] + 1):
                    act(S("oh", TW * m + 64, TW * m + 129), S("tb2", 64, 129), AF.Relu, S("bv", m, m + 1), -1.0)
                for m in (na[0], na[0] + 1):
                    mm(S("p3" if last else "p2", 0, 65, 1, 64 * (m // 16 % 2), 64 * (m // 16 % 2) + 64), S("oh", TW * m, TW * m + 64),
                       S("oh", TW * m + 64, TW * m + 129), m % 16 == 0, m % 16 == 15,
                       also=S("oh", TW * na[0] + TW + 64, TW * na[0] + TW + 129))
                na[0] += 2
            if last and n == YG:
                y_gain(t - 1, 1, LG[0])
                y_add(t - 1, 0)
                y_sum(0, "za")
            if last and n in YL:
                j = (2, 3, 0, 1)[YL.index(n)]
                pb = ("p2", PT, PF, PF)[j]
                act(S(phi, 512 * j, 512 * j + 512), gat(win, S("poff", 32 * j, 32 * j + 32)), ID)
                y_chunk(t, j, pb, S(pb) if j < 2 else S("exw", 512 * (j - 2), 512 * (j - 1)))
            if n % 32 == 1 and 32 < n < nv - 32:
                slot(n // 32 - 1, [(0, 128, "p%d" % ((n // 32 - 1) % 2), 0)])
            if n == PN and not last:
                ts(S("poff"), po, 2048.5, float(DUMMY), ALU.add, ALU.min)
                mm(S("p5"), I1, S("vw", w0 + 1536, w0 + 2048), True, False)
            if n == NA and not last:
                slot(3, [(0, 128, "p2", 1)])
            if n == (NA if not last else 3) and t > 0:
                y_chunk(t - 1, 3, PT)
        y_gain(t - 1, LG[0] if last else 1, LG[1] if last else 2)
        if last:
            slot(2, [(0, 128, "p0", 0)])
            slot(3, [(64, 128, "p3", 1), (0, 64, "p1", 0)], True)
        else:
            slot(1, [(0, 128, "p1", 0)])
            slot(2, [(0, 128, "p0", 0)], True)
            mm(S("p2"), I1, S("vw", w0 + 3584, w0 + 4096), True, False)
        ts(S("ub"), S("p4", 256, 512), 1.0, -256.0, ALU.is_equal, ALU.mult)
        y_gain(t - 1, LG[1] if last else 2, LG[2] if last else 3)
        for j in range(8):
            if last:
                pb = ("p3", "p0", "p4", PF, "p3", "p1", "p4", "p0")[j]
            else:
                pb = (PT, PF, "p1", "p5", "p0", "p3", PT, "p2")[j]
            c = 512 * j
            col = S("vw", w0 + c, w0 + c + 512)
            if j % 2 and last:
                filler(mm)(S(pb), IM32, S("gw", c, c + 512), True, False)
            for i in range(2):
                hx = 2 * j + i
                mm(S(pb, 256 * i, 256 * i + 256), S("ex", 128 * hx, 128 * hx + 128), S("ub"), j % 2 == 0, j % 2 == 0 or i == 1)
            if last:
                if j % 2:
                    act(S("gu", c, c + 512), S(pb), AF.Relu, -8.0, -1.0 / 32)
                else:
                    tt(S("gu", c, c + 512), S(pb), S("gneg", c // 2, c // 2 + 512), ALU.mult)
                    if j == 2:
                        cp(S("gu", 4096, 4098), S("gu", 0, 2))
                continue
            if j % 2:
                act(col, S(pb), ID)
            else:
                tt(col, S(pb), col, ALU.add)
            if j == 2:
                cp(S("vw", w0 + 4096, w0 + 4098), S("vw", w0, w0 + 2))
            if j == 3:
                send_half()
            if j == 7:
                send([(S("vw", w0 + 2048, w0 + WW), S("vw", w0 + WW + 2048, w0 + 2 * WW), prev, mask, "arrX%d" % (t + 1))])
        y_gain(t - 1, LG[2] if last else 3, 8 if last else 4)
        if last:
            y_sum(t - 1, "zz")
            GU = S("gu", 0, 4104)
            act(S("xg", 0, 1024), gat(GU, S("poff", 0, 64)), ID)
            tt(S("zw", 1024, 2048), gat(GU, S("poff", 64, 128)), S("exw"), ALU.mult)
            for j, pb in enumerate(("p2", PT)):
                tt(S("zw", 512 * j, 512 * j + 512), S(pb), S("xg", 512 * j, 512 * j + 512), ALU.mult)
            for q in range(4):
                scan(R("sc", q, q + 1, 16, 272), S("za", 256 * q, 256 * q + 256), S("zw", 256 * q, 256 * q + 256), ALU.add)
            y_sum(t, "zw")
            act(S("yo", 64, 128), S("p5", 0, 64), ID)
            tt(S("yo", 0, 64), R("sc", 0, 4, 31, 272, step=16), R("sc", 0, 4, 15, 256, step=16), ALU.subtract)
            put("S", "dma", (("y",), S("yo"), "o0"), [S("yo")], [])
            break
        for j in range(4):
            o, a = S(phi, 512 * j, 512 * j + 512), gat(win, S("poff", 32 * j, 32 * j + 32))
            if j % 2:
                act(o, a, AF.Relu, 0.0, -1.0)
            else:
                ts(o, a, -1.0, 0.0, ALU.mult, ALU.max)
        for j in range(2):
            y_diff(t, j, "p%d" % j)
        y_gain(t - 1, 4, 5)
        side(True)
        mm(S(PF, 0, 384), I1, S("ci"), True, False)
        mm(S(PF, 128, 256), I128, S("non"), False, False)
        mm(R(PT, 0, 8, 0, 32), S("tb"), S("wx"), True, False)
        for h in range(2):
            g0 = (8 - t) * h
            mm(R(PT, 0, 8, 16, 32, 64 * h, 64 * h + 64), S("st", 64 * h, 64 * h + 64, p1=8), R("ws", g0, g0 + 8, 0, 16, p1=8), False, False)
        for h in range(2):
            mm(S("p4", 0, 128, 1, 64 * h, 64 * h + 64), S("jj"), S("zp", zo + 128 * h, zo + 128 * h + 128))
        side(False)
        mm(R(PF, 0, 24, 0, 1), S(phi, 0, 2048, 16), S("fw", 1, 48, 2), False, False)
        for k in range(1, 16):
            w = 48 * (k == 15)
            mm(R(PF, 0, 24, k - 1, k + 1), S(phi, k, 2048, 16), S("fw", w, w + 48), False, k == 15)
        for h in range(2):
            ts(S("fl", 128 * h, 128 * h + 128), S(PF, 128 * h, 128 * h + 128), 0.5, None, ALU.is_gt)
        y_gain(t - 1, 5, 6)
        y_diff(t, 2, "p2")
        for h in range(2):
            mm(S(("p3", "p5")[h], 0, 128), S("fl", 128 * h, 128 * h + 128), I1)
        act(S("fb", 0, 128), S("p3", 0, 128), ID)
        act(S("fb", 128, 256), S("p5", 0, 128), ID)
        act(S("sa"), S(PF, 256, 384), AF.Sign, -0.5)
        mm(R(PT, 0, 8, 0, 32), S("fb", 0, 128), S("wv"), False, False)
        mm(R(PT, 0, 8, 0, 32), S("fb", 128, 256), S("wl"), False, True)
        mm(S("p3", 256, 384), S("sa"), I1)
        act(S("sb"), S("p3", 256, 384), ID)
        y_chunk(t, 0, "p0", diff=False)
        for k in range(16):
            mm(S("p4", 128, 256), S(phi, k, 2048, 16), IM2, k == 0, False)
        mm(S("p4", 128, 256), S("sb"), S("bl2", 0, 128), False, True)
        mm(S("p3", 384, 512), S("sb"), S("bl2", 128, 256))
        act(S("mu"), S("p3", 384, 512), ID, 0.5)
        y_chunk(t, 1, "p1", diff=False)
        side(True)
        mm(S("p3", 128, 256), ta, S("id16"), True, False)
        mm(S("p3", 128, 256), S("non"), IHALF, False, False)
        mm(S("p3", 128, 256), S("sa"), IM4K, False, True)
        ts(S("pofy", zo // 2, zo // 2 + 128), S("p3", 128, 256), 6144.5, float(DUMMY), ALU.add, ALU.min)
        side(False)
        dsteps = [lambda: tt(S("tt"), S("p4", 0, 128), S("mu"), ALU.mult),
                  lambda: ts(S("fi"), S("tt"), 4096 - 0.46875, None, ALU.add),
                  lambda: tt(S("p4", 128, 256), S("p4", 128, 256), S("fi"), ALU.add),
                  lambda: parts(t + 1, 0), lambda: parts(t + 1, 1)]
        for s in range(17):
            i0, i1, r = max(s - 1, 0), 15 if s == 15 else 16, 8 * min(s, 15)
            ts(R("qb", r, r + 8, i0, i1), R(PT, 0, 8, i0 + s, i1 + s), KEY * s - 8192, KEY * s + 8192, ALU.max, ALU.min)
            if s >= DS and (s - DS) % 2 == 0 and dsteps:
                dsteps.pop(0)()
            if s < MERGE:
                mm(R(PF, 0, 8, i0, 16), I32F, R("qb", r, r + 8, i0, 16), s == 0, False)
            elif s % 2 == 0 and s < 15:
                w = R("qb", 8 * s - 8, 8 * s, s - 1, 16)
                tt(w, w, R("qb", 8 * s, 8 * s + 8, s - 1, 16), ALU.add)
                mm(R(PF, 0, 8, s - 2, 16), I32F, R("qb", 8 * s - 8, 8 * s, s - 2, 16), False, False)
        mm(R(PF, 0, 8, 14, 16), I32F, R("qb", 120, 128, 14, 16), False, True)
        y_chunk(t, 2, "p2", diff=False)
        times_tail(t + 1)
        for f in dsteps:
            f()
        if t == 0:
            for j in range(4):
                filler(ts)(S("gneg", 512 * j, 512 * j + 512), S("gw", 1024 * j, 1024 * j + 512), -1.0 / 256, None, ALU.mult)
    return ops


def order(ops):
    hist = {}
    banks = {}
    deps = []
    after = {}
    for i, (q, kind, args, reads, writes, opt) in enumerate(ops):
        d = set()
        reads = reads + ([opt["also"]] if "also" in opt else [])
        for acc, w in [(r, False) for r in reads] + [(x, True) for x in writes]:
            name = acc[0]
            if SCRATCH[name][0] == "psum":
                st = banks.setdefault(name, [q, [], []])
                if st[0] != q:
                    st[:] = [q, [], st[1]]
                d.update(st[2])
                if q == "P":
                    after[i] = st[1][-1:]
                    continue
            for j, a, ww in hist.get(name, []):
                if (w or ww) and _meet(a, acc) and not (SCRATCH[name][0] == "psum" and ops[j][0] != q):
                    d.add(j)
        for acc, w in [(r, False) for r in reads] + [(x, True) for x in writes]:
            name = acc[0]
            if SCRATCH[name][0] == "psum" and i not in banks[name][1][-1:]:
                banks[name][1].append(i)
            h = hist.setdefault(name, [])
            if w:
                h[:] = [e for e in h if not (acc[1] <= e[1][1] and e[1][2] <= acc[2] and (e[1][4] & ~acc[4]) == 0)]
            h.append((i, acc, w))
        d.discard(i)
        deps.append(d)
    return deps, after


CYC, PCYC, GATHER, HOP, HOPS = 0.00104, 0.00052, 1.56, 0.19, (0.12, 0.3)
FLIGHT = {"W": 6.0, "X": 4.0, "G": 8.0}
LOAD = {"ivi": 2.0, "tai": 2.0, "pfi": 2.0, "za": 9.0}
PASSES, MOVES = 3, 150


def _cost(op):
    q, kind, a = op[0], op[1], op[2]

    def n(x):
        return 16 * x[2][5] if x[0] == "*" else x[5]

    def two(*xs):
        return all(SCRATCH[x[0]][2] in (BF, F16, U16) for x in xs if isinstance(x, tuple))
    if kind == "mm":
        return max(min(64, n(a[1])), n(a[2])) * PCYC * (4 if SCRATCH[a[1][0]][2] == F32 else 1)
    if kind in ("dma", "send", "arr"):
        return {"dma": 1.0 if q == "G" else 0.1, "send": 0.5, "arr": 0.0}[kind]
    if kind in ("aff", "iota"):
        return 0.17 + 2 * n(a[0]) * CYC
    if kind == "ms":
        return max(64, n(a[0]) * (0.5 if two(a[0]) else 1)) * CYC
    if a[1][0] == "*":
        return 0.06 + GATHER * n(a[1]) * CYC
    if kind == "act":
        return 0.03 + max(64, n(a[1])) * CYC
    if kind == "tt":
        return max(64, n(a[1]) * (1 if "psum" in (SCRATCH[a[1][0]][0], SCRATCH[a[2][0]][0]) else 2)) * CYC
    return max(64, n(a[1]) * (0.5 if kind != "scan" and two(*a[:4]) else 1)) * CYC


def schedule(ops, deps, after):
    n = len(ops)
    cost = [_cost(o) for o in ops]
    pred = [[(j, HOP) for j in deps[i]] + [(j, 0.0) for j in after.get(i, []) + ops[i][5].get("behind", [])] for i in range(n)]
    sender = {}
    for i, o in enumerate(ops):
        if o[1] == "send":
            for tr in o[2][0]:
                sender[tr[-1]] = i
        if o[1] == "arr":
            pred[i] = [(sender[o[2][0]], FLIGHT[o[2][0][3]])]
    for i in range(n):
        pred[i] = [(j, LOAD.get(ops[j][2][0][0], 4.5) if ops[j][1] == "dma" else w) for j, w in pred[i]]
    succ = [[] for _ in range(n)]
    for i in range(n):
        for j, w in pred[i]:
            succ[j].append((i, w))

    def lay(seq, before):
        start = [0.0] * n
        gaps = {}
        for i in seq:
            t = max([start[j] + cost[j] + w for j, w in before[i]] + [0.0])
            c = cost[i] + 1e-6
            gl = gaps.setdefault(ops[i][0], [[0.0, 1e9]])
            lo, hi = 0, len(gl) - 1
            while lo < hi:
                mid = (lo + hi) // 2
                if gl[mid][1] < t + c:
                    lo = mid + 1
                else:
                    hi = mid
            while gl[lo][1] - max(gl[lo][0], t) < c:
                lo += 1
            a, b = gl[lo]
            t = max(a, t)
            gl[lo:lo + 1] = [e for e in ([a, t], [t + c, b]) if e[1] - e[0] > 0.004]
            start[i] = t
        return start, max(start[i] + cost[i] for i in range(n))

    def again(start):
        back, _ = lay(sorted(range(n), key=lambda i: (-(start[i] + cost[i]), -i)), succ)
        return sorted(range(n), key=lambda i: (-(back[i] + cost[i]), i))

    def pulled(wanted):
        out, done = [], [False] * n
        for i in wanted:
            stack = [i]
            while stack:
                j = stack[-1]
                todo = [k for k, _ in pred[j] if not done[k]]
                if todo:
                    stack += sorted(todo, reverse=True)
                    continue
                stack.pop()
                if not done[j]:
                    done[j] = True
                    out.append(j)
        return out

    def worth(start):
        total = 0.0
        seq = sorted(range(n), key=lambda i: (start[i], i))
        for hop in HOPS:
            end, free = [0.0] * n, {}
            for i in seq:
                t = max([end[j] + (hop if w == HOP else w) for j, w in pred[i]] + [free.get(ops[i][0], 0.0) if ops[i][0] != "X" else 0.0])
                end[i] = free[ops[i][0]] = t + cost[i]
            total += max(end) / (1 + hop)
        return total

    best = None
    for seq in (pulled([j for j in range(n) if not ops[j][5]["late"]] + list(range(n))), list(range(n))):
        for _ in range(PASSES):
            start, _ = lay(seq, pred)
            span = worth(start)
            if best is None or span < best[0]:
                best = (span, start)
            seq = again(start)
    twins = {}
    for i, o in enumerate(ops):
        twins.setdefault(o[5]["kind"], []).append(i)
    span, start = best
    tried = set()
    for _ in range(MOVES):
        ends = {}
        for i in range(n):
            ends[(ops[i][0], round(start[i] + cost[i] + 1e-6, 5))] = i
        i = max(range(n), key=lambda k: start[k] + cost[k])
        pairs = []
        while start[i] > 1e-9:
            ready, j = max([(start[k] + cost[k] + w, k) for k, w in pred[i]] + [(0.0, -1)])
            if ready < start[i] - 1e-7:
                j = ends.get((ops[i][0], round(start[i], 5)), j)
                pairs.append((start[i] - ready, i, j))
            if j < 0:
                break
            i = j
        moves = [(w, ops[i][5]["kind"], how) for w, i, j in pairs for how in (0, 1)]
        moves += [(w, ops[j][5]["kind"], 2) for w, i, j in pairs if ops[j][5]["late"]]
        moves = [m for m in moves if m[1:] not in tried and m[0] > 0.05]
        if not moves:
            break
        w, kind, how = max(moves)
        tried.add((kind, how))
        key = list(start)
        for a in twins[kind]:
            ready = max([start[k] + cost[k] + x for k, x in pred[a]] + [0.0])
            key[a] = (ready - 1e-5, ready - 0.6, start[a] + 1.5)[how]
        s1, _ = lay(pulled(sorted(range(n), key=lambda k: (key[k], k))), pred)
        s2, _ = lay(again(s1), pred)
        e1, e2 = worth(s1), worth(s2)
        if e1 < e2:
            s2, e2 = s1, e1
        if e2 < span - 1e-6:
            span, start = e2, s2
            tried = set()
    return start


ORDERED = {}


def ordered(ops):
    if not ORDERED:
        deps, after = order(ops)
        start = schedule(ops, deps, after)
        seq = sorted(range(len(ops)), key=lambda i: (start[i], i))
        place = {j: i for i, j in enumerate(seq)}
        ORDERED["seq"] = seq
        ORDERED["deps"] = [set(place[k] for k in deps[j]) for j in seq]
        ORDERED["start"] = [start[j] for j in seq]
    return [ops[j] for j in ORDERED["seq"]], ORDERED["deps"]


def rank_program(g, core, T, topo):
    rank = T.rank_of(core)
    if rank is None:
        cores = list(T.cores)
        for r, c in helpers(cores, topo).items():
            if c == core:
                rid, pid, _ = topo.addr(cores[r - 1])
                engines = topo.engines(core, cores[r - 1])
                for i, (_, dst, sem) in enumerate(handed_on()):
                    piece = T[dst[0]][:, dst[3][0][0]:dst[3][0][1]]
                    g.wait_ge(T.sem["hop%d" % i], len(topo.engines(cores[r], core)))
                    g.remote_dma(piece, piece, T.sem[sem], T.sem.sent, pid, rid, sum(1 << e for e in engines))
                g.wait_ge(T.sem.sent, len(engines) * len(handed_on()))
        return
    ops, deps = ordered(plan(rank, list(T.cores), topo))
    queue = {"P": g.tensor, "V": g.vector, "A": g.scalar, "G": g, "S": g.sync}

    def own(j):
        return ops[j][1] in ("dma", "arr")
    need = []
    marked = set()
    for i, d in enumerate(deps):
        best = {}
        for j in d:
            if ops[j][1] == "send":
                continue
            key = ("own", j) if own(j) else ops[j][0]
            best[key] = max(best.get(key, -1), j)
        need.append(best)
    seen = {}
    for i, best in enumerate(need):
        s = seen.setdefault(ops[i][0], {})
        for key in list(best):
            if ops[i][0] == "X" or s.get(key, -1) >= best[key]:
                del best[key]
            else:
                s[key] = best[key]
                marked.add(best[key])
    count = {}
    ticket = {}
    for i, o in enumerate(ops):
        if o[1] == "dma":
            ticket[i] = (o[2][2], 16)
        elif o[1] == "arr":
            ticket[i] = o[2]
        elif i in marked:
            count[o[0]] = count.get(o[0], 0) + 1
            ticket[i] = ("c" + o[0], count[o[0]])

    def ap(x):
        if not isinstance(x, tuple):
            return x
        if x[0] == "*":
            return ap(x[1]).indirect(ap(x[2]))
        if len(x) == 1:
            return T[x[0]][:]
        if len(x) == 3:
            return T[x[0]][:, x[1]:x[2]]
        if len(x[3]) == 2 and x[3][0][1] - x[3][0][0] == 1:
            return T[x[0]][x[1]:x[2], x[3][0][0], x[3][1][0]:x[3][1][1]]
        return T[x[0]][(slice(x[1], x[2]),) + tuple(slice(a, b) if s == 1 else slice(a, b, s) for a, b, s in x[3])]

    sent = 0
    waited = set()
    for i, (q, kind, a, reads, writes, opt) in enumerate(ops):
        if kind == "arr":
            continue
        e = queue[q]
        for key in need[i]:
            s, n = ticket[need[i][key]]
            e.wait_ge(T.sem[s], n)
            waited.add((s, n))
        if kind == "ts":
            if a[5] is None:
                ins = e.tensor_scalar(ap(a[0]), ap(a[1]), ap(a[2]), None, a[4])
            else:
                ins = e.tensor_scalar(ap(a[0]), ap(a[1]), ap(a[2]), ap(a[3]), a[4], a[5])
        elif kind == "tt":
            ins = e.tensor_tensor(ap(a[0]), ap(a[1]), ap(a[2]), a[3])
        elif kind == "cp":
            ins = e.tensor_copy(ap(a[0]), ap(a[1]))
        elif kind == "ms":
            ins = e.memset(ap(a[0]), a[1])
        elif kind == "scan":
            ins = e.tensor_tensor_scan(ap(a[0]), ap(a[1]), ap(a[2]), 0.0, a[3], ALU.add)
        elif kind == "act":
            ins = e.activation(ap(a[0]), ap(a[1]), a[2], bias=ap(a[3]), scale=a[4])
        elif kind == "mm":
            ins = e.matmul(ap(a[0]), ap(a[1]), ap(a[2]), a[3], a[4])
        elif kind == "aff":
            ins = e.affine_select(ap(a[0]), ap(a[1]), a[2], a[3], 0.0, a[4], a[5])
        elif kind == "iota":
            ins = e.iota(ap(a[0]), a[1], a[2], 0, allow_small_or_imprecise_dtypes=True)
        elif kind == "dma":
            if a[0][0] == "za":
                e.dma_start(ap(a[0]), ap(a[1]), accum_op=ALU.add).then_inc(T.sem[a[2]], 16)
            else:
                e.dma_start(ap(a[0]), ap(a[1])).then_inc(T.sem[a[2]], 16)
            continue
        else:
            trs = []
            for src, dst, c, mask, sem in [x[:5] for x in a[0]]:
                rid, pid, _ = topo.addr(c)
                trs.append(RemoteDMATransfer(dst_ids=[DstId(rid=rid, pnc=pid)], dma_engine_mask=mask,
                                             remote_sem=T.sem[sem], src=ap(src), dst=ap(dst)))
                sent += bin(mask).count("1")
            e.remote_dma_fused(trs, local_sem=T.sem.sent)
            continue
        if i in ticket:
            ins.then_inc(T.sem[ticket[i][0]], 1)
    g.wait_ge(T.sem.sent, sent)
    for i in ticket:
        if own(i) and ticket[i] not in waited:
            g.sync.wait_ge(T.sem[ticket[i][0]], ticket[i][1])
